import numpy as np
import ml_dtypes


def mxq(x, axis, fmt="e4m3"):
    dtype, down = {"e4m3": (ml_dtypes.float8_e4m3fn, 7), "e5m2": (ml_dtypes.float8_e5m2, 14)}[fmt]
    v = np.moveaxis(np.asarray(x, np.float32).astype(ml_dtypes.bfloat16).astype(np.float64), axis, -1)
    blocks = v.reshape(v.shape[:-1] + (-1, 32))
    amax = np.abs(blocks).max(-1, keepdims=True)
    byte = np.maximum(np.where(amax > 0, np.frexp(amax)[1] - 1 + 127, 0) - down, 1)
    scale = np.exp2(byte - 127.0)
    codes = (blocks / scale).astype(np.float32).astype(dtype).astype(np.float64)
    return np.moveaxis((codes * scale).reshape(v.shape), -1, axis)


WIDE = False


def mx_kscale(k):
    if not WIDE:
        return np.ones(k)
    levels = np.array([10, -10, 5, -5, 0])
    if k % 512:
        return np.exp2(np.random.permutation(np.resize(levels, k // 32))).repeat(32)
    a = np.empty((k // 512, 16))
    for p in range(k // 512):
        a[p, :8] = np.random.permutation(np.resize(levels, 8))
        for g in range(8):
            far = levels[np.abs(levels - a[p, g]) >= 10]
            a[p, g + 8] = far[np.random.randint(len(far))]
    return np.exp2(a.ravel()).repeat(32)


def f64(x):
    return np.asarray(x).astype(np.float64)


def striped(idx):
    return np.tile(idx.reshape(-1, 16).T, (8, 1)).astype(np.uint16)


def unstriped(offs):
    return offs[:16].T.reshape(-1).astype(np.int64)


E2M1 = np.array([0.0, 0.5, 1.0, 1.5, 2.0, 3.0, 4.0, 6.0, -0.0, -0.5, -1.0, -1.5, -2.0, -3.0, -4.0, -6.0])


def pack_weight(w, fmt):
    k, n = w.shape
    w = f64(np.asarray(w, np.float32).astype(ml_dtypes.bfloat16)).reshape(k // 32, 32, n)
    amax = np.abs(w).max(1)
    if fmt == "e4m3":
        byte = np.frexp(amax)[1] - 1 + 127 - 7
    else:
        mant, ex = np.frexp(amax / 6.0)
        byte = np.where(mant > 0.5, ex, ex - 1) + 127
    byte = np.clip(np.where(amax > 0, byte, 1), 1, 254)
    scaled = (w * np.exp2(127.0 - byte)[:, None, :]).reshape(k, n).astype(np.float32)
    by_word = np.ascontiguousarray(scaled.reshape(k // 512, 128, 4, n).transpose(0, 1, 3, 2))
    if fmt == "e4m3":
        words = by_word.astype(ml_dtypes.float8_e4m3fn).view(np.uint8)
    else:
        c = by_word.astype(ml_dtypes.float4_e2m1fn).view(np.uint8) & 0xF
        words = (c[..., 0::2] | (c[..., 1::2] << 4)).reshape(k // 512, 128, 2 * n)
    return np.ascontiguousarray(words), np.ascontiguousarray(byte.astype(np.uint8).reshape(k // 512, 16, n))


def unpack_weight(words, scales, fmt):
    g, _, n = scales.shape
    words = np.ascontiguousarray(words).reshape(g, 128, n, -1)
    if fmt == "e4m3":
        vals = words.view(ml_dtypes.float8_e4m3fn).astype(np.float64)
    else:
        nib = np.empty((g, 128, n, 4), np.uint8)
        nib[..., 0::2] = words & 0xF
        nib[..., 1::2] = words >> 4
        vals = E2M1[nib]
    vals = vals * np.repeat(np.exp2(scales.astype(np.float64) - 127.0), 8, axis=1)[..., None]
    return vals.transpose(0, 1, 3, 2).reshape(g * 512, n)


def gelu(v):
    return 0.5 * v * (1.0 + np.tanh(np.sqrt(2.0 / np.pi) * (v + 0.044715 * v**3)))


K, T, K2, T2, S, P, H, N = 1024, 2048, 512, 2048, 1024, 1024, 1024, 256

def setup_inputs():
    n = np.random.standard_normal
    s = mx_kscale(K)[:, None]
    s2 = mx_kscale(K2)[:, None]
    u = mx_kscale(H)[:, None]
    tab_words, tab_scales = pack_weight(n((K, T)) * s, "e4m3")
    w4_words, w4_scales = pack_weight(0.45 * n((K, H)) / np.sqrt(K) / s, "e2m1")
    w8_words, w8_scales = pack_weight(1.2 * n((H, N)) / np.sqrt(H) / u, "e4m3")
    return {
        "tab_words": tab_words, "tab_scales": tab_scales,
        "offs": striped(np.random.permutation(T)[:P]),
        "base": (n((K2, T2)) * s2).astype(np.float32),
        "xs": (np.round(16 * n((K2, S))) / 16 * s2).astype(np.float32),
        "offs2": striped(np.random.permutation(T2)[:S]),
        "offs3": striped(np.random.permutation(T2)[:P]),
        "wm": (n((K2, H)) / np.sqrt(K2) / s2).astype(np.float32),
        "gm": (np.exp(0.3 * n(H)) * u[:, 0]).astype(np.float32),
        "w4_words": w4_words, "w4_scales": w4_scales,
        "gs": (np.exp(0.3 * n(H)) * u[:, 0]).astype(np.float32),
        "w1": (n((H, N)) / np.sqrt(H) / u).astype(np.float32),
        "w8_words": w8_words, "w8_scales": w8_scales,
        "bo": (0.3 * n(N)).astype(np.float32),
    }

def reference(tab_words, tab_scales, offs, base, xs, offs2, offs3, wm, gm, w4_words, w4_scales, gs, w1, w8_words, w8_scales, bo):
    page = f64(base).copy()
    page[:, unstriped(offs2)] = f64(xs)
    a = mxq(f64(wm), 0, "e4m3").T @ mxq(page, 0, "e4m3")
    h1 = np.tanh(a[:, unstriped(offs3)]) * f64(gm)[:, None]
    v = unpack_weight(tab_words, tab_scales, "e4m3")[:, unstriped(offs)]
    b = unpack_weight(w4_words, w4_scales, "e2m1").T @ v
    h2 = np.sin(b) * f64(gs)[:, None]
    w8 = unpack_weight(w8_words, w8_scales, "e4m3")
    y = mxq(f64(w1), 0, "e4m3").T @ mxq(h1, 0, "e4m3") + w8.T @ mxq(h2, 0, "e4m3")
    return np.tanh(y + f64(bo)[:, None])

@@ -1,0 +1,316 @@
+from contextlib import ExitStack
+
+import concourse.mybir as mybir
+
+K, T, K2, T2, S, NP, H, N = 1024, 2048, 512, 2048, 1024, 1024, 1024, 256
+FLOPS = 2 * (K2 * H * T2 + K * H * NP + 2 * H * N * NP)
+
+F32 = mybir.dt.float32
+BF16 = mybir.dt.bfloat16
+I32 = mybir.dt.int32
+U32 = mybir.dt.uint32
+U16 = mybir.dt.uint16
+U8 = mybir.dt.uint8
+FP8X4 = mybir.dt.float8_e4m3fn_x4
+FP4X4 = mybir.dt.float4_e2m1fn_x4
+ACT = mybir.ActivationFunctionType
+MULT = mybir.AluOpType.mult
+
+P = 128
+REP = 32
+H2_ENG = "gpsimd"
+H1_ENG = ["vector","vector","vector","vector","vector"]
+PAGE_V = [3]
+EVAC_V = []
+
+
+def tile_list_exoskeleton_gait_features_kernel(
+    tc, tab_words, tab_scales, offs, base, xs, offs2, offs3, wm, gm, w4_words, w4_scales, gs, w1, w8_words, w8_scales, bo, out
+):
+    nc = tc.nc
+    with ExitStack() as ctx:
+        lists = ctx.enter_context(tc.tile_pool(name="lists", bufs=1))
+        keep = ctx.enter_context(tc.tile_pool(name="keep", bufs=1))
+        psum = ctx.enter_context(tc.psum_pool(name="psum", bufs=8))
+        eng = {"vector": nc.vector, "gpsimd": nc.gpsimd}
+
+        def row_tile(dtype, name):
+            return keep.tile([P, 2048], dtype, tag="row", bufs=6, name=name, align_bytes=64)
+
+        def stage_tile(shape, name):
+            return keep.tile(shape, F32, tag="stage", bufs=4, name=name, align_bytes=64)
+
+        def bf_tile(name):
+            return keep.tile([P, 2048], BF16, tag="bf", bufs=6, name=name, align_bytes=64)
+
+        ts = keep.tile([P, T], U8, name="ts", align_bytes=64)
+        w4s_raw = keep.tile([P, 2 * H], U8, name="w4s_raw", align_bytes=64)
+        vs1 = keep.tile([P, NP], U8, name="vs1", align_bytes=64)
+        w8s = keep.tile([P, 2 * N], U8, name="w8s", align_bytes=64)
+        zin = keep.tile([P, 1], F32, name="zin")
+        zero = keep.tile([P, 1], F32, name="zero")
+        nc.vector.memset(ts[:].bitcast(I32), 0)
+        nc.gpsimd.memset(zin[:], 0.0)
+        nc.vector.memset(w4s_raw[:].bitcast(I32), 0)
+        nc.gpsimd.memset(vs1[:].bitcast(I32), 0)
+        nc.gpsimd.memset(w8s[:].bitcast(I32), 0)
+        nc.scalar.activation(zero[:], zin[:], ACT.Silu)
+
+        l1 = lists.tile([P, NP // 16], U16, name="l1")
+        l2 = lists.tile([P, S // 16], U16, name="l2")
+        l3 = lists.tile([P, NP // 16], U16, name="l3")
+        nc.sync.dma_start(l1[:], offs)
+        w4_raw = keep.tile([P, 2, 2 * H], U8, name="w4_raw", tag="w4out", bufs=2, align_bytes=64)
+        nc.sync.dma_start(w4_raw[:].bitcast(I32), w4_words.rearrange("a p c -> p a c").bitcast(I32))
+        for q in range(4):
+            nc.sync.dma_start(ts[32 * q : 32 * q + 8, :].bitcast(I32), tab_scales[:, 4 * q : 4 * q + 4, :].bitcast(I32))
+        tabw = []
+        for a in range(2):
+            tw = row_tile(I32, f"tabw{a}")
+            nc.sync.dma_start(tw[:], tab_words[a].rearrange("p t i -> p (t i)").bitcast(I32))
+            tabw.append(tw)
+        for q in range(4):
+            nc.sync.dma_start(
+                w4s_raw[32 * q : 32 * q + 4, :].rearrange("r (a c) -> r a c", a=2).bitcast(I32),
+                w4_scales[:, 4 * q : 4 * q + 4, :].rearrange("a r c -> r a c").bitcast(I32),
+            )
+        gsc = keep.tile([P, 2, 4], F32, name="gsc")
+        gmc = keep.tile([P, 2, 4], F32, name="gmc")
+        nc.sync.dma_start(l2[:], offs2)
+
+        base_v = base.rearrange("(p i) t -> p i t", i=4)
+        xs_v = xs.rearrange("(p i) t -> p i t", i=4)
+        wm_v = wm.rearrange("(p j) c -> p j c", j=4)
+        xs_t = keep.tile([P, 4, S], F32, name="xs_t", tag="late", align_bytes=64)
+        planes = []
+        wm_raw = []
+
+        def load_plane(i):
+            pl = row_tile(F32, f"plane{i}")
+            nc.sync.dma_start(pl[:], base_v[:, i, :])
+            nc.sync.dma_start(xs_t[:, i, :], xs_v[:, i, :])
+            planes.append(pl)
+
+        load_plane(0)
+        nc.sync.dma_start(gsc[:], gs.rearrange("(a p t) -> p a t", a=2, t=4))
+        nc.sync.dma_start(gmc[:], gm.rearrange("(a p t) -> p a t", a=2, t=4))
+        for g in range(2):
+            wr = stage_tile([P, 4, 512], f"wm_raw{g}")
+            nc.sync.dma_start(wr[:], wm_v[:, :, 512 * g : 512 * (g + 1)])
+            wm_raw.append(wr)
+        load_plane(1)
+        load_plane(2)
+        w1_raw = stage_tile([P, 2, 4, N], "w1_raw")
+        nc.sync.dma_start(w1_raw[:], w1.rearrange("(a p j) n -> p a j n", a=2, j=4))
+        load_plane(3)
+        w8c = keep.tile([P, 2, N], I32, name="w8c", align_bytes=64)
+        nc.sync.dma_start(w8c[:], w8_words.rearrange("a p c i -> p a (c i)").bitcast(I32))
+        nc.sync.dma_start(l3[:], offs3)
+        for q in range(4):
+            nc.sync.dma_start(
+                w8s[32 * q : 32 * q + 4, :].rearrange("r (a c) -> r a c", a=2).bitcast(I32),
+                w8_scales[:, 4 * q : 4 * q + 4, :].rearrange("a r c -> r a c").bitcast(I32),
+            )
+        boc = keep.tile([P, 2], F32, name="boc")
+        with nc.allow_non_contiguous_dma(reason="one bias value a partition"):
+            nc.sync.dma_start(boc[:], bo.rearrange("(h p) -> p h", p=P))
+
+        w4p = keep.tile([P, 2 * 2 * H], U8, name="w4p", tag="w4out", bufs=2, align_bytes=64)
+        w4sp = keep.tile([P, 2 * H], U8, name="w4sp", align_bytes=64)
+        for a in range(2):
+            nc.vector.tensor_copy(
+                w4p[:, 2 * H * a : 2 * H * (a + 1)].bitcast(U16).rearrange("p (g t m) -> p g t m", g=2, t=4),
+                w4_raw[:, a, :].bitcast(U16).rearrange("p (g m t) -> p g t m", g=2, t=4),
+            )
+        nc.gpsimd.tensor_copy(
+            w4sp[:].rearrange("p (g t m) -> p g t m", g=4, t=4),
+            w4s_raw[:].rearrange("p (g m t) -> p g t m", g=4, t=4),
+        )
+
+        vs0 = keep.tile([P, NP], U8, name="vs0", align_bytes=64)
+        nc.vector.tensor_copy(vs0[:], ts[:].indirect(l1[:]))
+        nc.gpsimd.dma_start(vs1[0:112, :].bitcast(I32), vs0[4:116, :].bitcast(I32))
+        vw = []
+        for a in range(2):
+            v = keep.tile([P, NP], U32, name=f"vw{a}", tag="vw", bufs=2, align_bytes=64)
+            nc.vector.tensor_copy(v[:], tabw[a][:].bitcast(U32).indirect(l1[:]))
+            vw.append(v)
+        vsc = [vs0, vs1]
+
+        grep = keep.tile([P, 4, REP, 4], F32, name="grep")
+        for a in range(2):
+            nc.gpsimd.tensor_copy(grep[:, a, :, :], gsc[:, a, :].unsqueeze(1).to_broadcast([P, REP, 4]))
+        for a in range(2):
+            nc.gpsimd.tensor_copy(grep[:, 2 + a, :, :], gmc[:, a, :].unsqueeze(1).to_broadcast([P, REP, 4]))
+
+        def scale_round(engine, dst, src, which, width):
+            reps = width // (4 * REP)
+            gain = grep[:, which, :, :].rearrange("p r t -> p (r t)").unsqueeze(1).to_broadcast([P, reps, 4 * REP])
+            eng[engine].tensor_tensor(
+                dst.rearrange("p (k e) -> p k e", k=reps), src.rearrange("p (k e) -> p k e", k=reps), gain, MULT
+            )
+
+        for i in range(4):
+            nc.vector.tensor_copy(planes[i][:].indirect(l2[:]), xs_t[:, i, :])
+
+        sact0 = keep.tile([P, 4 * NP], F32, name="sact0", tag="actA", align_bytes=64)
+        sact1 = [keep.tile([P, 2 * NP], F32, name=f"sact1_{k}", tag="actB", bufs=2, align_bytes=64) for k in range(2)]
+        h2bf = keep.tile([P, 2 * 4 * NP], BF16, name="h2bf", align_bytes=64)
+
+        def sact(a, lo, hi):
+            if a == 0:
+                return sact0[:, lo:hi]
+            return sact1[lo // 2048][:, lo % 2048 : (hi - 1) % 2048 + 1]
+
+        for a in range(2):
+            for jb in range(8):
+                bank = psum.tile([P, 4, P], F32, name="bank", tag="bank")
+                for t in range(4):
+                    c0 = 512 * a + P * t
+                    for ka in range(2):
+                        nc.tensor.matmul_mx(
+                            out=bank[:, t, :],
+                            lhsT=w4p[:, 2 * (H * ka + c0) : 2 * (H * ka + c0 + P)].bitcast(FP4X4),
+                            lhsT_scale=w4sp[:, H * ka + c0 : H * ka + c0 + P],
+                            rhs=vw[ka][:, P * jb : P * (jb + 1)].bitcast(FP8X4),
+                            rhs_scale=vsc[ka][:, P * jb : P * (jb + 1)],
+                            start=(ka == 0),
+                            stop=(ka == 1),
+                        )
+                nc.scalar.activation(
+                    sact(a, 512 * jb, 512 * (jb + 1)).rearrange("p (j t) -> p j t", t=4),
+                    bank[:].rearrange("p t j -> p j t"),
+                    ACT.Sin,
+                    bias=zero[:],
+                )
+                if jb % 2 == 1:
+                    lo, hi = 512 * (jb - 1), 512 * (jb + 1)
+                    scale_round(H2_ENG, h2bf[:, 4096 * a + lo : 4096 * a + hi], sact(a, lo, hi), a, 1024)
+
+        wm_bf = []
+        for g in range(2):
+            wb = bf_tile(f"wm_bf{g}")
+            nc.scalar.copy(
+                wb[:].rearrange("p (t m j) -> p m j t", t=4, j=4),
+                wm_raw[g][:].rearrange("p j (m t) -> p m j t", t=4),
+            )
+            wm_bf.append(wb)
+        w1_bf = bf_tile("w1_bf")
+        nc.scalar.copy(
+            w1_bf[:].rearrange("p (a c i j) -> p a c j i", a=2, i=4, j=4),
+            w1_raw[:].rearrange("p a j (c i) -> p a c j i", i=4),
+        )
+
+        late = keep.tile([P, 17920], U8, name="late", tag="late", align_bytes=64)
+        wmc, w1c, h2c = late[:, 0:4096], late[:, 4096:6144], late[:, 6144:14336]
+        wms, w1s, h2s = late[:, 14336:15360], late[:, 15360:15872], late[:, 15872:17920]
+
+        def quant(codes, scales, c0, src):
+            n = src.shape[1] // 4
+            nc.vector.quantize_mx(out=codes[:, 4 * c0 : 4 * (c0 + n)].bitcast(FP8X4), scales=scales[:, c0 : c0 + n], in_=src)
+
+        for g in range(2):
+            quant(wmc, wms, 512 * g, wm_bf[g][:])
+
+        stg = [stage_tile([P, 4, 512], f"stg{c}") for c in range(4)]
+        for i in range(4):
+            for c in range(4):
+                nc.sync.dma_start(stg[c][:, i, :], planes[i][:, 512 * c : 512 * (c + 1)])
+        pc = keep.tile([P, 4 * T2], U8, name="pc", align_bytes=64)
+        ps = keep.tile([P, T2], U8, name="ps", align_bytes=64)
+        for c in range(4):
+            pb = bf_tile(f"page_bf{c}")
+            dst = pb[:].rearrange("p (c i j) -> p c j i", i=4, j=4)
+            src = stg[c][:].rearrange("p j (c i) -> p c j i", i=4)
+            if c in PAGE_V:
+                nc.vector.tensor_copy(dst, src)
+            else:
+                nc.scalar.copy(dst, src)
+            quant(pc[:], ps[:], 512 * c, pb[:])
+
+        rows = []
+        for u in range(8):
+            row = row_tile(F32, f"arow{u}")
+            for c in range(4):
+                bank = psum.tile([P, 512], F32, name="bank", tag="bank")
+                nc.tensor.matmul_mx(
+                    out=bank[:],
+                    lhsT=wmc[:, 4 * P * u : 4 * P * (u + 1)].bitcast(FP8X4),
+                    lhsT_scale=wms[:, P * u : P * (u + 1)],
+                    rhs=pc[:, 2048 * c : 2048 * (c + 1)].bitcast(FP8X4),
+                    rhs_scale=ps[:, 512 * c : 512 * (c + 1)],
+                    start=True,
+                    stop=True,
+                )
+                if 4 * u + c in EVAC_V:
+                    nc.vector.tensor_copy(row[:, 512 * c : 512 * (c + 1)], bank[:])
+                else:
+                    nc.scalar.copy(row[:, 512 * c : 512 * (c + 1)], bank[:])
+            rows.append(row)
+
+        h1c = [keep.tile([P, NP], U32, name=f"h1c{a}", tag="vw", bufs=2, align_bytes=64) for a in range(2)]
+        h1s = keep.tile([P, 2 * NP], U8, name="h1s", align_bytes=64)
+
+        def gather(picked, a, j0, n):
+            for t in range(4):
+                nc.vector.tensor_copy(picked[:, t, :], rows[4 * a + t][:].indirect(l3[:, j0 // 16 : (j0 + n) // 16]))
+
+        def finish_h1(picked, a, j0, n, p0, engine):
+            th = stage_tile([P, 4 * n], f"th{a}_{j0}")
+            nc.scalar.activation(
+                th[:].rearrange("p (c i t) -> p c t i", i=4, t=4),
+                picked[:, :, p0 : p0 + n].rearrange("p t (c i) -> p c t i", i=4),
+                ACT.Tanh,
+                bias=zero[:],
+            )
+            hb = bf_tile(f"h1bf{a}_{j0}")
+            scale_round(engine, hb[:, 0 : 4 * n], th[:], 2 + a, 4 * n)
+            nc.vector.quantize_mx(
+                out=h1c[a][:, j0 : j0 + n].bitcast(FP8X4), scales=h1s[:, NP * a + j0 : NP * a + j0 + n], in_=hb[:, 0 : 4 * n]
+            )
+
+        chunks = [(0, 512), (512, 256), (768, 256)]
+        g0 = keep.tile([P, 4, NP], F32, name="g0", tag="actA", align_bytes=64)
+        gather(g0, 0, 0, NP)
+        g1 = [
+            keep.tile([P, 4, 512], F32, name="g1_0", tag="actB", bufs=2, align_bytes=64),
+            keep.tile([P, 4, 256], F32, name="g1_1", tag="actB", bufs=2, align_bytes=64),
+            keep.tile([P, 4, 256], F32, name="g1_2", align_bytes=64),
+        ]
+        for k, (j0, n) in enumerate(chunks):
+            gather(g1[k], 1, j0, n)
+
+        quant(w1c, w1s, 0, w1_bf[:])
+        for k in range(4):
+            quant(h2c, h2s, 512 * k, h2bf[:, 2048 * k : 2048 * (k + 1)])
+        for k in range(2):
+            finish_h1(g0, 0, 512 * k, 512, 512 * k, H1_ENG[k])
+
+        ost = [keep.tile([P, NP], F32, name=f"ost{h}", tag="w4out", bufs=2, align_bytes=64) for h in range(2)]
+        for k, (j0, n) in enumerate(chunks):
+            banks = []
+            for h in range(2):
+                bank = psum.tile([P, n], F32, name="bank", tag="bank")
+                banks.append(bank)
+
+            def y_pass(h, wc, ws, a, hc, hs, start, stop):
+                nc.tensor.matmul_mx(
+                    out=banks[h][:],
+                    lhsT=wc[:, 4 * (N * a + P * h) : 4 * (N * a + P * (h + 1))].bitcast(FP8X4),
+                    lhsT_scale=ws[:, N * a + P * h : N * a + P * (h + 1)],
+                    rhs=hc,
+                    rhs_scale=hs[:, NP * a + j0 : NP * a + j0 + n],
+                    start=start,
+                    stop=stop,
+                )
+
+            w8b = w8c[:].rearrange("p a n -> p (a n)").bitcast(U8)
+            for h in range(2):
+                y_pass(h, w1c, w1s, 0, h1c[0][:, j0 : j0 + n].bitcast(FP8X4), h1s, True, False)
+                for a in range(2):
+                    y_pass(h, w8b, w8s, a, h2c[:, 4 * (NP * a + j0) : 4 * (NP * a + j0 + n)].bitcast(FP8X4), h2s, False, False)
+            finish_h1(g1[k], 1, j0, n, 0, H1_ENG[2 + k])
+            for h in range(2):
+                y_pass(h, w1c, w1s, 1, h1c[1][:, j0 : j0 + n].bitcast(FP8X4), h1s, False, True)
+                nc.scalar.activation(ost[h][:, j0 : j0 + n], banks[h][:], ACT.Tanh, bias=boc[:, h : h + 1])
+                nc.sync.dma_start(out[P * h : P * (h + 1), j0 : j0 + n], ost[h][:, j0 : j0 + n])

@@ -19,8 +19,9 @@ MULT = mybir.AluOpType.mult
 P = 128
 REP = 32
 H2_ENG = "gpsimd"
-H1_ENG = ["vector","vector","vector","vector","vector"]
-PAGE_V = [3]
+H1_ENG = ["gpsimd","gpsimd","gpsimd","gpsimd","vector","vector","vector","vector"]
+PAIR = "VVVV"
+CP = "VDDD"
 EVAC_V = []
 
 
@@ -34,14 +35,16 @@ def tile_list_exoskeleton_gait_features_kernel(
         psum = ctx.enter_context(tc.psum_pool(name="psum", bufs=8))
         eng = {"vector": nc.vector, "gpsimd": nc.gpsimd}
 
-        def row_tile(dtype, name):
-            return keep.tile([P, 2048], dtype, tag="row", bufs=6, name=name, align_bytes=64)
+        def row_tile(dtype, name, last=False):
+            if last:
+                return keep.tile([P, 2048], dtype, tag="lastrow", name=name, align_bytes=64)
+            return keep.tile([P, 2048], dtype, tag="row", bufs=7, name=name, align_bytes=64)
 
         def stage_tile(shape, name):
-            return keep.tile(shape, F32, tag="stage", bufs=4, name=name, align_bytes=64)
+            return keep.tile(shape, F32, tag="stage", bufs=7, name=name, align_bytes=64)
 
         def bf_tile(name):
-            return keep.tile([P, 2048], BF16, tag="bf", bufs=6, name=name, align_bytes=64)
+            return keep.tile([P, 2048], BF16, tag="bf", bufs=7, name=name, align_bytes=64)
 
         ts = keep.tile([P, T], U8, name="ts", align_bytes=64)
         w4s_raw = keep.tile([P, 2 * H], U8, name="w4s_raw", align_bytes=64)
@@ -61,7 +64,8 @@ def tile_list_exoskeleton_gait_features_kernel(
         l3 = lists.tile([P, NP // 16], U16, name="l3")
         nc.sync.dma_start(l1[:], offs)
         w4_raw = keep.tile([P, 2, 2 * H], U8, name="w4_raw", tag="w4out", bufs=2, align_bytes=64)
-        nc.sync.dma_start(w4_raw[:].bitcast(I32), w4_words.rearrange("a p c -> p a c").bitcast(I32))
+        for a in range(2):
+            nc.sync.dma_start(w4_raw[:, a, :].bitcast(I32), w4_words[a].bitcast(I32))
         for q in range(4):
             nc.sync.dma_start(ts[32 * q : 32 * q + 8, :].bitcast(I32), tab_scales[:, 4 * q : 4 * q + 4, :].bitcast(I32))
         tabw = []
@@ -81,39 +85,39 @@ def tile_list_exoskeleton_gait_features_kernel(
         base_v = base.rearrange("(p i) t -> p i t", i=4)
         xs_v = xs.rearrange("(p i) t -> p i t", i=4)
         wm_v = wm.rearrange("(p j) c -> p j c", j=4)
-        xs_t = keep.tile([P, 4, S], F32, name="xs_t", tag="late", align_bytes=64)
+        xs_t = [keep.tile([P, S], F32, name=f"xs{i}", tag=f"xs{i}", align_bytes=64) for i in range(4)]
         planes = []
         wm_raw = []
+
+        boc = keep.tile([P, 2], F32, name="boc")
+
+        def load_w8_scales(q):
+            nc.sync.dma_start(
+                w8s[32 * q : 32 * q + 4, :].rearrange("r (a c) -> r a c", a=2).bitcast(I32),
+                w8_scales[:, 4 * q : 4 * q + 4, :].rearrange("a r c -> r a c").bitcast(I32),
+            )
 
         def load_plane(i):
             pl = row_tile(F32, f"plane{i}")
             nc.sync.dma_start(pl[:], base_v[:, i, :])
-            nc.sync.dma_start(xs_t[:, i, :], xs_v[:, i, :])
+            load_w8_scales(i)
+            nc.sync.dma_start(xs_t[i][:], xs_v[:, i, :])
             planes.append(pl)
 
         load_plane(0)
         nc.sync.dma_start(gsc[:], gs.rearrange("(a p t) -> p a t", a=2, t=4))
         nc.sync.dma_start(gmc[:], gm.rearrange("(a p t) -> p a t", a=2, t=4))
-        for g in range(2):
-            wr = stage_tile([P, 4, 512], f"wm_raw{g}")
-            nc.sync.dma_start(wr[:], wm_v[:, :, 512 * g : 512 * (g + 1)])
-            wm_raw.append(wr)
         load_plane(1)
+        wm_parts = [(256 * g, 256) for g in range(4)]
+        for c0, n in wm_parts:
+            wr = stage_tile([P, 4, n], "wm_raw")
+            nc.sync.dma_start(wr[:], wm_v[:, :, c0 : c0 + n])
+            wm_raw.append(wr)
         load_plane(2)
-        w1_raw = stage_tile([P, 2, 4, N], "w1_raw")
-        nc.sync.dma_start(w1_raw[:], w1.rearrange("(a p j) n -> p a j n", a=2, j=4))
-        load_plane(3)
-        w8c = keep.tile([P, 2, N], I32, name="w8c", align_bytes=64)
-        nc.sync.dma_start(w8c[:], w8_words.rearrange("a p c i -> p a (c i)").bitcast(I32))
         nc.sync.dma_start(l3[:], offs3)
-        for q in range(4):
-            nc.sync.dma_start(
-                w8s[32 * q : 32 * q + 4, :].rearrange("r (a c) -> r a c", a=2).bitcast(I32),
-                w8_scales[:, 4 * q : 4 * q + 4, :].rearrange("a r c -> r a c").bitcast(I32),
-            )
-        boc = keep.tile([P, 2], F32, name="boc")
         with nc.allow_non_contiguous_dma(reason="one bias value a partition"):
             nc.sync.dma_start(boc[:], bo.rearrange("(h p) -> p h", p=P))
+        load_plane(3)
 
         w4p = keep.tile([P, 2 * 2 * H], U8, name="w4p", tag="w4out", bufs=2, align_bytes=64)
         w4sp = keep.tile([P, 2 * H], U8, name="w4sp", align_bytes=64)
@@ -122,14 +126,14 @@ def tile_list_exoskeleton_gait_features_kernel(
                 w4p[:, 2 * H * a : 2 * H * (a + 1)].bitcast(U16).rearrange("p (g t m) -> p g t m", g=2, t=4),
                 w4_raw[:, a, :].bitcast(U16).rearrange("p (g m t) -> p g t m", g=2, t=4),
             )
-        nc.gpsimd.tensor_copy(
-            w4sp[:].rearrange("p (g t m) -> p g t m", g=4, t=4),
-            w4s_raw[:].rearrange("p (g m t) -> p g t m", g=4, t=4),
-        )
 
         vs0 = keep.tile([P, NP], U8, name="vs0", align_bytes=64)
         nc.vector.tensor_copy(vs0[:], ts[:].indirect(l1[:]))
         nc.gpsimd.dma_start(vs1[0:112, :].bitcast(I32), vs0[4:116, :].bitcast(I32))
+        nc.gpsimd.tensor_copy(
+            w4sp[:].rearrange("p (g t m) -> p g t m", g=4, t=4),
+            w4s_raw[:].rearrange("p (g m t) -> p g t m", g=4, t=4),
+        )
         vw = []
         for a in range(2):
             v = keep.tile([P, NP], U32, name=f"vw{a}", tag="vw", bufs=2, align_bytes=64)
@@ -151,7 +155,7 @@ def tile_list_exoskeleton_gait_features_kernel(
             )
 
         for i in range(4):
-            nc.vector.tensor_copy(planes[i][:].indirect(l2[:]), xs_t[:, i, :])
+            nc.vector.tensor_copy(planes[i][:].indirect(l2[:]), xs_t[i][:])
 
         sact0 = keep.tile([P, 4 * NP], F32, name="sact0", tag="actA", align_bytes=64)
         sact1 = [keep.tile([P, 2 * NP], F32, name=f"sact1_{k}", tag="actB", bufs=2, align_bytes=64) for k in range(2)]
@@ -187,66 +191,101 @@ def tile_list_exoskeleton_gait_features_kernel(
                     lo, hi = 512 * (jb - 1), 512 * (jb + 1)
                     scale_round(H2_ENG, h2bf[:, 4096 * a + lo : 4096 * a + hi], sact(a, lo, hi), a, 1024)
 
-        wm_bf = []
-        for g in range(2):
-            wb = bf_tile(f"wm_bf{g}")
+        wm_bf = [bf_tile(f"wm_bf{g}") for g in range(2)]
+        for (c0, n), wr in zip(wm_parts, wm_raw):
+            m0 = c0 % 512 // 4
             nc.scalar.copy(
-                wb[:].rearrange("p (t m j) -> p m j t", t=4, j=4),
-                wm_raw[g][:].rearrange("p j (m t) -> p m j t", t=4),
+                wm_bf[c0 // 512][:].rearrange("p (t m j) -> p m j t", t=4, j=4)[:, m0 : m0 + n // 4, :, :],
+                wr[:].rearrange("p j (m t) -> p m j t", t=4),
             )
-            wm_bf.append(wb)
-        w1_bf = bf_tile("w1_bf")
-        nc.scalar.copy(
-            w1_bf[:].rearrange("p (a c i j) -> p a c j i", a=2, i=4, j=4),
-            w1_raw[:].rearrange("p a j (c i) -> p a c j i", i=4),
-        )
 
-        late = keep.tile([P, 17920], U8, name="late", tag="late", align_bytes=64)
-        wmc, w1c, h2c = late[:, 0:4096], late[:, 4096:6144], late[:, 6144:14336]
-        wms, w1s, h2s = late[:, 14336:15360], late[:, 15360:15872], late[:, 15872:17920]
+        late = keep.tile([P, 4608], U8, name="late", tag="xs3", align_bytes=64)
+        wmc0, wms0, h2s = late[:, 0:2048], late[:, 2048:2560], late[:, 2560:4608]
 
         def quant(codes, scales, c0, src):
             n = src.shape[1] // 4
             nc.vector.quantize_mx(out=codes[:, 4 * c0 : 4 * (c0 + n)].bitcast(FP8X4), scales=scales[:, c0 : c0 + n], in_=src)
 
-        for g in range(2):
-            quant(wmc, wms, 512 * g, wm_bf[g][:])
-
-        stg = [stage_tile([P, 4, 512], f"stg{c}") for c in range(4)]
-        for i in range(4):
-            for c in range(4):
-                nc.sync.dma_start(stg[c][:, i, :], planes[i][:, 512 * c : 512 * (c + 1)])
-        pc = keep.tile([P, 4 * T2], U8, name="pc", align_bytes=64)
-        ps = keep.tile([P, T2], U8, name="ps", align_bytes=64)
-        for c in range(4):
-            pb = bf_tile(f"page_bf{c}")
-            dst = pb[:].rearrange("p (c i j) -> p c j i", i=4, j=4)
-            src = stg[c][:].rearrange("p j (c i) -> p c j i", i=4)
-            if c in PAGE_V:
+        def pair_copy(engine, pb, st, j0):
+            dst = pb[:].rearrange("p (c j) -> p c j", j=4)[:, :, j0 : j0 + 2]
+            src = st[:].rearrange("p j c -> p c j")
+            if engine == "vector":
                 nc.vector.tensor_copy(dst, src)
             else:
                 nc.scalar.copy(dst, src)
-            quant(pc[:], ps[:], 512 * c, pb[:])
 
-        rows = []
-        for u in range(8):
-            row = row_tile(F32, f"arow{u}")
-            for c in range(4):
-                bank = psum.tile([P, 512], F32, name="bank", tag="bank")
-                nc.tensor.matmul_mx(
-                    out=bank[:],
-                    lhsT=wmc[:, 4 * P * u : 4 * P * (u + 1)].bitcast(FP8X4),
-                    lhsT_scale=wms[:, P * u : P * (u + 1)],
-                    rhs=pc[:, 2048 * c : 2048 * (c + 1)].bitcast(FP8X4),
-                    rhs_scale=ps[:, 512 * c : 512 * (c + 1)],
-                    start=True,
-                    stop=True,
-                )
-                if 4 * u + c in EVAC_V:
-                    nc.vector.tensor_copy(row[:, 512 * c : 512 * (c + 1)], bank[:])
-                else:
-                    nc.scalar.copy(row[:, 512 * c : 512 * (c + 1)], bank[:])
-            rows.append(row)
+        page_bf = []
+        for c in range(4):
+            st = stage_tile([P, 2, 512], f"st01_{c}")
+            for i in range(2):
+                nc.sync.dma_start(st[:, i, :], planes[i][:, 512 * c : 512 * (c + 1)])
+            pb = bf_tile(f"page_bf{c}")
+            pair_copy("scalar", pb, st, 0)
+            page_bf.append(pb)
+        w1_raw = keep.tile([P, 2, 4, N], F32, name="w1_raw", tag="xs1", align_bytes=64)
+        nc.sync.dma_start(w1_raw[:], w1.rearrange("(a p j) n -> p a j n", a=2, j=4))
+        w1_bf = bf_tile("w1_bf")
+        nc.scalar.copy(
+            w1_bf[:].rearrange("p (a c i j) -> p a c j i", a=2, i=4, j=4),
+            w1_raw[:].rearrange("p a j (c i) -> p a c j i", i=4),
+        )
+        st23 = [
+            keep.tile([P, 2, 512], F32, name="st23_held", tag="late2", align_bytes=64) if c == 3 else stage_tile([P, 2, 512], f"st23_{c}")
+            for c in range(4)
+        ]
+        for c in range(4):
+            nc.sync.dma_start(st23[c][:, 0, :], planes[2][:, 512 * c : 512 * (c + 1)])
+        w8c = keep.tile([P, 2, N], I32, name="w8c", tag="xs2", align_bytes=64)
+        nc.sync.dma_start(w8c[:], w8_words.rearrange("a p c i -> p a (c i)").bitcast(I32))
+        pc = keep.tile([P, 4 * T2], U8, name="pc", align_bytes=64)
+        ps = keep.tile([P, T2], U8, name="ps", align_bytes=64)
+        quant(wmc0, wms0, 0, wm_bf[0][:])
+        for c in [0,1,2,3]:
+            last_plane = planes[3][:, 512 * c : 512 * (c + 1)]
+            if CP[c] == "V":
+                nc.vector.tensor_copy(st23[c][:, 1, :], last_plane)
+            elif CP[c] == "S":
+                nc.scalar.copy(st23[c][:, 1, :], last_plane)
+            else:
+                nc.sync.dma_start(st23[c][:, 1, :], last_plane)
+        pair_copy("scalar" if PAIR[0] == "S" else "vector", page_bf[0], st23[0], 2)
+        pair_copy("scalar" if PAIR[1] == "S" else "vector", page_bf[1], st23[1], 2)
+        quant(pc[:], ps[:], 512 * 0, page_bf[0][:])
+        pair_copy("scalar" if PAIR[2] == "S" else "vector", page_bf[2], st23[2], 2)
+        quant(pc[:], ps[:], 512 * 1, page_bf[1][:])
+        pair_copy("scalar" if PAIR[3] == "S" else "vector", page_bf[3], st23[3], 2)
+        quant(pc[:], ps[:], 512 * 2, page_bf[2][:])
+        quant(pc[:], ps[:], 512 * 3, page_bf[3][:])
+        late2 = keep.tile([P, 5120], U8, name="late2", tag="late2", align_bytes=64)
+        wmc1, w1c, wms1, w1s = late2[:, 0:2048], late2[:, 2048:4096], late2[:, 4096:4608], late2[:, 4608:5120]
+        quant(wmc1, wms1, 0, wm_bf[1][:])
+        wmc, wms = [wmc0, wmc1], [wms0, wms1]
+
+        rows = [row_tile(F32, f"arow{u}", u == 3) for u in range(8)]
+
+        def project(u, c):
+            bank = psum.tile([P, 512], F32, name="bank", tag="bank")
+            nc.tensor.matmul_mx(
+                out=bank[:],
+                lhsT=wmc[u // 4][:, 4 * P * (u % 4) : 4 * P * (u % 4 + 1)].bitcast(FP8X4),
+                lhsT_scale=wms[u // 4][:, P * (u % 4) : P * (u % 4 + 1)],
+                rhs=pc[:, 2048 * c : 2048 * (c + 1)].bitcast(FP8X4),
+                rhs_scale=ps[:, 512 * c : 512 * (c + 1)],
+                start=True,
+                stop=True,
+            )
+            if 4 * u + c in EVAC_V:
+                nc.vector.tensor_copy(rows[u][:, 512 * c : 512 * (c + 1)], bank[:])
+            else:
+                nc.scalar.copy(rows[u][:, 512 * c : 512 * (c + 1)], bank[:])
+
+        def project_row(u):
+            for c in range(2 if u < 3 else 0, 4):
+                project(u, c)
+
+        for c in range(2):
+            for u in range(3):
+                project(u, c)
 
         h1c = [keep.tile([P, NP], U32, name=f"h1c{a}", tag="vw", bufs=2, align_bytes=64) for a in range(2)]
         h1s = keep.tile([P, 2 * NP], U8, name="h1s", align_bytes=64)
@@ -255,23 +294,37 @@ def tile_list_exoskeleton_gait_features_kernel(
             for t in range(4):
                 nc.vector.tensor_copy(picked[:, t, :], rows[4 * a + t][:].indirect(l3[:, j0 // 16 : (j0 + n) // 16]))
 
-        def finish_h1(picked, a, j0, n, p0, engine):
-            th = stage_tile([P, 4 * n], f"th{a}_{j0}")
+        def squash(picked, p0, hb, h0, a, engine):
+            th = stage_tile([P, 1024], "th")
             nc.scalar.activation(
                 th[:].rearrange("p (c i t) -> p c t i", i=4, t=4),
-                picked[:, :, p0 : p0 + n].rearrange("p t (c i) -> p c t i", i=4),
+                picked[:, :, p0 : p0 + 256].rearrange("p t (c i) -> p c t i", i=4),
                 ACT.Tanh,
                 bias=zero[:],
             )
-            hb = bf_tile(f"h1bf{a}_{j0}")
-            scale_round(engine, hb[:, 0 : 4 * n], th[:], 2 + a, 4 * n)
+            scale_round(engine, hb[:, 4 * h0 : 4 * h0 + 1024], th[:], 2 + a, 1024)
+
+        def quant_h1(hb, a, j0, n):
             nc.vector.quantize_mx(
                 out=h1c[a][:, j0 : j0 + n].bitcast(FP8X4), scales=h1s[:, NP * a + j0 : NP * a + j0 + n], in_=hb[:, 0 : 4 * n]
             )
 
         chunks = [(0, 512), (512, 256), (768, 256)]
+        for u in range(4):
+            project_row(u)
         g0 = keep.tile([P, 4, NP], F32, name="g0", tag="actA", align_bytes=64)
         gather(g0, 0, 0, NP)
+        hb0 = [bf_tile(f"h1bf0_{k}") for k in range(2)]
+        for u in range(4, 6):
+            project_row(u)
+        for h0 in (0, 256):
+            squash(g0, h0, hb0[0], h0, 0, H1_ENG[h0 // 256])
+        for u in range(6, 7):
+            project_row(u)
+        for h0 in (0, 256):
+            squash(g0, 512 + h0, hb0[1], h0, 0, H1_ENG[2 + h0 // 256])
+        for u in range(7, 8):
+            project_row(u)
         g1 = [
             keep.tile([P, 4, 512], F32, name="g1_0", tag="actB", bufs=2, align_bytes=64),
             keep.tile([P, 4, 256], F32, name="g1_1", tag="actB", bufs=2, align_bytes=64),
@@ -281,11 +334,19 @@ def tile_list_exoskeleton_gait_features_kernel(
             gather(g1[k], 1, j0, n)
 
         quant(w1c, w1s, 0, w1_bf[:])
+        h2c = row_tile(U32, "h2c", True)[:].bitcast(U8)
         for k in range(4):
             quant(h2c, h2s, 512 * k, h2bf[:, 2048 * k : 2048 * (k + 1)])
         for k in range(2):
-            finish_h1(g0, 0, 512 * k, 512, 512 * k, H1_ENG[k])
+            quant_h1(hb0[k], 0, 512 * k, 512)
 
+        hb1 = [bf_tile(f"h1bf1_{k}") for k in range(3)]
+        for k, (j0, n) in enumerate(chunks):
+            for h0 in range(0, n, 256):
+                squash(g1[k], h0, hb1[k], h0, 1, H1_ENG[4 + (j0 + h0) // 256])
+            if k > 0:
+                quant_h1(hb1[k - 1], 1, *chunks[k - 1])
+        quant_h1(hb1[2], 1, *chunks[2])
         ost = [keep.tile([P, NP], F32, name=f"ost{h}", tag="w4out", bufs=2, align_bytes=64) for h in range(2)]
         for k, (j0, n) in enumerate(chunks):
             banks = []
@@ -309,7 +370,6 @@ def tile_list_exoskeleton_gait_features_kernel(
                 y_pass(h, w1c, w1s, 0, h1c[0][:, j0 : j0 + n].bitcast(FP8X4), h1s, True, False)
                 for a in range(2):
                     y_pass(h, w8b, w8s, a, h2c[:, 4 * (NP * a + j0) : 4 * (NP * a + j0 + n)].bitcast(FP8X4), h2s, False, False)
-            finish_h1(g1[k], 1, j0, n, 0, H1_ENG[2 + k])
             for h in range(2):
                 y_pass(h, w1c, w1s, 1, h1c[1][:, j0 : j0 + n].bitcast(FP8X4), h1s, False, True)
                 nc.scalar.activation(ost[h][:, j0 : j0 + n], banks[h][:], ACT.Tanh, bias=boc[:, h : h + 1])

@@ -19,7 +19,7 @@ MULT = mybir.AluOpType.mult
 P = 128
 REP = 32
 H2_ENG = "gpsimd"
-H1_ENG = ["gpsimd","gpsimd","gpsimd","gpsimd","vector","vector","vector","vector"]
+H1_ENG = ["vector","vector","vector","vector","vector","vector","vector","vector"]
 PAIR = "VVVV"
 CP = "VDDD"
 EVAC_V = []
@@ -70,7 +70,7 @@ def tile_list_exoskeleton_gait_features_kernel(
             nc.sync.dma_start(ts[32 * q : 32 * q + 8, :].bitcast(I32), tab_scales[:, 4 * q : 4 * q + 4, :].bitcast(I32))
         tabw = []
         for a in range(2):
-            tw = row_tile(I32, f"tabw{a}")
+            tw = row_tile(I32, f"tabw{a}", a == 1)
             nc.sync.dma_start(tw[:], tab_words[a].rearrange("p t i -> p (t i)").bitcast(I32))
             tabw.append(tw)
         for q in range(4):
@@ -120,7 +120,7 @@ def tile_list_exoskeleton_gait_features_kernel(
         load_plane(3)
 
         w4p = keep.tile([P, 2 * 2 * H], U8, name="w4p", tag="w4out", bufs=2, align_bytes=64)
-        w4sp = keep.tile([P, 2 * H], U8, name="w4sp", align_bytes=64)
+        w4sp = keep.tile([P, 2 * H], U8, name="w4sp", tag="lastrow", align_bytes=64)
         for a in range(2):
             nc.vector.tensor_copy(
                 w4p[:, 2 * H * a : 2 * H * (a + 1)].bitcast(U16).rearrange("p (g t m) -> p g t m", g=2, t=4),
@@ -280,11 +280,11 @@ def tile_list_exoskeleton_gait_features_kernel(
                 nc.scalar.copy(rows[u][:, 512 * c : 512 * (c + 1)], bank[:])
 
         def project_row(u):
-            for c in range(2 if u < 3 else 0, 4):
+            for c in range(2 if u < 4 else 0, 4):
                 project(u, c)
 
         for c in range(2):
-            for u in range(3):
+            for u in range(4):
                 project(u, c)
 
         h1c = [keep.tile([P, NP], U32, name=f"h1c{a}", tag="vw", bufs=2, align_bytes=64) for a in range(2)]
@@ -315,16 +315,21 @@ def tile_list_exoskeleton_gait_features_kernel(
         g0 = keep.tile([P, 4, NP], F32, name="g0", tag="actA", align_bytes=64)
         gather(g0, 0, 0, NP)
         hb0 = [bf_tile(f"h1bf0_{k}") for k in range(2)]
-        for u in range(4, 6):
-            project_row(u)
-        for h0 in (0, 256):
-            squash(g0, h0, hb0[0], h0, 0, H1_ENG[h0 // 256])
-        for u in range(6, 7):
-            project_row(u)
-        for h0 in (0, 256):
-            squash(g0, 512 + h0, hb0[1], h0, 0, H1_ENG[2 + h0 // 256])
-        for u in range(7, 8):
-            project_row(u)
+        planar = keep.tile([P, 4, 512], F32, name="planar", tag="xs1", align_bytes=64)
+        scaled = keep.tile([P, 4, 512], BF16, name="scaled", tag="xs0", align_bytes=64)
+        project_row(4)
+        project_row(5)
+        project_row(6)
+        project_row(7)
+        nc.scalar.activation(planar[:], g0[:, :, 0:512], ACT.Tanh, bias=zero[:])
+        for t in range(4):
+            nc.scalar.activation(scaled[:, t, :], planar[:, t, :], ACT.Copy, scale=gmc[:, 0, t : t + 1])
+        for j0 in range(512, NP, 256):
+            squash(g0, j0, hb0[j0 // 512], j0 % 512, 0, "vector")
+        nc.scalar.copy(
+            hb0[0][:, 0 : 4 * 512].rearrange("p (c i t) -> p c t i", i=4, t=4),
+            scaled[:].rearrange("p t (c i) -> p c t i", i=4),
+        )
         g1 = [
             keep.tile([P, 4, 512], F32, name="g1_0", tag="actB", bufs=2, align_bytes=64),
             keep.tile([P, 4, 256], F32, name="g1_1", tag="actB", bufs=2, align_bytes=64),
@@ -335,8 +340,8 @@ def tile_list_exoskeleton_gait_features_kernel(
 
         quant(w1c, w1s, 0, w1_bf[:])
         h2c = row_tile(U32, "h2c", True)[:].bitcast(U8)
-        for k in range(4):
-            quant(h2c, h2s, 512 * k, h2bf[:, 2048 * k : 2048 * (k + 1)])
+        for a in range(2):
+            quant(h2c, h2s, NP * a, h2bf[:, 4096 * a : 4096 * (a + 1)])
         for k in range(2):
             quant_h1(hb0[k], 0, 512 * k, 512)
 

@@ -20,8 +20,9 @@ P = 128
 REP = 32
 H2_ENG = "gpsimd"
 H1_ENG = ["vector","vector","vector","vector","vector","vector","vector","vector"]
-PAIR = "VVVV"
-CP = "VDDD"
+PAIR = "VSVV"
+CP = "VSDD"
+B_ENG = ["vector","vector","vector","vector"]
 EVAC_V = []
 
 
@@ -38,13 +39,13 @@ def tile_list_exoskeleton_gait_features_kernel(
         def row_tile(dtype, name, last=False):
             if last:
                 return keep.tile([P, 2048], dtype, tag="lastrow", name=name, align_bytes=64)
-            return keep.tile([P, 2048], dtype, tag="row", bufs=7, name=name, align_bytes=64)
+            return keep.tile([P, 2048], dtype, tag="row", bufs=6, name=name, align_bytes=64)
 
         def stage_tile(shape, name):
-            return keep.tile(shape, F32, tag="stage", bufs=7, name=name, align_bytes=64)
+            return keep.tile(shape, F32, tag="stage", bufs=4, name=name, align_bytes=64)
 
         def bf_tile(name):
-            return keep.tile([P, 2048], BF16, tag="bf", bufs=7, name=name, align_bytes=64)
+            return keep.tile([P, 2048], BF16, tag="bf", bufs=6, name=name, align_bytes=64)
 
         ts = keep.tile([P, T], U8, name="ts", align_bytes=64)
         w4s_raw = keep.tile([P, 2 * H], U8, name="w4s_raw", align_bytes=64)
@@ -70,7 +71,7 @@ def tile_list_exoskeleton_gait_features_kernel(
             nc.sync.dma_start(ts[32 * q : 32 * q + 8, :].bitcast(I32), tab_scales[:, 4 * q : 4 * q + 4, :].bitcast(I32))
         tabw = []
         for a in range(2):
-            tw = row_tile(I32, f"tabw{a}", a == 1)
+            tw = row_tile(I32, f"tabw{a}")
             nc.sync.dma_start(tw[:], tab_words[a].rearrange("p t i -> p (t i)").bitcast(I32))
             tabw.append(tw)
         for q in range(4):
@@ -108,19 +109,22 @@ def tile_list_exoskeleton_gait_features_kernel(
         nc.sync.dma_start(gsc[:], gs.rearrange("(a p t) -> p a t", a=2, t=4))
         nc.sync.dma_start(gmc[:], gm.rearrange("(a p t) -> p a t", a=2, t=4))
         load_plane(1)
-        wm_parts = [(256 * g, 256) for g in range(4)]
+        wm_parts = [(512 * g, 512) for g in range(2)]
         for c0, n in wm_parts:
-            wr = stage_tile([P, 4, n], "wm_raw")
+            wr = keep.tile([P, 4, n], F32, name="wm_raw", tag="pc" if c0 else "lastrow", align_bytes=64)
             nc.sync.dma_start(wr[:], wm_v[:, :, c0 : c0 + n])
             wm_raw.append(wr)
         load_plane(2)
         nc.sync.dma_start(l3[:], offs3)
         with nc.allow_non_contiguous_dma(reason="one bias value a partition"):
             nc.sync.dma_start(boc[:], bo.rearrange("(h p) -> p h", p=P))
+        w1_raw = [keep.tile([P, 4, N], F32, name=f"w1_raw{a}", tag="bf", bufs=6, align_bytes=64) for a in range(2)]
+        for a in range(2):
+            nc.sync.dma_start(w1_raw[a][:], w1[512 * a : 512 * (a + 1), :].rearrange("(p j) n -> p j n", j=4))
         load_plane(3)
 
         w4p = keep.tile([P, 2 * 2 * H], U8, name="w4p", tag="w4out", bufs=2, align_bytes=64)
-        w4sp = keep.tile([P, 2 * H], U8, name="w4sp", tag="lastrow", align_bytes=64)
+        w4sp = keep.tile([P, 2 * H], U8, name="w4sp", align_bytes=64)
         for a in range(2):
             nc.vector.tensor_copy(
                 w4p[:, 2 * H * a : 2 * H * (a + 1)].bitcast(U16).rearrange("p (g t m) -> p g t m", g=2, t=4),
@@ -191,6 +195,13 @@ def tile_list_exoskeleton_gait_features_kernel(
                     lo, hi = 512 * (jb - 1), 512 * (jb + 1)
                     scale_round(H2_ENG, h2bf[:, 4096 * a + lo : 4096 * a + hi], sact(a, lo, hi), a, 1024)
 
+        w1_bf = bf_tile("w1_bf")
+        for a in range(2):
+            nc.scalar.copy(
+                w1_bf[:, 1024 * a : 1024 * (a + 1)].rearrange("p (c i j) -> p c j i", i=4, j=4),
+                w1_raw[a][:].rearrange("p j (c i) -> p c j i", i=4),
+            )
+
         wm_bf = [bf_tile(f"wm_bf{g}") for g in range(2)]
         for (c0, n), wr in zip(wm_parts, wm_raw):
             m0 = c0 % 512 // 4
@@ -206,54 +217,45 @@ def tile_list_exoskeleton_gait_features_kernel(
             n = src.shape[1] // 4
             nc.vector.quantize_mx(out=codes[:, 4 * c0 : 4 * (c0 + n)].bitcast(FP8X4), scales=scales[:, c0 : c0 + n], in_=src)
 
-        def pair_copy(engine, pb, st, j0):
-            dst = pb[:].rearrange("p (c j) -> p c j", j=4)[:, :, j0 : j0 + 2]
-            src = st[:].rearrange("p j c -> p c j")
-            if engine == "vector":
+        def weave_page(engine, c):
+            pb = bf_tile(f"page_bf{c}")
+            dst = pb[:].rearrange("p (c i j) -> p c j i", i=4, j=4)
+            src = st23[c][:].rearrange("p j (c i) -> p c j i", i=4)
+            if engine == "V":
                 nc.vector.tensor_copy(dst, src)
             else:
                 nc.scalar.copy(dst, src)
+            page_bf[c] = pb
 
-        page_bf = []
-        for c in range(4):
-            st = stage_tile([P, 2, 512], f"st01_{c}")
-            for i in range(2):
-                nc.sync.dma_start(st[:, i, :], planes[i][:, 512 * c : 512 * (c + 1)])
-            pb = bf_tile(f"page_bf{c}")
-            pair_copy("scalar", pb, st, 0)
-            page_bf.append(pb)
-        w1_raw = keep.tile([P, 2, 4, N], F32, name="w1_raw", tag="xs1", align_bytes=64)
-        nc.sync.dma_start(w1_raw[:], w1.rearrange("(a p j) n -> p a j n", a=2, j=4))
-        w1_bf = bf_tile("w1_bf")
-        nc.scalar.copy(
-            w1_bf[:].rearrange("p (a c i j) -> p a c j i", a=2, i=4, j=4),
-            w1_raw[:].rearrange("p a j (c i) -> p a c j i", i=4),
-        )
+        page_bf = {}
         st23 = [
-            keep.tile([P, 2, 512], F32, name="st23_held", tag="late2", align_bytes=64) if c == 3 else stage_tile([P, 2, 512], f"st23_{c}")
+            keep.tile([P, 4, 512], F32, name="st_held", tag="late2", align_bytes=64)
+            if c == 3
+            else keep.tile([P, 4, 512], F32, name="st", tag="st", bufs=3, align_bytes=64)
             for c in range(4)
         ]
-        for c in range(4):
-            nc.sync.dma_start(st23[c][:, 0, :], planes[2][:, 512 * c : 512 * (c + 1)])
+        for i in range(3):
+            for c in range(4):
+                nc.sync.dma_start(st23[c][:, i, :], planes[i][:, 512 * c : 512 * (c + 1)])
         w8c = keep.tile([P, 2, N], I32, name="w8c", tag="xs2", align_bytes=64)
         nc.sync.dma_start(w8c[:], w8_words.rearrange("a p c i -> p a (c i)").bitcast(I32))
-        pc = keep.tile([P, 4 * T2], U8, name="pc", align_bytes=64)
+        pc = keep.tile([P, 4 * T2], U8, name="pc", tag="pc", align_bytes=64)
         ps = keep.tile([P, T2], U8, name="ps", align_bytes=64)
         quant(wmc0, wms0, 0, wm_bf[0][:])
         for c in [0,1,2,3]:
             last_plane = planes[3][:, 512 * c : 512 * (c + 1)]
             if CP[c] == "V":
-                nc.vector.tensor_copy(st23[c][:, 1, :], last_plane)
+                nc.vector.tensor_copy(st23[c][:, 3, :], last_plane)
             elif CP[c] == "S":
-                nc.scalar.copy(st23[c][:, 1, :], last_plane)
+                nc.scalar.copy(st23[c][:, 3, :], last_plane)
             else:
-                nc.sync.dma_start(st23[c][:, 1, :], last_plane)
-        pair_copy("scalar" if PAIR[0] == "S" else "vector", page_bf[0], st23[0], 2)
-        pair_copy("scalar" if PAIR[1] == "S" else "vector", page_bf[1], st23[1], 2)
+                nc.sync.dma_start(st23[c][:, 3, :], last_plane)
+        weave_page(PAIR[0], 0)
+        weave_page(PAIR[1], 1)
         quant(pc[:], ps[:], 512 * 0, page_bf[0][:])
-        pair_copy("scalar" if PAIR[2] == "S" else "vector", page_bf[2], st23[2], 2)
+        weave_page(PAIR[2], 2)
         quant(pc[:], ps[:], 512 * 1, page_bf[1][:])
-        pair_copy("scalar" if PAIR[3] == "S" else "vector", page_bf[3], st23[3], 2)
+        weave_page(PAIR[3], 3)
         quant(pc[:], ps[:], 512 * 2, page_bf[2][:])
         quant(pc[:], ps[:], 512 * 3, page_bf[3][:])
         late2 = keep.tile([P, 5120], U8, name="late2", tag="late2", align_bytes=64)
@@ -315,7 +317,7 @@ def tile_list_exoskeleton_gait_features_kernel(
         g0 = keep.tile([P, 4, NP], F32, name="g0", tag="actA", align_bytes=64)
         gather(g0, 0, 0, NP)
         hb0 = [bf_tile(f"h1bf0_{k}") for k in range(2)]
-        planar = keep.tile([P, 4, 512], F32, name="planar", tag="xs1", align_bytes=64)
+        planar = keep.tile([P, 4, 512], F32, name="planar", tag="st", bufs=3, align_bytes=64)
         scaled = keep.tile([P, 4, 512], BF16, name="scaled", tag="xs0", align_bytes=64)
         project_row(4)
         project_row(5)
@@ -325,7 +327,7 @@ def tile_list_exoskeleton_gait_features_kernel(
         for t in range(4):
             nc.scalar.activation(scaled[:, t, :], planar[:, t, :], ACT.Copy, scale=gmc[:, 0, t : t + 1])
         for j0 in range(512, NP, 256):
-            squash(g0, j0, hb0[j0 // 512], j0 % 512, 0, "vector")
+            squash(g0, j0, hb0[j0 // 512], j0 % 512, 0, B_ENG[j0 // 256])
         nc.scalar.copy(
             hb0[0][:, 0 : 4 * 512].rearrange("p (c i t) -> p c t i", i=4, t=4),
             scaled[:].rearrange("p t (c i) -> p c t i", i=4),
@@ -333,7 +335,7 @@ def tile_list_exoskeleton_gait_features_kernel(
         g1 = [
             keep.tile([P, 4, 512], F32, name="g1_0", tag="actB", bufs=2, align_bytes=64),
             keep.tile([P, 4, 256], F32, name="g1_1", tag="actB", bufs=2, align_bytes=64),
-            keep.tile([P, 4, 256], F32, name="g1_2", align_bytes=64),
+            keep.tile([P, 4, 256], F32, name="g1_2", tag="xs1", align_bytes=64),
         ]
         for k, (j0, n) in enumerate(chunks):
             gather(g1[k], 1, j0, n)

@@ -15,15 +15,12 @@ FP8X4 = mybir.dt.float8_e4m3fn_x4
 FP4X4 = mybir.dt.float4_e2m1fn_x4
 ACT = mybir.ActivationFunctionType
 MULT = mybir.AluOpType.mult
+ADD = mybir.AluOpType.add
 
 P = 128
 REP = 32
-H2_ENG = "gpsimd"
-H1_ENG = ["vector","vector","vector","vector","vector","vector","vector","vector"]
-PAIR = "VSVV"
-CP = "VSDD"
-B_ENG = ["vector","vector","vector","vector"]
-EVAC_V = []
+LEAD_ROWS = 2
+RANGES = [(0, 512), (512, 256), (768, 256)]
 
 
 def tile_list_exoskeleton_gait_features_kernel(
@@ -34,25 +31,22 @@ def tile_list_exoskeleton_gait_features_kernel(
         lists = ctx.enter_context(tc.tile_pool(name="lists", bufs=1))
         keep = ctx.enter_context(tc.tile_pool(name="keep", bufs=1))
         psum = ctx.enter_context(tc.psum_pool(name="psum", bufs=8))
-        eng = {"vector": nc.vector, "gpsimd": nc.gpsimd}
 
-        def row_tile(dtype, name, last=False):
-            if last:
-                return keep.tile([P, 2048], dtype, tag="lastrow", name=name, align_bytes=64)
-            return keep.tile([P, 2048], dtype, tag="row", bufs=6, name=name, align_bytes=64)
+        def sb(shape, dtype, name, tag=None, bufs=1):
+            return keep.tile(shape, dtype, name=name, tag=tag or name, bufs=bufs, align_bytes=64)
 
-        def stage_tile(shape, name):
-            return keep.tile(shape, F32, tag="stage", bufs=4, name=name, align_bytes=64)
+        def row_tile(dtype, name):
+            return sb([P, 2048], dtype, name, "row", 8)
 
-        def bf_tile(name):
-            return keep.tile([P, 2048], BF16, tag="bf", bufs=6, name=name, align_bytes=64)
+        def quant(codes, scales, src):
+            nc.vector.quantize_mx(out=codes.bitcast(FP8X4), scales=scales, in_=src)
 
-        ts = keep.tile([P, T], U8, name="ts", align_bytes=64)
-        w4s_raw = keep.tile([P, 2 * H], U8, name="w4s_raw", align_bytes=64)
-        vs1 = keep.tile([P, NP], U8, name="vs1", align_bytes=64)
-        w8s = keep.tile([P, 2 * N], U8, name="w8s", align_bytes=64)
-        zin = keep.tile([P, 1], F32, name="zin")
-        zero = keep.tile([P, 1], F32, name="zero")
+        ts = sb([P, T], U8, "ts")
+        w4s_raw = sb([P, 2 * H], U8, "w4s_raw")
+        vs1 = sb([P, NP], U8, "vs1")
+        w8s = sb([P, 2 * N], U8, "w8s")
+        zin = sb([P, 1], F32, "zin")
+        zero = sb([P, 1], F32, "zero")
         nc.vector.memset(ts[:].bitcast(I32), 0)
         nc.gpsimd.memset(zin[:], 0.0)
         nc.vector.memset(w4s_raw[:].bitcast(I32), 0)
@@ -63,10 +57,9 @@ def tile_list_exoskeleton_gait_features_kernel(
         l1 = lists.tile([P, NP // 16], U16, name="l1")
         l2 = lists.tile([P, S // 16], U16, name="l2")
         l3 = lists.tile([P, NP // 16], U16, name="l3")
+        w4_raw = sb([P, 2, 2 * H], U8, "w4_raw")
+        nc.sync.dma_start(w4_raw[:].bitcast(I32), w4_words.rearrange("a p c -> p a c").bitcast(I32))
         nc.sync.dma_start(l1[:], offs)
-        w4_raw = keep.tile([P, 2, 2 * H], U8, name="w4_raw", tag="w4out", bufs=2, align_bytes=64)
-        for a in range(2):
-            nc.sync.dma_start(w4_raw[:, a, :].bitcast(I32), w4_words[a].bitcast(I32))
         for q in range(4):
             nc.sync.dma_start(ts[32 * q : 32 * q + 8, :].bitcast(I32), tab_scales[:, 4 * q : 4 * q + 4, :].bitcast(I32))
         tabw = []
@@ -79,191 +72,192 @@ def tile_list_exoskeleton_gait_features_kernel(
                 w4s_raw[32 * q : 32 * q + 4, :].rearrange("r (a c) -> r a c", a=2).bitcast(I32),
                 w4_scales[:, 4 * q : 4 * q + 4, :].rearrange("a r c -> r a c").bitcast(I32),
             )
-        gsc = keep.tile([P, 2, 4], F32, name="gsc")
-        gmc = keep.tile([P, 2, 4], F32, name="gmc")
         nc.sync.dma_start(l2[:], offs2)
 
         base_v = base.rearrange("(p i) t -> p i t", i=4)
         xs_v = xs.rearrange("(p i) t -> p i t", i=4)
         wm_v = wm.rearrange("(p j) c -> p j c", j=4)
-        xs_t = [keep.tile([P, S], F32, name=f"xs{i}", tag=f"xs{i}", align_bytes=64) for i in range(4)]
-        planes = []
-        wm_raw = []
+        xs_t, planes = {}, {}
 
-        boc = keep.tile([P, 2], F32, name="boc")
+        def load_xs(i):
+            xs_t[i] = sb([P, S], F32, f"xs{i}")
+            nc.sync.dma_start(xs_t[i][:], xs_v[:, i, :])
 
-        def load_w8_scales(q):
+        def load_plane(i):
+            planes[i] = row_tile(F32, f"plane{i}")
+            nc.sync.dma_start(planes[i][:], base_v[:, i, :])
+
+        gsc = sb([P, 2, 4], F32, "gsc")
+        gmc = sb([P, 2, 4], F32, "gmc")
+        boc = sb([P, 2], F32, "boc")
+        wm_raw = [sb([P, 4, 512], F32, f"wm_raw{g}", "wm", 2) for g in range(2)]
+        w1_raw = sb([P, 2, 4, N], F32, "w1_raw")
+        w8c = sb([P, 2, N], I32, "w8c")
+        load_xs(2)
+        load_plane(2)
+        nc.sync.dma_start(gsc[:], gs.rearrange("(a p t) -> p a t", a=2, t=4))
+        nc.sync.dma_start(gmc[:], gm.rearrange("(a p t) -> p a t", a=2, t=4))
+        nc.sync.dma_start(l3[:], offs3)
+        for q in range(4):
             nc.sync.dma_start(
                 w8s[32 * q : 32 * q + 4, :].rearrange("r (a c) -> r a c", a=2).bitcast(I32),
                 w8_scales[:, 4 * q : 4 * q + 4, :].rearrange("a r c -> r a c").bitcast(I32),
             )
-
-        def load_plane(i):
-            pl = row_tile(F32, f"plane{i}")
-            nc.sync.dma_start(pl[:], base_v[:, i, :])
-            load_w8_scales(i)
-            nc.sync.dma_start(xs_t[i][:], xs_v[:, i, :])
-            planes.append(pl)
-
-        load_plane(0)
-        nc.sync.dma_start(gsc[:], gs.rearrange("(a p t) -> p a t", a=2, t=4))
-        nc.sync.dma_start(gmc[:], gm.rearrange("(a p t) -> p a t", a=2, t=4))
-        load_plane(1)
-        wm_parts = [(512 * g, 512) for g in range(2)]
-        for c0, n in wm_parts:
-            wr = keep.tile([P, 4, n], F32, name="wm_raw", tag="pc" if c0 else "lastrow", align_bytes=64)
-            nc.sync.dma_start(wr[:], wm_v[:, :, c0 : c0 + n])
-            wm_raw.append(wr)
-        load_plane(2)
-        nc.sync.dma_start(l3[:], offs3)
+        for i in (0, 1):
+            load_xs(i)
+            load_plane(i)
+        nc.sync.dma_start(wm_raw[0][:], wm_v[:, :, 0:512])
+        load_xs(3)
+        load_plane(3)
+        nc.sync.dma_start(wm_raw[1][:], wm_v[:, :, 512:1024])
+        nc.sync.dma_start(w1_raw[:].rearrange("p a j n -> p a (j n)"), w1.rearrange("(a p j) n -> p a (j n)", a=2, j=4))
+        nc.sync.dma_start(w8c[:], w8_words.rearrange("a p c i -> p a (c i)").bitcast(I32))
         with nc.allow_non_contiguous_dma(reason="one bias value a partition"):
             nc.sync.dma_start(boc[:], bo.rearrange("(h p) -> p h", p=P))
-        w1_raw = [keep.tile([P, 4, N], F32, name=f"w1_raw{a}", tag="bf", bufs=6, align_bytes=64) for a in range(2)]
-        for a in range(2):
-            nc.sync.dma_start(w1_raw[a][:], w1[512 * a : 512 * (a + 1), :].rearrange("(p j) n -> p j n", j=4))
-        load_plane(3)
 
-        w4p = keep.tile([P, 2 * 2 * H], U8, name="w4p", tag="w4out", bufs=2, align_bytes=64)
-        w4sp = keep.tile([P, 2 * H], U8, name="w4sp", align_bytes=64)
-        for a in range(2):
+        w4p = [sb([P, 2, H], U8, f"w4p{g}") for g in range(2)]
+        w4sp = [sb([P, 2, 512], U8, f"w4sp{g}") for g in range(2)]
+        for g in range(2):
             nc.vector.tensor_copy(
-                w4p[:, 2 * H * a : 2 * H * (a + 1)].bitcast(U16).rearrange("p (g t m) -> p g t m", g=2, t=4),
-                w4_raw[:, a, :].bitcast(U16).rearrange("p (g m t) -> p g t m", g=2, t=4),
+                w4p[g][:].bitcast(U16).rearrange("p a (t m) -> p a t m", t=4),
+                w4_raw[:, :, H * g : H * (g + 1)].bitcast(U16).rearrange("p a (m t) -> p a t m", t=4),
             )
 
-        vs0 = keep.tile([P, NP], U8, name="vs0", align_bytes=64)
+        vs0 = sb([P, NP], U8, "vs0")
         nc.vector.tensor_copy(vs0[:], ts[:].indirect(l1[:]))
         nc.gpsimd.dma_start(vs1[0:112, :].bitcast(I32), vs0[4:116, :].bitcast(I32))
-        nc.gpsimd.tensor_copy(
-            w4sp[:].rearrange("p (g t m) -> p g t m", g=4, t=4),
-            w4s_raw[:].rearrange("p (g m t) -> p g t m", g=4, t=4),
-        )
+        for g in range(2):
+            nc.gpsimd.tensor_copy(
+                w4sp[g][:].rearrange("p a (t m) -> p a t m", t=4),
+                w4s_raw[:].rearrange("p (a g m t) -> p g a t m", a=2, g=2, t=4)[:, g],
+            )
         vw = []
         for a in range(2):
-            v = keep.tile([P, NP], U32, name=f"vw{a}", tag="vw", bufs=2, align_bytes=64)
+            v = sb([P, NP], U32, f"vw{a}")
             nc.vector.tensor_copy(v[:], tabw[a][:].bitcast(U32).indirect(l1[:]))
             vw.append(v)
         vsc = [vs0, vs1]
 
-        grep = keep.tile([P, 4, REP, 4], F32, name="grep")
+        grep = sb([P, 2, REP, 4], F32, "grep")
         for a in range(2):
             nc.gpsimd.tensor_copy(grep[:, a, :, :], gsc[:, a, :].unsqueeze(1).to_broadcast([P, REP, 4]))
-        for a in range(2):
-            nc.gpsimd.tensor_copy(grep[:, 2 + a, :, :], gmc[:, a, :].unsqueeze(1).to_broadcast([P, REP, 4]))
 
-        def scale_round(engine, dst, src, which, width):
-            reps = width // (4 * REP)
-            gain = grep[:, which, :, :].rearrange("p r t -> p (r t)").unsqueeze(1).to_broadcast([P, reps, 4 * REP])
-            eng[engine].tensor_tensor(
-                dst.rearrange("p (k e) -> p k e", k=reps), src.rearrange("p (k e) -> p k e", k=reps), gain, MULT
-            )
-
-        for i in range(4):
+        def scatter(i):
             nc.vector.tensor_copy(planes[i][:].indirect(l2[:]), xs_t[i][:])
 
-        sact0 = keep.tile([P, 4 * NP], F32, name="sact0", tag="actA", align_bytes=64)
-        sact1 = [keep.tile([P, 2 * NP], F32, name=f"sact1_{k}", tag="actB", bufs=2, align_bytes=64) for k in range(2)]
-        h2bf = keep.tile([P, 2 * 4 * NP], BF16, name="h2bf", align_bytes=64)
+        for i in (2, 0, 1, 3):
+            scatter(i)
 
-        def sact(a, lo, hi):
-            if a == 0:
-                return sact0[:, lo:hi]
-            return sact1[lo // 2048][:, lo % 2048 : (hi - 1) % 2048 + 1]
-
+        sact = [sb([P, 4 * NP], F32, f"sact{a}", "act", 2) for a in range(2)]
+        h2bf = sb([P, 2 * 4 * NP], BF16, "h2bf")
         for a in range(2):
             for jb in range(8):
                 bank = psum.tile([P, 4, P], F32, name="bank", tag="bank")
                 for t in range(4):
-                    c0 = 512 * a + P * t
                     for ka in range(2):
                         nc.tensor.matmul_mx(
                             out=bank[:, t, :],
-                            lhsT=w4p[:, 2 * (H * ka + c0) : 2 * (H * ka + c0 + P)].bitcast(FP4X4),
-                            lhsT_scale=w4sp[:, H * ka + c0 : H * ka + c0 + P],
+                            lhsT=w4p[a][:, ka, 2 * P * t : 2 * P * (t + 1)].bitcast(FP4X4),
+                            lhsT_scale=w4sp[a][:, ka, P * t : P * (t + 1)],
                             rhs=vw[ka][:, P * jb : P * (jb + 1)].bitcast(FP8X4),
                             rhs_scale=vsc[ka][:, P * jb : P * (jb + 1)],
                             start=(ka == 0),
                             stop=(ka == 1),
                         )
                 nc.scalar.activation(
-                    sact(a, 512 * jb, 512 * (jb + 1)).rearrange("p (j t) -> p j t", t=4),
+                    sact[a][:, 512 * jb : 512 * (jb + 1)].rearrange("p (j t) -> p j t", t=4),
                     bank[:].rearrange("p t j -> p j t"),
                     ACT.Sin,
                     bias=zero[:],
                 )
                 if jb % 2 == 1:
                     lo, hi = 512 * (jb - 1), 512 * (jb + 1)
-                    scale_round(H2_ENG, h2bf[:, 4096 * a + lo : 4096 * a + hi], sact(a, lo, hi), a, 1024)
+                    reps = 1024 // (4 * REP)
+                    gain = grep[:, a, :, :].rearrange("p r t -> p (r t)").unsqueeze(1).to_broadcast([P, reps, 4 * REP])
+                    nc.gpsimd.tensor_tensor(
+                        h2bf[:, 4096 * a + lo : 4096 * a + hi].rearrange("p (k e) -> p k e", k=reps),
+                        sact[a][:, lo:hi].rearrange("p (k e) -> p k e", k=reps),
+                        gain,
+                        MULT,
+                    )
 
-        w1_bf = bf_tile("w1_bf")
+        pairs = [sb([P, 2, 512, 2], BF16, f"pairs{c}", tag) for c, tag in enumerate(("w4p0", "w4sp0", "vw0", "vw1"))]
+        wm_bf = [sb([P, 2048], BF16, f"wm_bf{g}", f"vs{g}") for g in range(2)]
+
+        def round_plane(copy, i, c):
+            copy(pairs[c][:, i // 2, :, i % 2], planes[i][:, 512 * c : 512 * (c + 1)])
+
+        def cast_wm(g):
+            nc.scalar.copy(
+                wm_bf[g][:].rearrange("p (t m j) -> p m j t", t=4, j=4),
+                wm_raw[g][:].rearrange("p j (m t) -> p m j t", t=4),
+            )
+
+        for c in range(4):
+            round_plane(nc.scalar.copy, 2, c)
+        cast_wm(0)
+        for c in range(4):
+            round_plane(nc.scalar.copy, 0, c)
+        for c in range(4):
+            round_plane(nc.scalar.copy, 1, c)
+        for k in range(2):
+            nc.gpsimd.tensor_scalar(
+                wm_bf[1][:].rearrange("p (t m j) -> p t m j", t=4, j=4)[:, 2 * k : 2 * (k + 1)],
+                wm_raw[1][:].rearrange("p j (m t) -> p t m j", t=4)[:, 2 * k : 2 * (k + 1)],
+                1.0,
+                0.0,
+                MULT,
+                ADD,
+            )
+
+        pw = [sb([P, 2048], BF16, f"pw{c}") for c in range(4)]
+        pc = sb([P, T2], U32, "pc")
+        ps = sb([P, T2], U8, "ps")
+        first = sb([P, 2560], U8, "first", "xs3")
+        wmc0, wms0 = first[:, 0:2048], first[:, 2048:2560]
+
+        def weave(copy, dtype, c):
+            copy(
+                pw[c][:].bitcast(dtype).rearrange("p (c u) -> p c u", u=2),
+                pairs[c][:].rearrange("p u c e -> p u (c e)").bitcast(dtype).rearrange("p u c -> p c u"),
+            )
+
+        def quant_page(c):
+            quant(pc[:, 512 * c : 512 * (c + 1)], ps[:, 512 * c : 512 * (c + 1)], pw[c][:])
+
+        quant(wmc0, wms0, wm_bf[0][:])
+        round_plane(nc.vector.tensor_copy, 3, 0)
+        round_plane(nc.vector.tensor_copy, 3, 1)
+        weave(nc.scalar.copy, U32, 0)
+        weave(nc.scalar.copy, U32, 1)
+        round_plane(nc.vector.tensor_copy, 3, 2)
+        round_plane(nc.vector.tensor_copy, 3, 3)
+        weave(nc.vector.tensor_copy, I32, 2)
+        quant_page(0)
+        weave(nc.vector.tensor_copy, I32, 3)
+        quant_page(1)
+        quant_page(2)
+        quant_page(3)
+        late = sb([P, 5120 + 8192 + 2048], U8, "late", "pw3")
+        wmc1, w1c, wms1, w1s = late[:, 0:2048], late[:, 2048:4096], late[:, 4096:4608], late[:, 4608:5120]
+        h2c, h2s = late[:, 5120 : 5120 + 8192], late[:, 5120 + 8192 :]
+        quant(wmc1, wms1, wm_bf[1][:])
         for a in range(2):
-            nc.scalar.copy(
-                w1_bf[:, 1024 * a : 1024 * (a + 1)].rearrange("p (c i j) -> p c j i", i=4, j=4),
-                w1_raw[a][:].rearrange("p j (c i) -> p c j i", i=4),
+            quant(h2c[:, 4096 * a : 4096 * (a + 1)], h2s[:, NP * a : NP * (a + 1)], h2bf[:, 4096 * a : 4096 * (a + 1)])
+        w1_bf = sb([P, 2048], BF16, "w1_bf", "h2bf")
+        for a in range(2):
+            nc.gpsimd.tensor_scalar(
+                w1_bf[:, 1024 * a : 1024 * (a + 1)].rearrange("p (c j) -> p c j", j=4),
+                w1_raw[:, a, :, :].rearrange("p j c -> p c j"),
+                1.0,
+                0.0,
+                MULT,
+                ADD,
             )
-
-        wm_bf = [bf_tile(f"wm_bf{g}") for g in range(2)]
-        for (c0, n), wr in zip(wm_parts, wm_raw):
-            m0 = c0 % 512 // 4
-            nc.scalar.copy(
-                wm_bf[c0 // 512][:].rearrange("p (t m j) -> p m j t", t=4, j=4)[:, m0 : m0 + n // 4, :, :],
-                wr[:].rearrange("p j (m t) -> p m j t", t=4),
-            )
-
-        late = keep.tile([P, 4608], U8, name="late", tag="xs3", align_bytes=64)
-        wmc0, wms0, h2s = late[:, 0:2048], late[:, 2048:2560], late[:, 2560:4608]
-
-        def quant(codes, scales, c0, src):
-            n = src.shape[1] // 4
-            nc.vector.quantize_mx(out=codes[:, 4 * c0 : 4 * (c0 + n)].bitcast(FP8X4), scales=scales[:, c0 : c0 + n], in_=src)
-
-        def weave_page(engine, c):
-            pb = bf_tile(f"page_bf{c}")
-            dst = pb[:].rearrange("p (c i j) -> p c j i", i=4, j=4)
-            src = st23[c][:].rearrange("p j (c i) -> p c j i", i=4)
-            if engine == "V":
-                nc.vector.tensor_copy(dst, src)
-            else:
-                nc.scalar.copy(dst, src)
-            page_bf[c] = pb
-
-        page_bf = {}
-        st23 = [
-            keep.tile([P, 4, 512], F32, name="st_held", tag="late2", align_bytes=64)
-            if c == 3
-            else keep.tile([P, 4, 512], F32, name="st", tag="st", bufs=3, align_bytes=64)
-            for c in range(4)
-        ]
-        for i in range(3):
-            for c in range(4):
-                nc.sync.dma_start(st23[c][:, i, :], planes[i][:, 512 * c : 512 * (c + 1)])
-        w8c = keep.tile([P, 2, N], I32, name="w8c", tag="xs2", align_bytes=64)
-        nc.sync.dma_start(w8c[:], w8_words.rearrange("a p c i -> p a (c i)").bitcast(I32))
-        pc = keep.tile([P, 4 * T2], U8, name="pc", tag="pc", align_bytes=64)
-        ps = keep.tile([P, T2], U8, name="ps", align_bytes=64)
-        quant(wmc0, wms0, 0, wm_bf[0][:])
-        for c in [0,1,2,3]:
-            last_plane = planes[3][:, 512 * c : 512 * (c + 1)]
-            if CP[c] == "V":
-                nc.vector.tensor_copy(st23[c][:, 3, :], last_plane)
-            elif CP[c] == "S":
-                nc.scalar.copy(st23[c][:, 3, :], last_plane)
-            else:
-                nc.sync.dma_start(st23[c][:, 3, :], last_plane)
-        weave_page(PAIR[0], 0)
-        weave_page(PAIR[1], 1)
-        quant(pc[:], ps[:], 512 * 0, page_bf[0][:])
-        weave_page(PAIR[2], 2)
-        quant(pc[:], ps[:], 512 * 1, page_bf[1][:])
-        weave_page(PAIR[3], 3)
-        quant(pc[:], ps[:], 512 * 2, page_bf[2][:])
-        quant(pc[:], ps[:], 512 * 3, page_bf[3][:])
-        late2 = keep.tile([P, 5120], U8, name="late2", tag="late2", align_bytes=64)
-        wmc1, w1c, wms1, w1s = late2[:, 0:2048], late2[:, 2048:4096], late2[:, 4096:4608], late2[:, 4608:5120]
-        quant(wmc1, wms1, 0, wm_bf[1][:])
         wmc, wms = [wmc0, wmc1], [wms0, wms1]
 
-        rows = [row_tile(F32, f"arow{u}", u == 3) for u in range(8)]
+        rows = [row_tile(F32, f"arow{u}") for u in range(8)]
+        picked = [sb([P, 4, NP], F32, f"picked{a}", "act", 2) for a in range(2)]
 
         def project(u, c):
             bank = psum.tile([P, 512], F32, name="bank", tag="bank")
@@ -271,95 +265,65 @@ def tile_list_exoskeleton_gait_features_kernel(
                 out=bank[:],
                 lhsT=wmc[u // 4][:, 4 * P * (u % 4) : 4 * P * (u % 4 + 1)].bitcast(FP8X4),
                 lhsT_scale=wms[u // 4][:, P * (u % 4) : P * (u % 4 + 1)],
-                rhs=pc[:, 2048 * c : 2048 * (c + 1)].bitcast(FP8X4),
+                rhs=pc[:, 512 * c : 512 * (c + 1)].bitcast(FP8X4),
                 rhs_scale=ps[:, 512 * c : 512 * (c + 1)],
                 start=True,
                 stop=True,
             )
-            if 4 * u + c in EVAC_V:
-                nc.vector.tensor_copy(rows[u][:, 512 * c : 512 * (c + 1)], bank[:])
-            else:
-                nc.scalar.copy(rows[u][:, 512 * c : 512 * (c + 1)], bank[:])
+            nc.scalar.copy(rows[u][:, 512 * c : 512 * (c + 1)], bank[:])
 
         def project_row(u):
-            for c in range(2 if u < 4 else 0, 4):
+            for c in range(4):
                 project(u, c)
 
-        for c in range(2):
-            for u in range(4):
+        def gather(u, j0, n):
+            nc.vector.tensor_copy(picked[u // 4][:, u % 4, j0 : j0 + n], rows[u][:].indirect(l3[:, j0 // 16 : (j0 + n) // 16]))
+
+        def squash(u, j0, n):
+            part = picked[u // 4][:, u % 4, j0 : j0 + n]
+            nc.scalar.activation(part, part, ACT.Tanh, bias=zero[:])
+
+        h1bf = [sb([P, 4 * NP], BF16, f"h1bf{a}", "wm", 2) for a in range(2)]
+        h1c = [sb([P, NP], U32, f"h1c{a}", f"vw{a}") for a in range(2)]
+        h1s = sb([P, 2 * NP], U8, "h1s")
+
+        def gain_h1(a, j0, n):
+            nc.vector.tensor_tensor(
+                h1bf[a][:, 4 * j0 : 4 * (j0 + n)].rearrange("p (c i t) -> p c t i", i=2, t=4),
+                picked[a][:, :, j0 : j0 + n].rearrange("p t (c i) -> p c t i", i=2),
+                gmc[:, a, :].unsqueeze(1).unsqueeze(3).to_broadcast([P, n // 2, 4, 2]),
+                MULT,
+            )
+
+        def quant_h1(a, j0, n):
+            quant(h1c[a][:, j0 : j0 + n], h1s[:, NP * a + j0 : NP * a + j0 + n], h1bf[a][:, 4 * j0 : 4 * (j0 + n)])
+
+        for c in range(4):
+            for u in range(LEAD_ROWS):
                 project(u, c)
-
-        h1c = [keep.tile([P, NP], U32, name=f"h1c{a}", tag="vw", bufs=2, align_bytes=64) for a in range(2)]
-        h1s = keep.tile([P, 2 * NP], U8, name="h1s", align_bytes=64)
-
-        def gather(picked, a, j0, n):
-            for t in range(4):
-                nc.vector.tensor_copy(picked[:, t, :], rows[4 * a + t][:].indirect(l3[:, j0 // 16 : (j0 + n) // 16]))
-
-        def squash(picked, p0, hb, h0, a, engine):
-            th = stage_tile([P, 1024], "th")
-            nc.scalar.activation(
-                th[:].rearrange("p (c i t) -> p c t i", i=4, t=4),
-                picked[:, :, p0 : p0 + 256].rearrange("p t (c i) -> p c t i", i=4),
-                ACT.Tanh,
-                bias=zero[:],
-            )
-            scale_round(engine, hb[:, 4 * h0 : 4 * h0 + 1024], th[:], 2 + a, 1024)
-
-        def quant_h1(hb, a, j0, n):
-            nc.vector.quantize_mx(
-                out=h1c[a][:, j0 : j0 + n].bitcast(FP8X4), scales=h1s[:, NP * a + j0 : NP * a + j0 + n], in_=hb[:, 0 : 4 * n]
-            )
-
-        chunks = [(0, 512), (512, 256), (768, 256)]
-        for u in range(4):
+        for u in range(LEAD_ROWS, 6):
             project_row(u)
-        g0 = keep.tile([P, 4, NP], F32, name="g0", tag="actA", align_bytes=64)
-        gather(g0, 0, 0, NP)
-        hb0 = [bf_tile(f"h1bf0_{k}") for k in range(2)]
-        planar = keep.tile([P, 4, 512], F32, name="planar", tag="st", bufs=3, align_bytes=64)
-        scaled = keep.tile([P, 4, 512], BF16, name="scaled", tag="xs0", align_bytes=64)
-        project_row(4)
-        project_row(5)
+        for u in range(6):
+            gather(u, 0, NP)
+        squash(0, 0, NP)
         project_row(6)
         project_row(7)
-        nc.scalar.activation(planar[:], g0[:, :, 0:512], ACT.Tanh, bias=zero[:])
-        for t in range(4):
-            nc.scalar.activation(scaled[:, t, :], planar[:, t, :], ACT.Copy, scale=gmc[:, 0, t : t + 1])
-        for j0 in range(512, NP, 256):
-            squash(g0, j0, hb0[j0 // 512], j0 % 512, 0, B_ENG[j0 // 256])
-        nc.scalar.copy(
-            hb0[0][:, 0 : 4 * 512].rearrange("p (c i t) -> p c t i", i=4, t=4),
-            scaled[:].rearrange("p t (c i) -> p c t i", i=4),
-        )
-        g1 = [
-            keep.tile([P, 4, 512], F32, name="g1_0", tag="actB", bufs=2, align_bytes=64),
-            keep.tile([P, 4, 256], F32, name="g1_1", tag="actB", bufs=2, align_bytes=64),
-            keep.tile([P, 4, 256], F32, name="g1_2", tag="xs1", align_bytes=64),
-        ]
-        for k, (j0, n) in enumerate(chunks):
-            gather(g1[k], 1, j0, n)
-
-        quant(w1c, w1s, 0, w1_bf[:])
-        h2c = row_tile(U32, "h2c", True)[:].bitcast(U8)
-        for a in range(2):
-            quant(h2c, h2s, NP * a, h2bf[:, 4096 * a : 4096 * (a + 1)])
+        for j0, n in RANGES:
+            for u in (6, 7):
+                gather(u, j0, n)
+        for u in range(1, 6):
+            squash(u, 0, NP)
+        quant(w1c, w1s, w1_bf[:])
         for k in range(2):
-            quant_h1(hb0[k], 0, 512 * k, 512)
+            gain_h1(0, 512 * k, 512)
+        for k in range(2):
+            quant_h1(0, 512 * k, 512)
 
-        hb1 = [bf_tile(f"h1bf1_{k}") for k in range(3)]
-        for k, (j0, n) in enumerate(chunks):
-            for h0 in range(0, n, 256):
-                squash(g1[k], h0, hb1[k], h0, 1, H1_ENG[4 + (j0 + h0) // 256])
-            if k > 0:
-                quant_h1(hb1[k - 1], 1, *chunks[k - 1])
-        quant_h1(hb1[2], 1, *chunks[2])
-        ost = [keep.tile([P, NP], F32, name=f"ost{h}", tag="w4out", bufs=2, align_bytes=64) for h in range(2)]
-        for k, (j0, n) in enumerate(chunks):
-            banks = []
-            for h in range(2):
-                bank = psum.tile([P, n], F32, name="bank", tag="bank")
-                banks.append(bank)
+        ost = [sb([P, NP], F32, f"ost{h}", tag) for h, tag in enumerate(("w4_raw", "w4p0"))]
+        w8b = w8c[:].rearrange("p a n -> p (a n)").bitcast(U8)
+
+        def finish(j0, n):
+            banks = [psum.tile([P, n], F32, name="bank", tag="bank") for h in range(2)]
 
             def y_pass(h, wc, ws, a, hc, hs, start, stop):
                 nc.tensor.matmul_mx(
@@ -372,12 +336,22 @@ def tile_list_exoskeleton_gait_features_kernel(
                     stop=stop,
                 )
 
-            w8b = w8c[:].rearrange("p a n -> p (a n)").bitcast(U8)
             for h in range(2):
-                y_pass(h, w1c, w1s, 0, h1c[0][:, j0 : j0 + n].bitcast(FP8X4), h1s, True, False)
                 for a in range(2):
-                    y_pass(h, w8b, w8s, a, h2c[:, 4 * (NP * a + j0) : 4 * (NP * a + j0 + n)].bitcast(FP8X4), h2s, False, False)
+                    y_pass(h, w8b, w8s, a, h2c[:, 4 * (NP * a + j0) : 4 * (NP * a + j0 + n)].bitcast(FP8X4), h2s, a == 0, False)
+                y_pass(h, w1c, w1s, 0, h1c[0][:, j0 : j0 + n].bitcast(FP8X4), h1s, False, False)
             for h in range(2):
                 y_pass(h, w1c, w1s, 1, h1c[1][:, j0 : j0 + n].bitcast(FP8X4), h1s, False, True)
                 nc.scalar.activation(ost[h][:, j0 : j0 + n], banks[h][:], ACT.Tanh, bias=boc[:, h : h + 1])
                 nc.sync.dma_start(out[P * h : P * (h + 1), j0 : j0 + n], ost[h][:, j0 : j0 + n])
+
+        for j0, n in RANGES:
+            for u in (6, 7):
+                squash(u, j0, n)
+        for k, (j0, n) in enumerate(RANGES):
+            gain_h1(1, j0, n)
+            if k > 0:
+                quant_h1(1, *RANGES[k - 1])
+                finish(*RANGES[k - 1])
+        quant_h1(1, *RANGES[-1])
+        finish(*RANGES[-1])

@@ -36,7 +36,7 @@ def tile_list_exoskeleton_gait_features_kernel(
             return keep.tile(shape, dtype, name=name, tag=tag or name, bufs=bufs, align_bytes=64)
 
         def row_tile(dtype, name):
-            return sb([P, 2048], dtype, name, "row", 8)
+            return sb([P, 2048], dtype, name, "row", 7)
 
         def quant(codes, scales, src):
             nc.vector.quantize_mx(out=codes.bitcast(FP8X4), scales=scales, in_=src)
@@ -238,9 +238,9 @@ def tile_list_exoskeleton_gait_features_kernel(
         quant_page(1)
         quant_page(2)
         quant_page(3)
-        late = sb([P, 5120 + 8192 + 2048], U8, "late", "pw3")
-        wmc1, w1c, wms1, w1s = late[:, 0:2048], late[:, 2048:4096], late[:, 4096:4608], late[:, 4608:5120]
-        h2c, h2s = late[:, 5120 : 5120 + 8192], late[:, 5120 + 8192 :]
+        late = sb([P, 2560 + 8192 + 2048], U8, "late", "pw3")
+        wmc1, wms1 = late[:, 0:2048], late[:, 2048:2560]
+        h2c, h2s = late[:, 2560 : 2560 + 8192], late[:, 2560 + 8192 :]
         quant(wmc1, wms1, wm_bf[1][:])
         for a in range(2):
             quant(h2c[:, 4096 * a : 4096 * (a + 1)], h2s[:, NP * a : NP * (a + 1)], h2bf[:, 4096 * a : 4096 * (a + 1)])
@@ -256,7 +256,7 @@ def tile_list_exoskeleton_gait_features_kernel(
             )
         wmc, wms = [wmc0, wmc1], [wms0, wms1]
 
-        rows = [row_tile(F32, f"arow{u}") for u in range(8)]
+        rows = [sb([P, T2], F32, "arow6") if u == 6 else row_tile(F32, f"arow{u}") for u in range(8)]
         picked = [sb([P, 4, NP], F32, f"picked{a}", "act", 2) for a in range(2)]
 
         def project(u, c):
@@ -284,7 +284,6 @@ def tile_list_exoskeleton_gait_features_kernel(
             nc.scalar.activation(part, part, ACT.Tanh, bias=zero[:])
 
         h1bf = [sb([P, 4 * NP], BF16, f"h1bf{a}", "wm", 2) for a in range(2)]
-        h1c = [sb([P, NP], U32, f"h1c{a}", f"vw{a}") for a in range(2)]
         h1s = sb([P, 2 * NP], U8, "h1s")
 
         def gain_h1(a, j0, n):
@@ -298,24 +297,39 @@ def tile_list_exoskeleton_gait_features_kernel(
         def quant_h1(a, j0, n):
             quant(h1c[a][:, j0 : j0 + n], h1s[:, NP * a + j0 : NP * a + j0 + n], h1bf[a][:, 4 * j0 : 4 * (j0 + n)])
 
+        def gain_h1_pool(j0, n):
+            nc.gpsimd.tensor_tensor(
+                h1bf[0][:, 4 * j0 : 4 * (j0 + n)].rearrange("p (j t) -> p j t", t=4),
+                picked[0][:, :, j0 : j0 + n].rearrange("p t j -> p j t"),
+                gmc[:, 0, :].unsqueeze(1).to_broadcast([P, n, 4]),
+                MULT,
+            )
+
         for c in range(4):
             for u in range(LEAD_ROWS):
                 project(u, c)
-        for u in range(LEAD_ROWS, 6):
+        for u in range(LEAD_ROWS, 4):
             project_row(u)
-        for u in range(6):
-            gather(u, 0, NP)
-        squash(0, 0, NP)
+        for k in range(2):
+            for u in range(4):
+                gather(u, 512 * k, 512)
+            project_row(4 + k)
+            for u in range(4):
+                squash(u, 512 * k, 512)
+            for j0 in (512 * k, 512 * k + 256):
+                gain_h1_pool(j0, 256)
         project_row(6)
         project_row(7)
+        for u in (4, 5, 6):
+            gather(u, 0, NP)
         for j0, n in RANGES:
-            for u in (6, 7):
-                gather(u, j0, n)
-        for u in range(1, 6):
+            gather(7, j0, n)
+        for u in (4, 5, 6):
             squash(u, 0, NP)
+        held = sb([P, 4096 + 2560], U8, "held", "arow6")
+        w1c, w1s = held[:, 4096:6144], held[:, 6144:6656]
+        h1c = [held[:, 0:4096].bitcast(U32), sb([P, NP], U32, "h1c1", "vw1")[:]]
         quant(w1c, w1s, w1_bf[:])
-        for k in range(2):
-            gain_h1(0, 512 * k, 512)
         for k in range(2):
             quant_h1(0, 512 * k, 512)
 
@@ -346,8 +360,7 @@ def tile_list_exoskeleton_gait_features_kernel(
                 nc.sync.dma_start(out[P * h : P * (h + 1), j0 : j0 + n], ost[h][:, j0 : j0 + n])
 
         for j0, n in RANGES:
-            for u in (6, 7):
-                squash(u, j0, n)
+            squash(7, j0, n)
         for k, (j0, n) in enumerate(RANGES):
             gain_h1(1, j0, n)
             if k > 0:

@@ -210,13 +210,14 @@ def tile_list_exoskeleton_gait_features_kernel(
                 ADD,
             )
 
-        pw = [sb([P, 2048], BF16, f"pw{c}") for c in range(4)]
+        pw = {}
         pc = sb([P, T2], U32, "pc")
         ps = sb([P, T2], U8, "ps")
         first = sb([P, 2560], U8, "first", "xs3")
         wmc0, wms0 = first[:, 0:2048], first[:, 2048:2560]
 
         def weave(copy, dtype, c):
+            pw[c] = sb([P, 2048], BF16, f"pw{c}", f"pw{c % 2}")
             copy(
                 pw[c][:].bitcast(dtype).rearrange("p (c u) -> p c u", u=2),
                 pairs[c][:].rearrange("p u c e -> p u (c e)").bitcast(dtype).rearrange("p u c -> p c u"),
@@ -226,22 +227,25 @@ def tile_list_exoskeleton_gait_features_kernel(
             quant(pc[:, 512 * c : 512 * (c + 1)], ps[:, 512 * c : 512 * (c + 1)], pw[c][:])
 
         quant(wmc0, wms0, wm_bf[0][:])
-        round_plane(nc.vector.tensor_copy, 3, 0)
-        round_plane(nc.vector.tensor_copy, 3, 1)
+        for c in range(4):
+            round_plane(nc.vector.tensor_copy, 3, c)
         weave(nc.scalar.copy, U32, 0)
         weave(nc.scalar.copy, U32, 1)
-        round_plane(nc.vector.tensor_copy, 3, 2)
-        round_plane(nc.vector.tensor_copy, 3, 3)
-        weave(nc.vector.tensor_copy, I32, 2)
         quant_page(0)
-        weave(nc.vector.tensor_copy, I32, 3)
+        weave(nc.vector.tensor_copy, I32, 2)
         quant_page(1)
+        weave(nc.vector.tensor_copy, I32, 3)
         quant_page(2)
         quant_page(3)
-        late = sb([P, 2560 + 8192 + 2048], U8, "late", "pw3")
+        late = sb([P, 2560 + 8192 + 2048], U8, "late", "pw1")
         wmc1, wms1 = late[:, 0:2048], late[:, 2048:2560]
         h2c, h2s = late[:, 2560 : 2560 + 8192], late[:, 2560 + 8192 :]
-        quant(wmc1, wms1, wm_bf[1][:])
+        row5 = sb([P, 640], U8, "row5", "pw0")
+        wm_codes = [wmc0[:, 512 * t : 512 * (t + 1)] for t in range(4)] + [wmc1[:, 0:512], row5[:, 0:512], wmc1[:, 1024:1536], wmc1[:, 1536:2048]]
+        wm_scales = [wms0[:, P * t : P * (t + 1)] for t in range(4)] + [wms1[:, 0:128], row5[:, 512:640], wms1[:, 256:384], wms1[:, 384:512]]
+        quant(wm_codes[4], wm_scales[4], wm_bf[1][:, 0:512])
+        quant(wm_codes[5], wm_scales[5], wm_bf[1][:, 512:1024])
+        quant(wmc1[:, 1024:2048], wms1[:, 256:512], wm_bf[1][:, 1024:2048])
         for a in range(2):
             quant(h2c[:, 4096 * a : 4096 * (a + 1)], h2s[:, NP * a : NP * (a + 1)], h2bf[:, 4096 * a : 4096 * (a + 1)])
         w1_bf = sb([P, 2048], BF16, "w1_bf", "h2bf")
@@ -254,33 +258,37 @@ def tile_list_exoskeleton_gait_features_kernel(
                 MULT,
                 ADD,
             )
-        wmc, wms = [wmc0, wmc1], [wms0, wms1]
 
-        rows = [sb([P, T2], F32, "arow6") if u == 6 else row_tile(F32, f"arow{u}") for u in range(8)]
-        picked = [sb([P, 4, NP], F32, f"picked{a}", "act", 2) for a in range(2)]
+        rows = [sb([P, T2], F32, "arow7") if u == 7 else row_tile(F32, f"arow{u}") for u in range(8)]
+        picked0 = [sb([P, 4, 512], F32, "picked0_0", "act", 2)]
+        picked1 = sb([P, 4, NP], F32, "picked1", "act", 2)
 
-        def project(u, c):
+        def picked(a, j0, n):
+            return picked1[:, :, j0 : j0 + n] if a == 1 else picked0[j0 // 512][:, :, j0 % 512 : j0 % 512 + n]
+
+
+        def project(u, c, copy=nc.scalar.copy):
             bank = psum.tile([P, 512], F32, name="bank", tag="bank")
             nc.tensor.matmul_mx(
                 out=bank[:],
-                lhsT=wmc[u // 4][:, 4 * P * (u % 4) : 4 * P * (u % 4 + 1)].bitcast(FP8X4),
-                lhsT_scale=wms[u // 4][:, P * (u % 4) : P * (u % 4 + 1)],
+                lhsT=wm_codes[u].bitcast(FP8X4),
+                lhsT_scale=wm_scales[u],
                 rhs=pc[:, 512 * c : 512 * (c + 1)].bitcast(FP8X4),
                 rhs_scale=ps[:, 512 * c : 512 * (c + 1)],
                 start=True,
                 stop=True,
             )
-            nc.scalar.copy(rows[u][:, 512 * c : 512 * (c + 1)], bank[:])
+            copy(rows[u][:, 512 * c : 512 * (c + 1)], bank[:])
 
         def project_row(u):
             for c in range(4):
                 project(u, c)
 
         def gather(u, j0, n):
-            nc.vector.tensor_copy(picked[u // 4][:, u % 4, j0 : j0 + n], rows[u][:].indirect(l3[:, j0 // 16 : (j0 + n) // 16]))
+            nc.vector.tensor_copy(picked(u // 4, j0, n)[:, u % 4, :], rows[u][:].indirect(l3[:, j0 // 16 : (j0 + n) // 16]))
 
         def squash(u, j0, n):
-            part = picked[u // 4][:, u % 4, j0 : j0 + n]
+            part = picked(u // 4, j0, n)[:, u % 4, :]
             nc.scalar.activation(part, part, ACT.Tanh, bias=zero[:])
 
         h1bf = [sb([P, 4 * NP], BF16, f"h1bf{a}", "wm", 2) for a in range(2)]
@@ -289,7 +297,7 @@ def tile_list_exoskeleton_gait_features_kernel(
         def gain_h1(a, j0, n):
             nc.vector.tensor_tensor(
                 h1bf[a][:, 4 * j0 : 4 * (j0 + n)].rearrange("p (c i t) -> p c t i", i=2, t=4),
-                picked[a][:, :, j0 : j0 + n].rearrange("p t (c i) -> p c t i", i=2),
+                picked(a, j0, n).rearrange("p t (c i) -> p c t i", i=2),
                 gmc[:, a, :].unsqueeze(1).unsqueeze(3).to_broadcast([P, n // 2, 4, 2]),
                 MULT,
             )
@@ -300,7 +308,7 @@ def tile_list_exoskeleton_gait_features_kernel(
         def gain_h1_pool(j0, n):
             nc.gpsimd.tensor_tensor(
                 h1bf[0][:, 4 * j0 : 4 * (j0 + n)].rearrange("p (j t) -> p j t", t=4),
-                picked[0][:, :, j0 : j0 + n].rearrange("p t j -> p j t"),
+                picked(0, j0, n).rearrange("p t j -> p j t"),
                 gmc[:, 0, :].unsqueeze(1).to_broadcast([P, n, 4]),
                 MULT,
             )
@@ -309,15 +317,24 @@ def tile_list_exoskeleton_gait_features_kernel(
             for u in range(LEAD_ROWS):
                 project(u, c)
         for u in range(LEAD_ROWS, 4):
-            project_row(u)
-        for k in range(2):
-            for u in range(4):
-                gather(u, 512 * k, 512)
-            project_row(4 + k)
-            for u in range(4):
-                squash(u, 512 * k, 512)
-            for j0 in (512 * k, 512 * k + 256):
-                gain_h1_pool(j0, 256)
+            for c in range(4):
+                project(u, c, nc.vector.tensor_copy if (u, c) == (3, 3) else nc.scalar.copy)
+        for u in range(4):
+            gather(u, 0, 512)
+        for c in range(2):
+            project(4, c)
+        for u in range(4):
+            squash(u, 0, 512)
+        for c in range(2, 4):
+            project(4, c)
+        project_row(5)
+        picked0.append(sb([P, 4, 512], F32, "picked0_1", "pw0"))
+        for u in range(4):
+            gather(u, 512, 512)
+        for u in range(4):
+            squash(u, 512, 512)
+        for j0 in range(0, NP, 256):
+            gain_h1_pool(j0, 256)
         project_row(6)
         project_row(7)
         for u in (4, 5, 6):
@@ -326,7 +343,7 @@ def tile_list_exoskeleton_gait_features_kernel(
             gather(7, j0, n)
         for u in (4, 5, 6):
             squash(u, 0, NP)
-        held = sb([P, 4096 + 2560], U8, "held", "arow6")
+        held = sb([P, 4096 + 2560], U8, "held", "arow7")
         w1c, w1s = held[:, 4096:6144], held[:, 6144:6656]
         h1c = [held[:, 0:4096].bitcast(U32), sb([P, NP], U32, "h1c1", "vw1")[:]]
         quant(w1c, w1s, w1_bf[:])
@@ -361,10 +378,31 @@ def tile_list_exoskeleton_gait_features_kernel(
 
         for j0, n in RANGES:
             squash(7, j0, n)
-        for k, (j0, n) in enumerate(RANGES):
-            gain_h1(1, j0, n)
-            if k > 0:
-                quant_h1(1, *RANGES[k - 1])
-                finish(*RANGES[k - 1])
-        quant_h1(1, *RANGES[-1])
-        finish(*RANGES[-1])
+
+        def scale_h1(j0, n):
+            hp = sb([P, 2, n, 2], BF16, f"h1_pairs{j0}")
+            for t in range(4):
+                nc.scalar.activation(hp[:, t // 2, :, t % 2], picked1[:, t, j0 : j0 + n], ACT.Copy, scale=gmc[:, 1, t : t + 1])
+            return hp
+
+        def weave_h1(hp, j0, n):
+            nc.vector.tensor_copy(
+                h1bf[1][:, 4 * j0 : 4 * (j0 + n)].bitcast(I32).rearrange("p (c u) -> p c u", u=2),
+                hp[:].rearrange("p u c e -> p u (c e)").bitcast(I32).rearrange("p u c -> p c u"),
+            )
+
+        Q = NP // 4
+        hp2 = scale_h1(2 * Q, Q)
+        hp3 = scale_h1(3 * Q, Q)
+        gain_h1(1, 0, Q)
+        gain_h1(1, Q, Q)
+        quant_h1(1, 0, Q)
+        finish(0, Q)
+        weave_h1(hp2, 2 * Q, Q)
+        quant_h1(1, Q, Q)
+        finish(Q, Q)
+        weave_h1(hp3, 3 * Q, Q)
+        quant_h1(1, 2 * Q, Q)
+        finish(2 * Q, Q)
+        quant_h1(1, 3 * Q, Q)
+        finish(3 * Q, Q)

@@ -57,11 +57,13 @@ def tile_list_exoskeleton_gait_features_kernel(
         l1 = lists.tile([P, NP // 16], U16, name="l1")
         l2 = lists.tile([P, S // 16], U16, name="l2")
         l3 = lists.tile([P, NP // 16], U16, name="l3")
-        w4_raw = sb([P, 2, 2 * H], U8, "w4_raw")
-        nc.sync.dma_start(w4_raw[:].bitcast(I32), w4_words.rearrange("a p c -> p a c").bitcast(I32))
+        w4_raw = [sb([P, 2, H], U8, f"w4_raw{g}") for g in range(2)]
+        for g in range(2):
+            nc.sync.dma_start(w4_raw[g][:].bitcast(I32), w4_words[:, :, H * g : H * (g + 1)].rearrange("a p c -> p a c").bitcast(I32))
         nc.sync.dma_start(l1[:], offs)
-        for q in range(4):
-            nc.sync.dma_start(ts[32 * q : 32 * q + 8, :].bitcast(I32), tab_scales[:, 4 * q : 4 * q + 4, :].bitcast(I32))
+        ts_rows = tab_scales.rearrange("a (q r) t -> r q a t", r=4)
+        for r in range(4):
+            nc.sync.dma_start(ts[r:P:16, :].bitcast(I32), ts_rows[r].bitcast(I32))
         tabw = []
         for a in range(2):
             tw = row_tile(I32, f"tabw{a}")
@@ -93,8 +95,10 @@ def tile_list_exoskeleton_gait_features_kernel(
         wm_raw = [sb([P, 4, 512], F32, f"wm_raw{g}", "wm", 2) for g in range(2)]
         w1_raw = sb([P, 2, 4, N], F32, "w1_raw")
         w8c = sb([P, 2, N], I32, "w8c")
-        load_xs(2)
+        xs2 = [sb([P, S // 2], F32, f"xs2_{k}") for k in range(2)]
+        nc.sync.dma_start(xs2[0][:], xs_v[:, 2, 0 : S // 2])
         load_plane(2)
+        nc.sync.dma_start(xs2[1][:], xs_v[:, 2, S // 2 : S])
         nc.sync.dma_start(gsc[:], gs.rearrange("(a p t) -> p a t", a=2, t=4))
         nc.sync.dma_start(gmc[:], gm.rearrange("(a p t) -> p a t", a=2, t=4))
         nc.sync.dma_start(l3[:], offs3)
@@ -120,12 +124,12 @@ def tile_list_exoskeleton_gait_features_kernel(
         for g in range(2):
             nc.vector.tensor_copy(
                 w4p[g][:].bitcast(U16).rearrange("p a (t m) -> p a t m", t=4),
-                w4_raw[:, :, H * g : H * (g + 1)].bitcast(U16).rearrange("p a (m t) -> p a t m", t=4),
+                w4_raw[g][:].bitcast(U16).rearrange("p a (m t) -> p a t m", t=4),
             )
 
         vs0 = sb([P, NP], U8, "vs0")
         nc.vector.tensor_copy(vs0[:], ts[:].indirect(l1[:]))
-        nc.gpsimd.dma_start(vs1[0:112, :].bitcast(I32), vs0[4:116, :].bitcast(I32))
+        nc.gpsimd.dma_start(vs1[0:112, :].bitcast(I32), vs0[16:128, :].bitcast(I32))
         for g in range(2):
             nc.gpsimd.tensor_copy(
                 w4sp[g][:].rearrange("p a (t m) -> p a t m", t=4),
@@ -145,7 +149,9 @@ def tile_list_exoskeleton_gait_features_kernel(
         def scatter(i):
             nc.vector.tensor_copy(planes[i][:].indirect(l2[:]), xs_t[i][:])
 
-        for i in (2, 0, 1, 3):
+        for k in range(2):
+            nc.vector.tensor_copy(planes[2][:].indirect(l2[:, 32 * k : 32 * (k + 1)]), xs2[k][:])
+        for i in (0, 1, 3):
             scatter(i)
 
         sact = [sb([P, 4 * NP], F32, f"sact{a}", "act", 2) for a in range(2)]
@@ -213,8 +219,7 @@ def tile_list_exoskeleton_gait_features_kernel(
         pw = {}
         pc = sb([P, T2], U32, "pc")
         ps = sb([P, T2], U8, "ps")
-        first = sb([P, 2560], U8, "first", "xs3")
-        wmc0, wms0 = first[:, 0:2048], first[:, 2048:2560]
+        first = sb([P, 3840], U8, "first", "xs3")
 
         def weave(copy, dtype, c):
             pw[c] = sb([P, 2048], BF16, f"pw{c}", f"pw{c % 2}")
@@ -226,9 +231,11 @@ def tile_list_exoskeleton_gait_features_kernel(
         def quant_page(c):
             quant(pc[:, 512 * c : 512 * (c + 1)], ps[:, 512 * c : 512 * (c + 1)], pw[c][:])
 
-        quant(wmc0, wms0, wm_bf[0][:])
-        for c in range(4):
+        round_plane(nc.scalar.copy, 3, 0)
+        quant(first[:, 0:2048], first[:, 3072:3584], wm_bf[0][:])
+        for c in range(1, 4):
             round_plane(nc.vector.tensor_copy, 3, c)
+        quant(first[:, 2048:3072], first[:, 3584:3840], wm_bf[1][:, 0:1024])
         weave(nc.scalar.copy, U32, 0)
         weave(nc.scalar.copy, U32, 1)
         quant_page(0)
@@ -237,15 +244,11 @@ def tile_list_exoskeleton_gait_features_kernel(
         weave(nc.vector.tensor_copy, I32, 3)
         quant_page(2)
         quant_page(3)
-        late = sb([P, 2560 + 8192 + 2048], U8, "late", "pw1")
-        wmc1, wms1 = late[:, 0:2048], late[:, 2048:2560]
-        h2c, h2s = late[:, 2560 : 2560 + 8192], late[:, 2560 + 8192 :]
-        row5 = sb([P, 640], U8, "row5", "pw0")
-        wm_codes = [wmc0[:, 512 * t : 512 * (t + 1)] for t in range(4)] + [wmc1[:, 0:512], row5[:, 0:512], wmc1[:, 1024:1536], wmc1[:, 1536:2048]]
-        wm_scales = [wms0[:, P * t : P * (t + 1)] for t in range(4)] + [wms1[:, 0:128], row5[:, 512:640], wms1[:, 256:384], wms1[:, 384:512]]
-        quant(wm_codes[4], wm_scales[4], wm_bf[1][:, 0:512])
-        quant(wm_codes[5], wm_scales[5], wm_bf[1][:, 512:1024])
-        quant(wmc1[:, 1024:2048], wms1[:, 256:512], wm_bf[1][:, 1024:2048])
+        late = sb([P, 1280 + 8192 + 2048], U8, "late", "pw1")
+        h2c, h2s = late[:, 1280 : 1280 + 8192], late[:, 1280 + 8192 :]
+        quant(late[:, 0:1024], late[:, 1024:1280], wm_bf[1][:, 1024:2048])
+        wm_codes = [first[:, 512 * u : 512 * (u + 1)] for u in range(6)] + [late[:, 512 * u : 512 * (u + 1)] for u in range(2)]
+        wm_scales = [first[:, 3072 + P * u : 3072 + P * (u + 1)] for u in range(6)] + [late[:, 1024 + P * u : 1024 + P * (u + 1)] for u in range(2)]
         for a in range(2):
             quant(h2c[:, 4096 * a : 4096 * (a + 1)], h2s[:, NP * a : NP * (a + 1)], h2bf[:, 4096 * a : 4096 * (a + 1)])
         w1_bf = sb([P, 2048], BF16, "w1_bf", "h2bf")
@@ -287,8 +290,8 @@ def tile_list_exoskeleton_gait_features_kernel(
         def gather(u, j0, n):
             nc.vector.tensor_copy(picked(u // 4, j0, n)[:, u % 4, :], rows[u][:].indirect(l3[:, j0 // 16 : (j0 + n) // 16]))
 
-        def squash(u, j0, n):
-            part = picked(u // 4, j0, n)[:, u % 4, :]
+        def squash(u, j0, n, count=1):
+            part = picked(u // 4, j0, n)[:, u % 4 : u % 4 + count, :]
             nc.scalar.activation(part, part, ACT.Tanh, bias=zero[:])
 
         h1bf = [sb([P, 4 * NP], BF16, f"h1bf{a}", "wm", 2) for a in range(2)]
@@ -321,28 +324,27 @@ def tile_list_exoskeleton_gait_features_kernel(
                 project(u, c, nc.vector.tensor_copy if (u, c) == (3, 3) else nc.scalar.copy)
         for u in range(4):
             gather(u, 0, 512)
-        for c in range(2):
+        for c in range(3):
             project(4, c)
-        for u in range(4):
-            squash(u, 0, 512)
-        for c in range(2, 4):
-            project(4, c)
+        for j0 in (0, 256):
+            squash(0, j0, 256, 4)
+        project(4, 3)
         project_row(5)
-        picked0.append(sb([P, 4, 512], F32, "picked0_1", "pw0"))
+        picked0.append(sb([P, 4, 512], F32, "picked0_1", "xs3"))
         for u in range(4):
             gather(u, 512, 512)
-        for u in range(4):
-            squash(u, 512, 512)
+        squash(0, 512, 512, 4)
         for j0 in range(0, NP, 256):
             gain_h1_pool(j0, 256)
-        project_row(6)
+        for c in range(4):
+            project(6, c, nc.vector.tensor_copy if c == 3 else nc.scalar.copy)
         project_row(7)
         for u in (4, 5, 6):
             gather(u, 0, NP)
         for j0, n in RANGES:
             gather(7, j0, n)
-        for u in (4, 5, 6):
-            squash(u, 0, NP)
+        squash(4, 0, NP, 2)
+        squash(6, 0, NP)
         held = sb([P, 4096 + 2560], U8, "held", "arow7")
         w1c, w1s = held[:, 4096:6144], held[:, 6144:6656]
         h1c = [held[:, 0:4096].bitcast(U32), sb([P, NP], U32, "h1c1", "vw1")[:]]
@@ -350,7 +352,7 @@ def tile_list_exoskeleton_gait_features_kernel(
         for k in range(2):
             quant_h1(0, 512 * k, 512)
 
-        ost = [sb([P, NP], F32, f"ost{h}", tag) for h, tag in enumerate(("w4_raw", "w4p0"))]
+        ost = [sb([P, NP], F32, f"ost{h}", tag) for h, tag in enumerate(("w4_raw0", "w4p0"))]
         w8b = w8c[:].rearrange("p a n -> p (a n)").bitcast(U8)
 
         def finish(j0, n):

@@ -20,7 +20,8 @@ ADD = mybir.AluOpType.add
 P = 128
 REP = 32
 LEAD_ROWS = 2
-RANGES = [(0, 512), (512, 256), (768, 256)]
+CHUNK_ORDER = (2, 0, 1, 3)
+RANGES = [(0, 512), (512, 512)]
 
 
 def tile_list_exoskeleton_gait_features_kernel(
@@ -36,7 +37,7 @@ def tile_list_exoskeleton_gait_features_kernel(
             return keep.tile(shape, dtype, name=name, tag=tag or name, bufs=bufs, align_bytes=64)
 
         def row_tile(dtype, name):
-            return sb([P, 2048], dtype, name, "row", 7)
+            return sb([P, 2048], dtype, name, "row", 6)
 
         def quant(codes, scales, src):
             nc.vector.quantize_mx(out=codes.bitcast(FP8X4), scales=scales, in_=src)
@@ -86,7 +87,7 @@ def tile_list_exoskeleton_gait_features_kernel(
             nc.sync.dma_start(xs_t[i][:], xs_v[:, i, :])
 
         def load_plane(i):
-            planes[i] = row_tile(F32, f"plane{i}")
+            planes[i] = sb([P, T2], F32, "plane3") if i == 3 else row_tile(F32, f"plane{i}")
             nc.sync.dma_start(planes[i][:], base_v[:, i, :])
 
         gsc = sb([P, 2, 4], F32, "gsc")
@@ -111,9 +112,9 @@ def tile_list_exoskeleton_gait_features_kernel(
             load_xs(i)
             load_plane(i)
         nc.sync.dma_start(wm_raw[0][:], wm_v[:, :, 0:512])
+        nc.sync.dma_start(wm_raw[1][:], wm_v[:, :, 512:1024])
         load_xs(3)
         load_plane(3)
-        nc.sync.dma_start(wm_raw[1][:], wm_v[:, :, 512:1024])
         nc.sync.dma_start(w1_raw[:].rearrange("p a j n -> p a (j n)"), w1.rearrange("(a p j) n -> p a (j n)", a=2, j=4))
         nc.sync.dma_start(w8c[:], w8_words.rearrange("a p c i -> p a (c i)").bitcast(I32))
         with nc.allow_non_contiguous_dma(reason="one bias value a partition"):
@@ -187,11 +188,21 @@ def tile_list_exoskeleton_gait_features_kernel(
                         MULT,
                     )
 
-        pairs = [sb([P, 2, 512, 2], BF16, f"pairs{c}", tag) for c, tag in enumerate(("w4p0", "w4sp0", "vw0", "vw1"))]
+        pairs01 = [sb([P, 2, 512, 2], BF16, f"pairs{c}", tag) for c, tag in enumerate(("w4p0", "w4sp0"))]
+        pairs23 = sb([P, 2, 1024, 2], BF16, "pairs23", "vw0")
+        pairs = [pairs01[0][:], pairs01[1][:], pairs23[:, :, 0:512, :], pairs23[:, :, 512:1024, :]]
         wm_bf = [sb([P, 2048], BF16, f"wm_bf{g}", f"vs{g}") for g in range(2)]
 
         def round_plane(copy, i, c):
             copy(pairs[c][:, i // 2, :, i % 2], planes[i][:, 512 * c : 512 * (c + 1)])
+
+        def round_upper(copy, i):
+            copy(pairs23[:, i // 2, :, i % 2], planes[i][:, 1024:2048])
+
+        def round_early(i):
+            for c in range(2):
+                round_plane(nc.scalar.copy, i, c)
+            round_upper(nc.scalar.copy, i)
 
         def cast_wm(g):
             nc.scalar.copy(
@@ -199,13 +210,10 @@ def tile_list_exoskeleton_gait_features_kernel(
                 wm_raw[g][:].rearrange("p j (m t) -> p m j t", t=4),
             )
 
-        for c in range(4):
-            round_plane(nc.scalar.copy, 2, c)
+        round_early(2)
         cast_wm(0)
-        for c in range(4):
-            round_plane(nc.scalar.copy, 0, c)
-        for c in range(4):
-            round_plane(nc.scalar.copy, 1, c)
+        round_early(0)
+        round_early(1)
         for k in range(2):
             nc.gpsimd.tensor_scalar(
                 wm_bf[1][:].rearrange("p (t m j) -> p t m j", t=4, j=4)[:, 2 * k : 2 * (k + 1)],
@@ -222,33 +230,34 @@ def tile_list_exoskeleton_gait_features_kernel(
         first = sb([P, 3840], U8, "first", "xs3")
 
         def weave(copy, dtype, c):
-            pw[c] = sb([P, 2048], BF16, f"pw{c}", f"pw{c % 2}")
+            pw[c] = sb([P, 2048], BF16, f"pw{c}", f"pw{min(c, 2)}")
             copy(
                 pw[c][:].bitcast(dtype).rearrange("p (c u) -> p c u", u=2),
-                pairs[c][:].rearrange("p u c e -> p u (c e)").bitcast(dtype).rearrange("p u c -> p c u"),
+                pairs[c].rearrange("p u c e -> p u (c e)").bitcast(dtype).rearrange("p u c -> p c u"),
             )
 
         def quant_page(c):
             quant(pc[:, 512 * c : 512 * (c + 1)], ps[:, 512 * c : 512 * (c + 1)], pw[c][:])
 
-        round_plane(nc.scalar.copy, 3, 0)
+        for c in range(2):
+            round_plane(nc.scalar.copy, 3, c)
         quant(first[:, 0:2048], first[:, 3072:3584], wm_bf[0][:])
-        for c in range(1, 4):
-            round_plane(nc.vector.tensor_copy, 3, c)
+        round_upper(nc.vector.tensor_copy, 3)
+        for c in range(2):
+            weave(nc.scalar.copy, U32, c)
         quant(first[:, 2048:3072], first[:, 3584:3840], wm_bf[1][:, 0:1024])
-        weave(nc.scalar.copy, U32, 0)
-        weave(nc.scalar.copy, U32, 1)
-        quant_page(0)
         weave(nc.vector.tensor_copy, I32, 2)
-        quant_page(1)
-        weave(nc.vector.tensor_copy, I32, 3)
+        second = sb([P, 1280], U8, "second", "plane3")
+        quant(second[:, 0:1024], second[:, 1024:1280], wm_bf[1][:, 1024:2048])
         quant_page(2)
+        quant_page(0)
+        weave(nc.vector.tensor_copy, I32, 3)
+        quant_page(1)
         quant_page(3)
-        late = sb([P, 1280 + 8192 + 2048], U8, "late", "pw1")
-        h2c, h2s = late[:, 1280 : 1280 + 8192], late[:, 1280 + 8192 :]
-        quant(late[:, 0:1024], late[:, 1024:1280], wm_bf[1][:, 1024:2048])
-        wm_codes = [first[:, 512 * u : 512 * (u + 1)] for u in range(6)] + [late[:, 512 * u : 512 * (u + 1)] for u in range(2)]
-        wm_scales = [first[:, 3072 + P * u : 3072 + P * (u + 1)] for u in range(6)] + [late[:, 1024 + P * u : 1024 + P * (u + 1)] for u in range(2)]
+        late = sb([P, 8192 + 2048], U8, "late", "pw2")
+        h2c, h2s = late[:, 0:8192], late[:, 8192:]
+        wm_codes = [first[:, 512 * u : 512 * (u + 1)] for u in range(6)] + [second[:, 512 * u : 512 * (u + 1)] for u in range(2)]
+        wm_scales = [first[:, 3072 + P * u : 3072 + P * (u + 1)] for u in range(6)] + [second[:, 1024 + P * u : 1024 + P * (u + 1)] for u in range(2)]
         for a in range(2):
             quant(h2c[:, 4096 * a : 4096 * (a + 1)], h2s[:, NP * a : NP * (a + 1)], h2bf[:, 4096 * a : 4096 * (a + 1)])
         w1_bf = sb([P, 2048], BF16, "w1_bf", "h2bf")
@@ -316,7 +325,7 @@ def tile_list_exoskeleton_gait_features_kernel(
                 MULT,
             )
 
-        for c in range(4):
+        for c in CHUNK_ORDER:
             for u in range(LEAD_ROWS):
                 project(u, c)
         for u in range(LEAD_ROWS, 4):
@@ -382,7 +391,7 @@ def tile_list_exoskeleton_gait_features_kernel(
             squash(7, j0, n)
 
         def scale_h1(j0, n):
-            hp = sb([P, 2, n, 2], BF16, f"h1_pairs{j0}")
+            hp = sb([P, 2, n, 2], BF16, f"h1_pairs{j0}", "pw0")
             for t in range(4):
                 nc.scalar.activation(hp[:, t // 2, :, t % 2], picked1[:, t, j0 : j0 + n], ACT.Copy, scale=gmc[:, 1, t : t + 1])
             return hp
@@ -390,20 +399,19 @@ def tile_list_exoskeleton_gait_features_kernel(
         def weave_h1(hp, j0, n):
             nc.vector.tensor_copy(
                 h1bf[1][:, 4 * j0 : 4 * (j0 + n)].bitcast(I32).rearrange("p (c u) -> p c u", u=2),
-                hp[:].rearrange("p u c e -> p u (c e)").bitcast(I32).rearrange("p u c -> p c u"),
+                hp.rearrange("p u c e -> p u (c e)").bitcast(I32).rearrange("p u c -> p c u"),
             )
 
         Q = NP // 4
-        hp2 = scale_h1(2 * Q, Q)
-        hp3 = scale_h1(3 * Q, Q)
+        hp = scale_h1(2 * Q, 2 * Q)
         gain_h1(1, 0, Q)
         gain_h1(1, Q, Q)
         quant_h1(1, 0, Q)
         finish(0, Q)
-        weave_h1(hp2, 2 * Q, Q)
+        weave_h1(hp[:, :, 0:Q, :], 2 * Q, Q)
         quant_h1(1, Q, Q)
         finish(Q, Q)
-        weave_h1(hp3, 3 * Q, Q)
+        weave_h1(hp[:, :, Q : 2 * Q, :], 3 * Q, Q)
         quant_h1(1, 2 * Q, Q)
         finish(2 * Q, Q)
         quant_h1(1, 3 * Q, Q)

@@ -65,17 +65,20 @@ def tile_list_exoskeleton_gait_features_kernel(
         ts_rows = tab_scales.rearrange("a (q r) t -> r q a t", r=4)
         for r in range(4):
             nc.sync.dma_start(ts[r:P:16, :].bitcast(I32), ts_rows[r].bitcast(I32))
-        tabw = []
-        for a in range(2):
-            tw = row_tile(I32, f"tabw{a}")
-            nc.sync.dma_start(tw[:], tab_words[a].rearrange("p t i -> p (t i)").bitcast(I32))
-            tabw.append(tw)
+        tabw = [row_tile(I32, f"tabw{a}") for a in range(2)]
+
+        def load_table(a):
+            nc.sync.dma_start(tabw[a][:], tab_words[a].rearrange("p t i -> p (t i)").bitcast(I32))
+
+        load_table(0)
         for q in range(4):
             nc.sync.dma_start(
                 w4s_raw[32 * q : 32 * q + 4, :].rearrange("r (a c) -> r a c", a=2).bitcast(I32),
                 w4_scales[:, 4 * q : 4 * q + 4, :].rearrange("a r c -> r a c").bitcast(I32),
             )
-        nc.sync.dma_start(l2[:], offs2)
+        load_table(1)
+        gsc = sb([P, 2, 4], F32, "gsc")
+        nc.sync.dma_start(gsc[:], gs.rearrange("(a p t) -> p a t", a=2, t=4))
 
         base_v = base.rearrange("(p i) t -> p i t", i=4)
         xs_v = xs.rearrange("(p i) t -> p i t", i=4)
@@ -90,7 +93,6 @@ def tile_list_exoskeleton_gait_features_kernel(
             planes[i] = sb([P, T2], F32, "plane3") if i == 3 else row_tile(F32, f"plane{i}")
             nc.sync.dma_start(planes[i][:], base_v[:, i, :])
 
-        gsc = sb([P, 2, 4], F32, "gsc")
         gmc = sb([P, 2, 4], F32, "gmc")
         boc = sb([P, 2], F32, "boc")
         wm_raw = [sb([P, 4, 512], F32, f"wm_raw{g}", "wm", 2) for g in range(2)]
@@ -99,8 +101,8 @@ def tile_list_exoskeleton_gait_features_kernel(
         xs2 = [sb([P, S // 2], F32, f"xs2_{k}") for k in range(2)]
         nc.sync.dma_start(xs2[0][:], xs_v[:, 2, 0 : S // 2])
         load_plane(2)
+        nc.sync.dma_start(l2[:], offs2)
         nc.sync.dma_start(xs2[1][:], xs_v[:, 2, S // 2 : S])
-        nc.sync.dma_start(gsc[:], gs.rearrange("(a p t) -> p a t", a=2, t=4))
         nc.sync.dma_start(gmc[:], gm.rearrange("(a p t) -> p a t", a=2, t=4))
         nc.sync.dma_start(l3[:], offs3)
         for q in range(4):
@@ -108,11 +110,10 @@ def tile_list_exoskeleton_gait_features_kernel(
                 w8s[32 * q : 32 * q + 4, :].rearrange("r (a c) -> r a c", a=2).bitcast(I32),
                 w8_scales[:, 4 * q : 4 * q + 4, :].rearrange("a r c -> r a c").bitcast(I32),
             )
-        for i in (0, 1):
-            load_xs(i)
-            load_plane(i)
-        nc.sync.dma_start(wm_raw[0][:], wm_v[:, :, 0:512])
-        nc.sync.dma_start(wm_raw[1][:], wm_v[:, :, 512:1024])
+        for g in range(2):
+            load_xs(g)
+            load_plane(g)
+            nc.sync.dma_start(wm_raw[g][:], wm_v[:, :, 512 * g : 512 * (g + 1)])
         load_xs(3)
         load_plane(3)
         nc.sync.dma_start(w1_raw[:].rearrange("p a j n -> p a (j n)"), w1.rearrange("(a p j) n -> p a (j n)", a=2, j=4))
@@ -214,15 +215,12 @@ def tile_list_exoskeleton_gait_features_kernel(
         cast_wm(0)
         round_early(0)
         round_early(1)
-        for k in range(2):
-            nc.gpsimd.tensor_scalar(
-                wm_bf[1][:].rearrange("p (t m j) -> p t m j", t=4, j=4)[:, 2 * k : 2 * (k + 1)],
-                wm_raw[1][:].rearrange("p j (m t) -> p t m j", t=4)[:, 2 * k : 2 * (k + 1)],
-                1.0,
-                0.0,
-                MULT,
-                ADD,
-            )
+        wm_src = wm_raw[1][:].rearrange("p j (m t) -> p t m j", t=4)
+        nc.gpsimd.tensor_scalar(wm_bf[1][:, 0:1024].rearrange("p (t m j) -> p t m j", t=2, j=4), wm_src[:, 0:2], 1.0, 0.0, MULT, ADD)
+        nc.scalar.copy(
+            wm_bf[1][:, 1024:2048].rearrange("p (t m j) -> p m j t", t=2, j=4),
+            wm_raw[1][:].rearrange("p j (m t) -> p m j t", t=4)[:, :, :, 2:4],
+        )
 
         pw = {}
         pc = sb([P, T2], U32, "pc")
@@ -254,7 +252,7 @@ def tile_list_exoskeleton_gait_features_kernel(
         weave(nc.vector.tensor_copy, I32, 3)
         quant_page(1)
         quant_page(3)
-        late = sb([P, 8192 + 2048], U8, "late", "pw2")
+        late = sb([P, 8192 + 2048], U8, "late", "pw1")
         h2c, h2s = late[:, 0:8192], late[:, 8192:]
         wm_codes = [first[:, 512 * u : 512 * (u + 1)] for u in range(6)] + [second[:, 512 * u : 512 * (u + 1)] for u in range(2)]
         wm_scales = [first[:, 3072 + P * u : 3072 + P * (u + 1)] for u in range(6)] + [second[:, 1024 + P * u : 1024 + P * (u + 1)] for u in range(2)]
@@ -330,23 +328,23 @@ def tile_list_exoskeleton_gait_features_kernel(
                 project(u, c)
         for u in range(LEAD_ROWS, 4):
             for c in range(4):
-                project(u, c, nc.vector.tensor_copy if (u, c) == (3, 3) else nc.scalar.copy)
+                project(u, c, nc.vector.tensor_copy if (u, c) in ((3, 2), (3, 3)) else nc.scalar.copy)
         for u in range(4):
             gather(u, 0, 512)
-        for c in range(3):
-            project(4, c)
+        project_row(4)
         for j0 in (0, 256):
             squash(0, j0, 256, 4)
-        project(4, 3)
         project_row(5)
+        project(6, 0)
         picked0.append(sb([P, 4, 512], F32, "picked0_1", "xs3"))
         for u in range(4):
             gather(u, 512, 512)
-        squash(0, 512, 512, 4)
+        for j0 in (512, 768):
+            squash(0, j0, 256, 4)
         for j0 in range(0, NP, 256):
             gain_h1_pool(j0, 256)
-        for c in range(4):
-            project(6, c, nc.vector.tensor_copy if c == 3 else nc.scalar.copy)
+        for c in range(1, 4):
+            project(6, c)
         project_row(7)
         for u in (4, 5, 6):
             gather(u, 0, NP)

@@ -20,6 +20,7 @@ ADD = mybir.AluOpType.add
 P = 128
 REP = 32
 LEAD_ROWS = 2
+FIRST = 256
 CHUNK_ORDER = (2, 0, 1, 3)
 RANGES = [(0, 512), (512, 512)]
 
@@ -58,9 +59,9 @@ def tile_list_exoskeleton_gait_features_kernel(
         l1 = lists.tile([P, NP // 16], U16, name="l1")
         l2 = lists.tile([P, S // 16], U16, name="l2")
         l3 = lists.tile([P, NP // 16], U16, name="l3")
-        w4_raw = [sb([P, 2, H], U8, f"w4_raw{g}") for g in range(2)]
-        for g in range(2):
-            nc.sync.dma_start(w4_raw[g][:].bitcast(I32), w4_words[:, :, H * g : H * (g + 1)].rearrange("a p c -> p a c").bitcast(I32))
+        w4_raw = [sb([P, 2 * H], U8, f"w4_raw{a}") for a in range(2)]
+        for a in range(2):
+            nc.sync.dma_start(w4_raw[a][:].bitcast(I32), w4_words[a].bitcast(I32))
         nc.sync.dma_start(l1[:], offs)
         ts_rows = tab_scales.rearrange("a (q r) t -> r q a t", r=4)
         for r in range(4):
@@ -77,8 +78,7 @@ def tile_list_exoskeleton_gait_features_kernel(
                 w4_scales[:, 4 * q : 4 * q + 4, :].rearrange("a r c -> r a c").bitcast(I32),
             )
         load_table(1)
-        gsc = sb([P, 2, 4], F32, "gsc")
-        nc.sync.dma_start(gsc[:], gs.rearrange("(a p t) -> p a t", a=2, t=4))
+        nc.sync.dma_start(l2[:], offs2)
 
         base_v = base.rearrange("(p i) t -> p i t", i=4)
         xs_v = xs.rearrange("(p i) t -> p i t", i=4)
@@ -98,11 +98,12 @@ def tile_list_exoskeleton_gait_features_kernel(
         wm_raw = [sb([P, 4, 512], F32, f"wm_raw{g}", "wm", 2) for g in range(2)]
         w1_raw = sb([P, 2, 4, N], F32, "w1_raw")
         w8c = sb([P, 2, N], I32, "w8c")
-        xs2 = [sb([P, S // 2], F32, f"xs2_{k}") for k in range(2)]
-        nc.sync.dma_start(xs2[0][:], xs_v[:, 2, 0 : S // 2])
+        xs2 = [sb([P, n], F32, f"xs2_{k}") for k, n in enumerate((FIRST, S - FIRST))]
+        nc.sync.dma_start(xs2[0][:], xs_v[:, 2, 0:FIRST])
         load_plane(2)
-        nc.sync.dma_start(l2[:], offs2)
-        nc.sync.dma_start(xs2[1][:], xs_v[:, 2, S // 2 : S])
+        gsc = sb([P, 2, 4], F32, "gsc")
+        nc.sync.dma_start(gsc[:], gs.rearrange("(a p t) -> p a t", a=2, t=4))
+        nc.sync.dma_start(xs2[1][:], xs_v[:, 2, FIRST:S])
         nc.sync.dma_start(gmc[:], gm.rearrange("(a p t) -> p a t", a=2, t=4))
         nc.sync.dma_start(l3[:], offs3)
         for q in range(4):
@@ -121,12 +122,12 @@ def tile_list_exoskeleton_gait_features_kernel(
         with nc.allow_non_contiguous_dma(reason="one bias value a partition"):
             nc.sync.dma_start(boc[:], bo.rearrange("(h p) -> p h", p=P))
 
-        w4p = [sb([P, 2, H], U8, f"w4p{g}") for g in range(2)]
+        w4p = [sb([P, 2, H], U8, f"w4p{a}") for a in range(2)]
         w4sp = [sb([P, 2, 512], U8, f"w4sp{g}") for g in range(2)]
-        for g in range(2):
+        for a in range(2):
             nc.vector.tensor_copy(
-                w4p[g][:].bitcast(U16).rearrange("p a (t m) -> p a t m", t=4),
-                w4_raw[g][:].bitcast(U16).rearrange("p a (m t) -> p a t m", t=4),
+                w4p[a][:].bitcast(U16).rearrange("p g (t m) -> p g t m", t=4),
+                w4_raw[a][:].bitcast(U16).rearrange("p (g m t) -> p g t m", g=2, t=4),
             )
 
         vs0 = sb([P, NP], U8, "vs0")
@@ -151,8 +152,8 @@ def tile_list_exoskeleton_gait_features_kernel(
         def scatter(i):
             nc.vector.tensor_copy(planes[i][:].indirect(l2[:]), xs_t[i][:])
 
-        for k in range(2):
-            nc.vector.tensor_copy(planes[2][:].indirect(l2[:, 32 * k : 32 * (k + 1)]), xs2[k][:])
+        nc.vector.tensor_copy(planes[2][:].indirect(l2[:, 0 : FIRST // 16]), xs2[0][:])
+        nc.vector.tensor_copy(planes[2][:].indirect(l2[:, FIRST // 16 : S // 16]), xs2[1][:])
         for i in (0, 1, 3):
             scatter(i)
 
@@ -165,7 +166,7 @@ def tile_list_exoskeleton_gait_features_kernel(
                     for ka in range(2):
                         nc.tensor.matmul_mx(
                             out=bank[:, t, :],
-                            lhsT=w4p[a][:, ka, 2 * P * t : 2 * P * (t + 1)].bitcast(FP4X4),
+                            lhsT=w4p[ka][:, a, 2 * P * t : 2 * P * (t + 1)].bitcast(FP4X4),
                             lhsT_scale=w4sp[a][:, ka, P * t : P * (t + 1)],
                             rhs=vw[ka][:, P * jb : P * (jb + 1)].bitcast(FP8X4),
                             rhs_scale=vsc[ka][:, P * jb : P * (jb + 1)],
@@ -189,7 +190,7 @@ def tile_list_exoskeleton_gait_features_kernel(
                         MULT,
                     )
 
-        pairs01 = [sb([P, 2, 512, 2], BF16, f"pairs{c}", tag) for c, tag in enumerate(("w4p0", "w4sp0"))]
+        pairs01 = [sb([P, 2, 512, 2], BF16, f"pairs{c}", tag) for c, tag in enumerate(("w4sp0", "w4p0"))]
         pairs23 = sb([P, 2, 1024, 2], BF16, "pairs23", "vw0")
         pairs = [pairs01[0][:], pairs01[1][:], pairs23[:, :, 0:512, :], pairs23[:, :, 512:1024, :]]
         wm_bf = [sb([P, 2048], BF16, f"wm_bf{g}", f"vs{g}") for g in range(2)]

@@ -324,8 +324,11 @@ def tile_list_exoskeleton_gait_features_kernel(
                 MULT,
             )
 
-        for c in CHUNK_ORDER:
+        for c in CHUNK_ORDER[:2]:
             for u in range(LEAD_ROWS):
+                project(u, c)
+        for u in range(LEAD_ROWS):
+            for c in CHUNK_ORDER[2:]:
                 project(u, c)
         for u in range(LEAD_ROWS, 4):
             for c in range(4):
@@ -390,7 +393,7 @@ def tile_list_exoskeleton_gait_features_kernel(
             squash(7, j0, n)
 
         def scale_h1(j0, n):
-            hp = sb([P, 2, n, 2], BF16, f"h1_pairs{j0}", "pw0")
+            hp = sb([P, 2, n, 2], BF16, f"h1_pairs{j0}")
             for t in range(4):
                 nc.scalar.activation(hp[:, t // 2, :, t % 2], picked1[:, t, j0 : j0 + n], ACT.Copy, scale=gmc[:, 1, t : t + 1])
             return hp
@@ -402,16 +405,16 @@ def tile_list_exoskeleton_gait_features_kernel(
             )
 
         Q = NP // 4
-        hp = scale_h1(2 * Q, 2 * Q)
+        hp = [scale_h1(j0, Q) for j0 in (2 * Q, 3 * Q)]
         gain_h1(1, 0, Q)
         gain_h1(1, Q, Q)
         quant_h1(1, 0, Q)
         finish(0, Q)
-        weave_h1(hp[:, :, 0:Q, :], 2 * Q, Q)
+        weave_h1(hp[0][:], 2 * Q, Q)
         quant_h1(1, Q, Q)
         finish(Q, Q)
-        weave_h1(hp[:, :, Q : 2 * Q, :], 3 * Q, Q)
         quant_h1(1, 2 * Q, Q)
         finish(2 * Q, Q)
+        weave_h1(hp[1][:], 3 * Q, Q)
         quant_h1(1, 3 * Q, Q)
         finish(3 * Q, Q)

@@ -18,11 +18,29 @@ MULT = mybir.AluOpType.mult
 ADD = mybir.AluOpType.add
 
 P = 128
+KB = 1024
 REP = 32
-LEAD_ROWS = 2
 FIRST = 256
-CHUNK_ORDER = (2, 0, 1, 3)
-RANGES = [(0, 512), (512, 512)]
+CH = 512
+Q = 256
+
+TAB = 0
+SIN_EXTRA = 16 * KB
+PLANE = 24 * KB
+XS = 56 * KB
+WM_RAW = 72 * KB
+W1_RAW = 88 * KB
+H2BF = 96 * KB
+PAIRS = 112 * KB
+WOVEN = 128 * KB
+WM_BF = 144 * KB
+PAGE_C = 152 * KB
+PAGE_S = 160 * KB
+VW = 162 * KB
+W4_RAW = 170 * KB
+VS = 174 * KB
+SMALL = 178 * KB
+LATE = 192 * KB
 
 
 def tile_list_exoskeleton_gait_features_kernel(
@@ -32,45 +50,69 @@ def tile_list_exoskeleton_gait_features_kernel(
     with ExitStack() as ctx:
         lists = ctx.enter_context(tc.tile_pool(name="lists", bufs=1))
         keep = ctx.enter_context(tc.tile_pool(name="keep", bufs=1))
-        psum = ctx.enter_context(tc.psum_pool(name="psum", bufs=8))
+        psum = ctx.enter_context(tc.psum_pool(name="psum", bufs=1))
 
-        def sb(shape, dtype, name, tag=None, bufs=1):
-            return keep.tile(shape, dtype, name=name, tag=tag or name, bufs=bufs, align_bytes=64)
+        def sb(shape, dtype, name, offset):
+            return keep.tile(shape, dtype, name=name, align_bytes=64, offset=offset)
 
-        def row_tile(dtype, name):
-            return sb([P, 2048], dtype, name, "row", 6)
+        ring = list(range(8))
+
+        def next_bank(shape, name, again=True):
+            slot = ring.pop(0)
+            if again:
+                ring.append(slot)
+            return psum.tile(shape, F32, name=name, offset=2 * KB * slot)
 
         def quant(codes, scales, src):
             nc.vector.quantize_mx(out=codes.bitcast(FP8X4), scales=scales, in_=src)
 
-        ts = sb([P, T], U8, "ts")
-        w4s_raw = sb([P, 2 * H], U8, "w4s_raw")
-        vs1 = sb([P, NP], U8, "vs1")
-        w8s = sb([P, 2 * N], U8, "w8s")
-        zin = sb([P, 1], F32, "zin")
-        zero = sb([P, 1], F32, "zero")
+        ts = sb([P, T], U8, "ts", SMALL)
+        w4s_raw = sb([P, 2 * H], U8, "w4s_raw", SMALL + 2 * KB)
+        vs = [sb([P, NP], U8, f"vs{a}", VS + KB * a) for a in range(2)]
+        w4sp = [sb([P, 2, 512], U8, f"w4sp{g}", at) for g, at in enumerate((PAIRS + 12 * KB - 512, SMALL + 6 * KB))]
+        grep = sb([P, 2, REP, 4], F32, "grep", SMALL + 7 * KB)
+        w8c = sb([P, 2, N], I32, "w8c", SMALL + 8 * KB)
+        w8s = sb([P, 2 * N], U8, "w8s", SMALL + 10 * KB)
+        gsc = sb([P, 2, 4], F32, "gsc", SMALL + 11 * KB)
+        gmc = sb([P, 2, 4], F32, "gmc", SMALL + 11 * KB + 64)
+        boc = sb([P, 2], F32, "boc", SMALL + 11 * KB + 128)
+        zin = sb([P, 1], F32, "zin", SMALL + 11 * KB + 192)
+        zero = sb([P, 1], F32, "zero", SMALL + 11 * KB + 256)
         nc.vector.memset(ts[:].bitcast(I32), 0)
         nc.gpsimd.memset(zin[:], 0.0)
         nc.vector.memset(w4s_raw[:].bitcast(I32), 0)
-        nc.gpsimd.memset(vs1[:].bitcast(I32), 0)
+        nc.gpsimd.memset(vs[1][:].bitcast(I32), 0)
         nc.gpsimd.memset(w8s[:].bitcast(I32), 0)
         nc.scalar.activation(zero[:], zin[:], ACT.Silu)
 
         l1 = lists.tile([P, NP // 16], U16, name="l1")
         l2 = lists.tile([P, S // 16], U16, name="l2")
         l3 = lists.tile([P, NP // 16], U16, name="l3")
-        w4_raw = [sb([P, 2 * H], U8, f"w4_raw{a}") for a in range(2)]
-        for a in range(2):
-            nc.sync.dma_start(w4_raw[a][:].bitcast(I32), w4_words[a].bitcast(I32))
-        nc.sync.dma_start(l1[:], offs)
-        ts_rows = tab_scales.rearrange("a (q r) t -> r q a t", r=4)
-        for r in range(4):
-            nc.sync.dma_start(ts[r:P:16, :].bitcast(I32), ts_rows[r].bitcast(I32))
-        tabw = [row_tile(I32, f"tabw{a}") for a in range(2)]
+        w4_raw = [sb([P, 2, H], U8, f"w4_raw{g}", W4_RAW + 2 * KB * g) for g in range(2)]
+        tabw = [sb([P, T], I32, f"tabw{a}", TAB + 8 * KB * a) for a in range(2)]
+        planes = [sb([P, T2], F32, f"plane{i}", PLANE + 8 * KB * i) for i in range(4)]
+        xs2 = [sb([P, FIRST], F32, "xs2a", XS + 8 * KB), sb([P, S - FIRST], F32, "xs2b", XS + 8 * KB + 4 * FIRST)]
+        xs_t = {i: sb([P, S], F32, f"xs{i}", XS + 4 * KB * i) for i in (0, 1, 3)}
+        wm_raw = [sb([P, 4, 512], F32, f"wm_raw{g}", WM_RAW + 8 * KB * g) for g in range(2)]
+        w1_raw = sb([P, 2, 4, N], F32, "w1_raw", W1_RAW)
+        base_v = base.rearrange("(p i) t -> p i t", i=4)
+        xs_v = xs.rearrange("(p i) t -> p i t", i=4)
+        wm_v = wm.rearrange("(p j) c -> p j c", j=4)
+
+        def load_w4(g):
+            nc.sync.dma_start(w4_raw[g][:].bitcast(I32), w4_words[:, :, H * g : H * (g + 1)].rearrange("a p c -> p a c").bitcast(I32))
+
+        def load_scale_rows(tile, rows):
+            by_row = rows.rearrange("a (q r) t -> r q a t", r=4)
+            for r in range(4):
+                nc.sync.dma_start(tile[r:P:16, :].bitcast(I32), by_row[r].bitcast(I32))
 
         def load_table(a):
             nc.sync.dma_start(tabw[a][:], tab_words[a].rearrange("p t i -> p (t i)").bitcast(I32))
 
+        load_w4(0)
+        nc.sync.dma_start(l1[:], offs)
+        load_scale_rows(ts, tab_scales)
         load_table(0)
         for q in range(4):
             nc.sync.dma_start(
@@ -79,31 +121,11 @@ def tile_list_exoskeleton_gait_features_kernel(
             )
         load_table(1)
         nc.sync.dma_start(l2[:], offs2)
-
-        base_v = base.rearrange("(p i) t -> p i t", i=4)
-        xs_v = xs.rearrange("(p i) t -> p i t", i=4)
-        wm_v = wm.rearrange("(p j) c -> p j c", j=4)
-        xs_t, planes = {}, {}
-
-        def load_xs(i):
-            xs_t[i] = sb([P, S], F32, f"xs{i}")
-            nc.sync.dma_start(xs_t[i][:], xs_v[:, i, :])
-
-        def load_plane(i):
-            planes[i] = sb([P, T2], F32, "plane3") if i == 3 else row_tile(F32, f"plane{i}")
-            nc.sync.dma_start(planes[i][:], base_v[:, i, :])
-
-        gmc = sb([P, 2, 4], F32, "gmc")
-        boc = sb([P, 2], F32, "boc")
-        wm_raw = [sb([P, 4, 512], F32, f"wm_raw{g}", "wm", 2) for g in range(2)]
-        w1_raw = sb([P, 2, 4, N], F32, "w1_raw")
-        w8c = sb([P, 2, N], I32, "w8c")
-        xs2 = [sb([P, n], F32, f"xs2_{k}") for k, n in enumerate((FIRST, S - FIRST))]
         nc.sync.dma_start(xs2[0][:], xs_v[:, 2, 0:FIRST])
-        load_plane(2)
-        gsc = sb([P, 2, 4], F32, "gsc")
+        nc.sync.dma_start(planes[2][:], base_v[:, 2, :])
         nc.sync.dma_start(gsc[:], gs.rearrange("(a p t) -> p a t", a=2, t=4))
         nc.sync.dma_start(xs2[1][:], xs_v[:, 2, FIRST:S])
+        load_w4(1)
         nc.sync.dma_start(gmc[:], gm.rearrange("(a p t) -> p a t", a=2, t=4))
         nc.sync.dma_start(l3[:], offs3)
         for q in range(4):
@@ -111,155 +133,137 @@ def tile_list_exoskeleton_gait_features_kernel(
                 w8s[32 * q : 32 * q + 4, :].rearrange("r (a c) -> r a c", a=2).bitcast(I32),
                 w8_scales[:, 4 * q : 4 * q + 4, :].rearrange("a r c -> r a c").bitcast(I32),
             )
-        for g in range(2):
-            load_xs(g)
-            load_plane(g)
-            nc.sync.dma_start(wm_raw[g][:], wm_v[:, :, 512 * g : 512 * (g + 1)])
-        load_xs(3)
-        load_plane(3)
+        for i in (0, 1, 3):
+            nc.sync.dma_start(xs_t[i][:], xs_v[:, i, :])
+            nc.sync.dma_start(planes[i][:], base_v[:, i, :])
+            if i < 2:
+                nc.sync.dma_start(wm_raw[i][:], wm_v[:, :, 512 * i : 512 * (i + 1)])
         nc.sync.dma_start(w1_raw[:].rearrange("p a j n -> p a (j n)"), w1.rearrange("(a p j) n -> p a (j n)", a=2, j=4))
         nc.sync.dma_start(w8c[:], w8_words.rearrange("a p c i -> p a (c i)").bitcast(I32))
         with nc.allow_non_contiguous_dma(reason="one bias value a partition"):
             nc.sync.dma_start(boc[:], bo.rearrange("(h p) -> p h", p=P))
 
-        w4p = [sb([P, 2, H], U8, f"w4p{a}") for a in range(2)]
-        w4sp = [sb([P, 2, 512], U8, f"w4sp{g}") for g in range(2)]
-        for a in range(2):
-            nc.vector.tensor_copy(
-                w4p[a][:].bitcast(U16).rearrange("p g (t m) -> p g t m", t=4),
-                w4_raw[a][:].bitcast(U16).rearrange("p (g m t) -> p g t m", g=2, t=4),
+        w4p = [sb([P, 2, H], U8, f"w4p{g}", at) for g, at in enumerate((PAIRS + 3 * KB, VS + 2 * KB))]
+
+        def order_w4(copy, g):
+            copy(
+                w4p[g][:].bitcast(U16).rearrange("p a (t m) -> p a t m", t=4),
+                w4_raw[g][:].bitcast(U16).rearrange("p a (m t) -> p a t m", t=4),
             )
 
-        vs0 = sb([P, NP], U8, "vs0")
-        nc.vector.tensor_copy(vs0[:], ts[:].indirect(l1[:]))
-        nc.gpsimd.dma_start(vs1[0:112, :].bitcast(I32), vs0[16:128, :].bitcast(I32))
+        def move_second_pass(dst, src):
+            nc.gpsimd.dma_start(dst[0:112, :].bitcast(I32), src[16:128, :].bitcast(I32))
+
+        order_w4(nc.vector.tensor_copy, 0)
+
+        nc.vector.tensor_copy(vs[0][:], ts[:].indirect(l1[:]))
+        move_second_pass(vs[1], vs[0])
         for g in range(2):
             nc.gpsimd.tensor_copy(
                 w4sp[g][:].rearrange("p a (t m) -> p a t m", t=4),
                 w4s_raw[:].rearrange("p (a g m t) -> p g a t m", a=2, g=2, t=4)[:, g],
             )
-        vw = []
+        vw = [sb([P, NP], U32, f"vw{a}", VW + 4 * KB * a) for a in range(2)]
         for a in range(2):
-            v = sb([P, NP], U32, f"vw{a}")
-            nc.vector.tensor_copy(v[:], tabw[a][:].bitcast(U32).indirect(l1[:]))
-            vw.append(v)
-        vsc = [vs0, vs1]
-
-        grep = sb([P, 2, REP, 4], F32, "grep")
+            nc.vector.tensor_copy(vw[a][:], tabw[a][:].bitcast(U32).indirect(l1[:]))
         for a in range(2):
-            nc.gpsimd.tensor_copy(grep[:, a, :, :], gsc[:, a, :].unsqueeze(1).to_broadcast([P, REP, 4]))
-
-        def scatter(i):
-            nc.vector.tensor_copy(planes[i][:].indirect(l2[:]), xs_t[i][:])
+            nc.gpsimd.tensor_scalar(grep[:, a, :, :], gsc[:, a, :].unsqueeze(1).to_broadcast([P, REP, 4]), 1.0, 0.0, MULT, ADD)
 
         nc.vector.tensor_copy(planes[2][:].indirect(l2[:, 0 : FIRST // 16]), xs2[0][:])
         nc.vector.tensor_copy(planes[2][:].indirect(l2[:, FIRST // 16 : S // 16]), xs2[1][:])
         for i in (0, 1, 3):
-            scatter(i)
+            nc.vector.tensor_copy(planes[i][:].indirect(l2[:]), xs_t[i][:])
 
-        sact = [sb([P, 4 * NP], F32, f"sact{a}", "act", 2) for a in range(2)]
-        h2bf = sb([P, 2 * 4 * NP], BF16, "h2bf")
-        for a in range(2):
-            for jb in range(8):
-                bank = psum.tile([P, 4, P], F32, name="bank", tag="bank")
-                for t in range(4):
-                    for ka in range(2):
-                        nc.tensor.matmul_mx(
-                            out=bank[:, t, :],
-                            lhsT=w4p[ka][:, a, 2 * P * t : 2 * P * (t + 1)].bitcast(FP4X4),
-                            lhsT_scale=w4sp[a][:, ka, P * t : P * (t + 1)],
-                            rhs=vw[ka][:, P * jb : P * (jb + 1)].bitcast(FP8X4),
-                            rhs_scale=vsc[ka][:, P * jb : P * (jb + 1)],
-                            start=(ka == 0),
-                            stop=(ka == 1),
-                        )
-                nc.scalar.activation(
-                    sact[a][:, 512 * jb : 512 * (jb + 1)].rearrange("p (j t) -> p j t", t=4),
-                    bank[:].rearrange("p t j -> p j t"),
-                    ACT.Sin,
-                    bias=zero[:],
-                )
-                if jb % 2 == 1:
-                    lo, hi = 512 * (jb - 1), 512 * (jb + 1)
-                    reps = 1024 // (4 * REP)
-                    gain = grep[:, a, :, :].rearrange("p r t -> p (r t)").unsqueeze(1).to_broadcast([P, reps, 4 * REP])
-                    nc.gpsimd.tensor_tensor(
-                        h2bf[:, 4096 * a + lo : 4096 * a + hi].rearrange("p (k e) -> p k e", k=reps),
-                        sact[a][:, lo:hi].rearrange("p (k e) -> p k e", k=reps),
-                        gain,
-                        MULT,
+        h2bf = [sb([P, 4 * NP], BF16, f"h2bf{g}", H2BF + 8 * KB * g) for g in range(2)]
+        for g in range(2):
+            for pair in range(4):
+                sines = sb([P, 2, 512], F32, f"sines{g}{pair}", TAB + 4 * KB * ((4 * g + pair) % 6))
+                for half in range(2):
+                    j0 = P * (2 * pair + half)
+                    bank = next_bank([P, 4, P], f"phase{g}{pair}{half}")
+                    for t in range(4):
+                        for ka in range(2):
+                            nc.tensor.matmul_mx(
+                                out=bank[:, t, :],
+                                lhsT=w4p[g][:, ka, 2 * P * t : 2 * P * (t + 1)].bitcast(FP4X4),
+                                lhsT_scale=w4sp[g][:, ka, P * t : P * (t + 1)],
+                                rhs=vw[ka][:, j0 : j0 + P].bitcast(FP8X4),
+                                rhs_scale=vs[ka][:, j0 : j0 + P],
+                                start=(ka == 0),
+                                stop=(ka == 1),
+                            )
+                    nc.scalar.activation(
+                        sines[:, half, :].rearrange("p (j t) -> p j t", t=4), bank[:].rearrange("p t j -> p j t"), ACT.Sin, bias=zero[:]
                     )
+                reps = 1024 // (4 * REP)
+                gain = grep[:, g, :, :].rearrange("p r t -> p (r t)").unsqueeze(1).to_broadcast([P, reps, 4 * REP])
+                nc.gpsimd.tensor_tensor(
+                    h2bf[g][:, 1024 * pair : 1024 * (pair + 1)].rearrange("p (k e) -> p k e", k=reps),
+                    sines[:].rearrange("p h (k e) -> p (h k) e", e=4 * REP),
+                    gain,
+                    MULT,
+                )
+                if (g, pair) == (0, 1):
+                    order_w4(nc.scalar.copy, 1)
 
-        pairs01 = [sb([P, 2, 512, 2], BF16, f"pairs{c}", tag) for c, tag in enumerate(("w4sp0", "w4p0"))]
-        pairs23 = sb([P, 2, 1024, 2], BF16, "pairs23", "vw0")
-        pairs = [pairs01[0][:], pairs01[1][:], pairs23[:, :, 0:512, :], pairs23[:, :, 512:1024, :]]
-        wm_bf = [sb([P, 2048], BF16, f"wm_bf{g}", f"vs{g}") for g in range(2)]
+        pairs = [sb([P, 2, CH, 2], BF16, f"pairs{c}", PAIRS + 4 * KB * ((c + 2) % 4))[:] for c in range(4)]
+        wm_bf = [sb([P, 2048], BF16, f"wm_bf{g}", at) for g, at in enumerate((SMALL + 3 * KB, VS))]
 
-        def round_plane(copy, i, c):
-            copy(pairs[c][:, i // 2, :, i % 2], planes[i][:, 512 * c : 512 * (c + 1)])
+        def round_chunk(copy, i, c):
+            copy(pairs[c][:, i // 2, :, i % 2], planes[i][:, CH * c : CH * (c + 1)])
 
-        def round_upper(copy, i):
-            copy(pairs23[:, i // 2, :, i % 2], planes[i][:, 1024:2048])
+        def weave(copy, dtype, dst, src):
+            copy(dst.bitcast(dtype).rearrange("p (c u) -> p c u", u=2), src.rearrange("p u c e -> p u (c e)").bitcast(dtype).rearrange("p u c -> p c u"))
 
-        def round_early(i):
-            for c in range(2):
-                round_plane(nc.scalar.copy, i, c)
-            round_upper(nc.scalar.copy, i)
-
-        def cast_wm(g):
+        def cast_wm(g, t0, t1):
             nc.scalar.copy(
-                wm_bf[g][:].rearrange("p (t m j) -> p m j t", t=4, j=4),
-                wm_raw[g][:].rearrange("p j (m t) -> p m j t", t=4),
+                wm_bf[g][:].rearrange("p (t m j) -> p m j t", t=4, j=4)[:, :, :, t0:t1],
+                wm_raw[g][:].rearrange("p j (m t) -> p m j t", t=4)[:, :, :, t0:t1],
             )
 
-        round_early(2)
-        cast_wm(0)
-        round_early(0)
-        round_early(1)
-        wm_src = wm_raw[1][:].rearrange("p j (m t) -> p t m j", t=4)
-        nc.gpsimd.tensor_scalar(wm_bf[1][:, 0:1024].rearrange("p (t m j) -> p t m j", t=2, j=4), wm_src[:, 0:2], 1.0, 0.0, MULT, ADD)
-        nc.scalar.copy(
-            wm_bf[1][:, 1024:2048].rearrange("p (t m j) -> p m j t", t=2, j=4),
-            wm_raw[1][:].rearrange("p j (m t) -> p m j t", t=4)[:, :, :, 2:4],
+        for i in (2, 0, 1):
+            for c in (2, 3, 0, 1):
+                round_chunk(nc.scalar.copy, i, c)
+            if i == 2:
+                cast_wm(0, 0, 4)
+        nc.gpsimd.tensor_scalar(
+            wm_bf[1][:, 0:1024].rearrange("p (t m j) -> p t m j", t=2, j=4),
+            wm_raw[1][:].rearrange("p j (m t) -> p t m j", t=4)[:, 0:2],
+            1.0,
+            0.0,
+            MULT,
+            ADD,
         )
+        cast_wm(1, 2, 4)
+        for c in range(2):
+            round_chunk(nc.scalar.copy, 3, c)
+        woven = [sb([P, 4 * CH], BF16, f"woven{c}", WOVEN + 4 * KB * ((c + 2) % 4)) for c in range(4)]
+        for c in range(2):
+            weave(nc.scalar.copy, U32, woven[c][:], pairs[c])
 
-        pw = {}
-        pc = sb([P, T2], U32, "pc")
-        ps = sb([P, T2], U8, "ps")
-        first = sb([P, 3840], U8, "first", "xs3")
-
-        def weave(copy, dtype, c):
-            pw[c] = sb([P, 2048], BF16, f"pw{c}", f"pw{min(c, 2)}")
-            copy(
-                pw[c][:].bitcast(dtype).rearrange("p (c u) -> p c u", u=2),
-                pairs[c].rearrange("p u c e -> p u (c e)").bitcast(dtype).rearrange("p u c -> p c u"),
-            )
+        pc = [sb([P, CH], U32, f"page_c{c}", PAGE_C + 2 * KB * c) for c in range(4)]
+        ps = [sb([P, CH], U8, f"page_s{c}", PAGE_S + 512 * c) for c in range(4)]
+        wmq = [sb([P, 1280], U8, "wmq0", XS + 12 * KB), sb([P, 1280], U8, "wmq1", XS + 14 * KB), sb([P, 640], U8, "wmq2", WOVEN + 2 * KB - 320), sb([P, 1920], U8, "wmq3", PAIRS + 12 * KB)]
 
         def quant_page(c):
-            quant(pc[:, 512 * c : 512 * (c + 1)], ps[:, 512 * c : 512 * (c + 1)], pw[c][:])
+            quant(pc[c][:], ps[c][:], woven[c][:])
 
-        for c in range(2):
-            round_plane(nc.scalar.copy, 3, c)
-        quant(first[:, 0:2048], first[:, 3072:3584], wm_bf[0][:])
-        round_upper(nc.vector.tensor_copy, 3)
-        for c in range(2):
-            weave(nc.scalar.copy, U32, c)
-        quant(first[:, 2048:3072], first[:, 3584:3840], wm_bf[1][:, 0:1024])
-        weave(nc.vector.tensor_copy, I32, 2)
-        second = sb([P, 1280], U8, "second", "plane3")
-        quant(second[:, 0:1024], second[:, 1024:1280], wm_bf[1][:, 1024:2048])
+        quant(wmq[0][:, 0:1024], wmq[0][:, 1024:1280], wm_bf[0][:, 0:1024])
+        for c in (2, 3):
+            round_chunk(nc.vector.tensor_copy, 3, c)
+        weave(nc.vector.tensor_copy, I32, woven[2][:], pairs[2])
+        quant(wmq[1][:, 0:1024], wmq[1][:, 1024:1280], wm_bf[0][:, 1024:2048])
         quant_page(2)
-        quant_page(0)
-        weave(nc.vector.tensor_copy, I32, 3)
-        quant_page(1)
-        quant_page(3)
-        late = sb([P, 8192 + 2048], U8, "late", "pw1")
-        h2c, h2s = late[:, 0:8192], late[:, 8192:]
-        wm_codes = [first[:, 512 * u : 512 * (u + 1)] for u in range(6)] + [second[:, 512 * u : 512 * (u + 1)] for u in range(2)]
-        wm_scales = [first[:, 3072 + P * u : 3072 + P * (u + 1)] for u in range(6)] + [second[:, 1024 + P * u : 1024 + P * (u + 1)] for u in range(2)]
+        weave(nc.vector.tensor_copy, I32, woven[3][:], pairs[3])
+        quant(wmq[2][:, 0:512], wmq[2][:, 512:640], wm_bf[1][:, 0:512])
+        for c in (3, 0, 1):
+            quant_page(c)
+        quant(wmq[3][:, 0:1536], wmq[3][:, 1536:1920], wm_bf[1][:, 512:2048])
+        h2c = [sb([P, NP], U32, f"h2c{a}", WOVEN + (10 + 4 * a) * KB) for a in range(2)]
+        h2s = [sb([P, NP], U8, f"h2s{a}", LATE + KB * a) for a in range(2)]
         for a in range(2):
-            quant(h2c[:, 4096 * a : 4096 * (a + 1)], h2s[:, NP * a : NP * (a + 1)], h2bf[:, 4096 * a : 4096 * (a + 1)])
-        w1_bf = sb([P, 2048], BF16, "w1_bf", "h2bf")
+            quant(h2c[a][:], h2s[a][:], h2bf[a][:])
+        w1_bf = sb([P, 2048], BF16, "w1_bf", H2BF + 8 * KB)
         for a in range(2):
             nc.gpsimd.tensor_scalar(
                 w1_bf[:, 1024 * a : 1024 * (a + 1)].rearrange("p (c j) -> p c j", j=4),
@@ -270,151 +274,112 @@ def tile_list_exoskeleton_gait_features_kernel(
                 ADD,
             )
 
-        rows = [sb([P, T2], F32, "arow7") if u == 7 else row_tile(F32, f"arow{u}") for u in range(8)]
-        picked0 = [sb([P, 4, 512], F32, "picked0_0", "act", 2)]
-        picked1 = sb([P, 4, NP], F32, "picked1", "act", 2)
+        def wm_operand(u):
+            tile, first, count = (wmq[u // 2], u % 2, 2) if u < 4 else (wmq[2], 0, 1) if u == 4 else (wmq[3], u - 5, 3)
+            return tile[:, 512 * first : 512 * (first + 1)], tile[:, 512 * count + P * first : 512 * count + P * (first + 1)]
 
-        def picked(a, j0, n):
-            return picked1[:, :, j0 : j0 + n] if a == 1 else picked0[j0 // 512][:, :, j0 % 512 : j0 % 512 + n]
+        row_at = (PLANE, PLANE + 8 * KB, PLANE + 16 * KB, WM_RAW, WM_RAW + 8 * KB, TAB, TAB + 8 * KB, SIN_EXTRA)
+        pick_at = (XS, XS + 4 * KB, XS + 8 * KB, PLANE + 24 * KB, PLANE + 28 * KB, WM_BF + 4 * KB, VS, PAIRS)
+        rows = [sb([P, T2], F32, f"row{u}", row_at[u]) for u in range(8)]
+        picked = [sb([P, NP], F32, f"picked{u}", pick_at[u]) for u in range(8)]
+        hp0 = sb([P, 2, NP, 2], BF16, "hp0", H2BF)
+        hp1 = [sb([P, 2, CH, 2], BF16, f"hp1{h}", W1_RAW + 4 * KB * h) for h in range(2)]
 
-
-        def project(u, c, copy=nc.scalar.copy):
-            bank = psum.tile([P, 512], F32, name="bank", tag="bank")
+        def project(u, c, by_vector=False):
+            bank = next_bank([P, CH], f"muscle{u}{c}", not by_vector)
+            codes, scales = wm_operand(u)
             nc.tensor.matmul_mx(
-                out=bank[:],
-                lhsT=wm_codes[u].bitcast(FP8X4),
-                lhsT_scale=wm_scales[u],
-                rhs=pc[:, 512 * c : 512 * (c + 1)].bitcast(FP8X4),
-                rhs_scale=ps[:, 512 * c : 512 * (c + 1)],
-                start=True,
-                stop=True,
+                out=bank[:], lhsT=codes.bitcast(FP8X4), lhsT_scale=scales, rhs=pc[c][:].bitcast(FP8X4), rhs_scale=ps[c][:], start=True, stop=True
             )
-            copy(rows[u][:, 512 * c : 512 * (c + 1)], bank[:])
-
-        def project_row(u):
-            for c in range(4):
-                project(u, c)
+            copy = nc.vector.tensor_copy if by_vector else nc.scalar.copy
+            copy(rows[u][:, CH * c : CH * (c + 1)], bank[:])
 
         def gather(u, j0, n):
-            nc.vector.tensor_copy(picked(u // 4, j0, n)[:, u % 4, :], rows[u][:].indirect(l3[:, j0 // 16 : (j0 + n) // 16]))
+            nc.vector.tensor_copy(picked[u][:, j0 : j0 + n], rows[u][:].indirect(l3[:, j0 // 16 : (j0 + n) // 16]))
 
-        def squash(u, j0, n, count=1):
-            part = picked(u // 4, j0, n)[:, u % 4 : u % 4 + count, :]
-            nc.scalar.activation(part, part, ACT.Tanh, bias=zero[:])
+        def squash(u, j0, n):
+            nc.scalar.activation(picked[u][:, j0 : j0 + n], picked[u][:, j0 : j0 + n], ACT.Tanh, bias=zero[:])
 
-        h1bf = [sb([P, 4 * NP], BF16, f"h1bf{a}", "wm", 2) for a in range(2)]
-        h1s = sb([P, 2 * NP], U8, "h1s")
+        def pair_slot(u, j0, n):
+            t = u % 4
+            return hp0[:, t // 2, j0 : j0 + n, t % 2] if u < 4 else hp1[j0 // CH][:, t // 2, j0 % CH : j0 % CH + n, t % 2]
 
-        def gain_h1(a, j0, n):
-            nc.vector.tensor_tensor(
-                h1bf[a][:, 4 * j0 : 4 * (j0 + n)].rearrange("p (c i t) -> p c t i", i=2, t=4),
-                picked(a, j0, n).rearrange("p t (c i) -> p c t i", i=2),
-                gmc[:, a, :].unsqueeze(1).unsqueeze(3).to_broadcast([P, n // 2, 4, 2]),
-                MULT,
-            )
+        def squash_and_gain(u):
+            for h in range(2):
+                half = sb([P, CH], F32, f"half{u}{h}", WOVEN + 2 * KB * h)
+                nc.scalar.activation(half[:], picked[u][:, CH * h : CH * (h + 1)], ACT.Tanh, bias=zero[:])
+                nc.gpsimd.tensor_scalar(pair_slot(u, CH * h, CH), half[:], gmc[:, u // 4, u % 4 : u % 4 + 1], 0.0, MULT, ADD)
 
-        def quant_h1(a, j0, n):
-            quant(h1c[a][:, j0 : j0 + n], h1s[:, NP * a + j0 : NP * a + j0 + n], h1bf[a][:, 4 * j0 : 4 * (j0 + n)])
+        def gain_scalar(u, j0, n):
+            nc.scalar.activation(pair_slot(u, j0, n), picked[u][:, j0 : j0 + n], ACT.Copy, scale=gmc[:, u // 4, u % 4 : u % 4 + 1])
 
-        def gain_h1_pool(j0, n):
-            nc.gpsimd.tensor_tensor(
-                h1bf[0][:, 4 * j0 : 4 * (j0 + n)].rearrange("p (j t) -> p j t", t=4),
-                picked(0, j0, n).rearrange("p t j -> p j t"),
-                gmc[:, 0, :].unsqueeze(1).to_broadcast([P, n, 4]),
-                MULT,
-            )
+        todo = [(u, c) for c in (2, 3) for u in range(2)] + [(u, c) for u in range(2) for c in (0, 1)]
+        todo += [(u, c) for u in range(2, 8) for c in range(4 if u < 5 else 3)]
 
-        for c in CHUNK_ORDER[:2]:
-            for u in range(LEAD_ROWS):
-                project(u, c)
-        for u in range(LEAD_ROWS):
-            for c in CHUNK_ORDER[2:]:
-                project(u, c)
-        for u in range(LEAD_ROWS, 4):
-            for c in range(4):
-                project(u, c, nc.vector.tensor_copy if (u, c) in ((3, 2), (3, 3)) else nc.scalar.copy)
-        for u in range(4):
-            gather(u, 0, 512)
-        project_row(4)
-        for j0 in (0, 256):
-            squash(0, j0, 256, 4)
-        project_row(5)
-        project(6, 0)
-        picked0.append(sb([P, 4, 512], F32, "picked0_1", "xs3"))
-        for u in range(4):
-            gather(u, 512, 512)
-        for j0 in (512, 768):
-            squash(0, j0, 256, 4)
-        for j0 in range(0, NP, 256):
-            gain_h1_pool(j0, 256)
-        for c in range(1, 4):
-            project(6, c)
-        project_row(7)
-        for u in (4, 5, 6):
+        def project_next(count):
+            for k in range(count):
+                project(*todo.pop(0))
+
+        project_next(14)
+        for u in range(5):
             gather(u, 0, NP)
-        for j0, n in RANGES:
-            gather(7, j0, n)
-        squash(4, 0, NP, 2)
+            if u >= 2:
+                project(u + 3, 3, True)
+            squash_and_gain(u)
+            project_next(3)
+        gather(5, 0, NP)
+        squash_and_gain(5)
+        gather(6, 0, NP)
+        for j0 in (0, CH):
+            gather(7, j0, CH)
         squash(6, 0, NP)
-        held = sb([P, 4096 + 2560], U8, "held", "arow7")
-        w1c, w1s = held[:, 4096:6144], held[:, 6144:6656]
-        h1c = [held[:, 0:4096].bitcast(U32), sb([P, NP], U32, "h1c1", "vw1")[:]]
-        quant(w1c, w1s, w1_bf[:])
-        for k in range(2):
-            quant_h1(0, 512 * k, 512)
+        squash(7, 0, CH)
+        for u in (6, 7):
+            gain_scalar(u, 0, CH)
+        squash(7, CH, CH)
+        for u in (6, 7):
+            gain_scalar(u, CH, CH)
 
-        ost = [sb([P, NP], F32, f"ost{h}", tag) for h, tag in enumerate(("w4_raw0", "w4p0"))]
+        ost = [sb([P, NP], F32, f"ost{h}", LATE + 2 * KB + 4 * KB * h) for h in range(2)]
         w8b = w8c[:].rearrange("p a n -> p (a n)").bitcast(U8)
+        ybank = {}
 
-        def finish(j0, n):
-            banks = [psum.tile([P, n], F32, name="bank", tag="bank") for h in range(2)]
-
-            def y_pass(h, wc, ws, a, hc, hs, start, stop):
-                nc.tensor.matmul_mx(
-                    out=banks[h][:],
-                    lhsT=wc[:, 4 * (N * a + P * h) : 4 * (N * a + P * (h + 1))].bitcast(FP8X4),
-                    lhsT_scale=ws[:, N * a + P * h : N * a + P * (h + 1)],
-                    rhs=hc,
-                    rhs_scale=hs[:, NP * a + j0 : NP * a + j0 + n],
-                    start=start,
-                    stop=stop,
-                )
-
-            for h in range(2):
-                for a in range(2):
-                    y_pass(h, w8b, w8s, a, h2c[:, 4 * (NP * a + j0) : 4 * (NP * a + j0 + n)].bitcast(FP8X4), h2s, a == 0, False)
-                y_pass(h, w1c, w1s, 0, h1c[0][:, j0 : j0 + n].bitcast(FP8X4), h1s, False, False)
-            for h in range(2):
-                y_pass(h, w1c, w1s, 1, h1c[1][:, j0 : j0 + n].bitcast(FP8X4), h1s, False, True)
-                nc.scalar.activation(ost[h][:, j0 : j0 + n], banks[h][:], ACT.Tanh, bias=boc[:, h : h + 1])
-                nc.sync.dma_start(out[P * h : P * (h + 1), j0 : j0 + n], ost[h][:, j0 : j0 + n])
-
-        for j0, n in RANGES:
-            squash(7, j0, n)
-
-        def scale_h1(j0, n):
-            hp = sb([P, 2, n, 2], BF16, f"h1_pairs{j0}")
-            for t in range(4):
-                nc.scalar.activation(hp[:, t // 2, :, t % 2], picked1[:, t, j0 : j0 + n], ACT.Copy, scale=gmc[:, 1, t : t + 1])
-            return hp
-
-        def weave_h1(hp, j0, n):
-            nc.vector.tensor_copy(
-                h1bf[1][:, 4 * j0 : 4 * (j0 + n)].bitcast(I32).rearrange("p (c u) -> p c u", u=2),
-                hp.rearrange("p u c e -> p u (c e)").bitcast(I32).rearrange("p u c -> p c u"),
+        def y_pass(k, h, wc, ws, a, hc, hs, start, stop):
+            nc.tensor.matmul_mx(
+                out=ybank[k, h],
+                lhsT=wc[:, 4 * (N * a + P * h) : 4 * (N * a + P * (h + 1))].bitcast(FP8X4),
+                lhsT_scale=ws[:, N * a + P * h : N * a + P * (h + 1)],
+                rhs=hc.bitcast(FP8X4),
+                rhs_scale=hs,
+                start=start,
+                stop=stop,
             )
 
-        Q = NP // 4
-        hp = [scale_h1(j0, Q) for j0 in (2 * Q, 3 * Q)]
-        gain_h1(1, 0, Q)
-        gain_h1(1, Q, Q)
-        quant_h1(1, 0, Q)
-        finish(0, Q)
-        weave_h1(hp[0][:], 2 * Q, Q)
-        quant_h1(1, Q, Q)
-        finish(Q, Q)
-        quant_h1(1, 2 * Q, Q)
-        finish(2 * Q, Q)
-        weave_h1(hp[1][:], 3 * Q, Q)
-        quant_h1(1, 3 * Q, Q)
-        finish(3 * Q, Q)
+        for k in range(4):
+            shared = next_bank([P, 2, Q], f"y{k}") if k < 3 else None
+            for h in range(2):
+                ybank[k, h] = shared[:, h, :] if k < 3 else next_bank([P, Q], f"y{k}{h}")[:]
+                for a in range(2):
+                    y_pass(k, h, w8b, w8s, a, h2c[a][:, Q * k : Q * (k + 1)], h2s[a][:, Q * k : Q * (k + 1)], a == 0 and (h == 0 or k == 3), False)
+
+        w1c = sb([P, 2048], U8, "w1c", SIN_EXTRA)
+        w1s = sb([P, 512], U8, "w1s", SIN_EXTRA + 2 * KB)
+        h1w0 = [sb([P, 4 * CH], BF16, f"h1w0{h}", SIN_EXTRA + (3 + 4 * h) * KB) for h in range(2)]
+        h1w1 = [sb([P, 4 * Q], BF16, f"h1w1{k}", LATE + 10 * KB + 2 * KB * k) for k in range(4)]
+        code_at = [[LATE + 18 * KB] + [LATE + 10 * KB + 2 * KB * k for k in range(3)], [LATE + (19 + k) * KB for k in range(4)]]
+        h1c = [[sb([P, Q], U32, f"h1c{a}{k}", code_at[a][k]) for k in range(4)] for a in range(2)]
+        h1s = [[sb([P, Q], U8, f"h1s{a}{k}", LATE + 26 * KB + Q * (4 * a + k)) for k in range(4)] for a in range(2)]
+        quant(w1c[:], w1s[:], w1_bf[:])
+        for h in range(2):
+            weave(nc.vector.tensor_copy, I32, h1w0[h][:], hp0[:, :, CH * h : CH * (h + 1), :])
+        for k in range(4):
+            lo = Q * (k % 2)
+            weave(nc.vector.tensor_copy, I32, h1w1[k][:], hp1[k // 2][:, :, lo : lo + Q, :])
+            quant(h1c[0][k][:], h1s[0][k][:], h1w0[k // 2][:, 4 * lo : 4 * (lo + Q)])
+            quant(h1c[1][k][:], h1s[1][k][:], h1w1[k][:])
+            for a in (0, 1) if k == 0 else (1, 0):
+                for h in range(2):
+                    y_pass(k, h, w1c, w1s, a, h1c[a][k][:], h1s[a][k][:], False, (a == 1) == (k == 0) and (h == 1 or k == 3))
+            for h in range(2):
+                nc.scalar.activation(ost[h][:, Q * k : Q * (k + 1)], ybank[k, h], ACT.Tanh, bias=boc[:, h : h + 1])
+                nc.sync.dma_start(out[P * h : P * (h + 1), Q * k : Q * (k + 1)], ost[h][:, Q * k : Q * (k + 1)])

@@ -22,7 +22,8 @@ KB = 1024
 REP = 32
 FIRST = 256
 CH = 512
-Q = 256
+PIECES = ((0, 512), (512, 256), (768, 256))
+RANGES = ((0, 256), (256, 256), (512, 256), (768, 128), (896, 128))
 
 TAB = 0
 SIN_EXTRA = 16 * KB
@@ -41,6 +42,7 @@ W4_RAW = 170 * KB
 VS = 174 * KB
 SMALL = 178 * KB
 LATE = 192 * KB
+LAST = 222 * KB
 
 
 def tile_list_exoskeleton_gait_features_kernel(
@@ -283,7 +285,7 @@ def tile_list_exoskeleton_gait_features_kernel(
         rows = [sb([P, T2], F32, f"row{u}", row_at[u]) for u in range(8)]
         picked = [sb([P, NP], F32, f"picked{u}", pick_at[u]) for u in range(8)]
         hp0 = sb([P, 2, NP, 2], BF16, "hp0", H2BF)
-        hp1 = [sb([P, 2, CH, 2], BF16, f"hp1{h}", W1_RAW + 4 * KB * h) for h in range(2)]
+        hp1 = [sb([P, 2, n, 2], BF16, f"hp1{j0}", W1_RAW + 8 * j0) for j0, n in PIECES]
 
         def project(u, c, by_vector=False):
             bank = next_bank([P, CH], f"muscle{u}{c}", not by_vector)
@@ -300,18 +302,30 @@ def tile_list_exoskeleton_gait_features_kernel(
         def squash(u, j0, n):
             nc.scalar.activation(picked[u][:, j0 : j0 + n], picked[u][:, j0 : j0 + n], ACT.Tanh, bias=zero[:])
 
+        def piece_of(j0):
+            return max(k for k, (first, n) in enumerate(PIECES) if first <= j0)
+
         def pair_slot(u, j0, n):
             t = u % 4
-            return hp0[:, t // 2, j0 : j0 + n, t % 2] if u < 4 else hp1[j0 // CH][:, t // 2, j0 % CH : j0 % CH + n, t % 2]
+            if u < 4:
+                return hp0[:, t // 2, j0 : j0 + n, t % 2]
+            lo = j0 - PIECES[piece_of(j0)][0]
+            return hp1[piece_of(j0)][:, t // 2, lo : lo + n, t % 2]
+
+        halves = {}
 
         def squash_and_gain(u):
             for h in range(2):
                 half = sb([P, CH], F32, f"half{u}{h}", WOVEN + 2 * KB * h)
                 nc.scalar.activation(half[:], picked[u][:, CH * h : CH * (h + 1)], ACT.Tanh, bias=zero[:])
-                nc.gpsimd.tensor_scalar(pair_slot(u, CH * h, CH), half[:], gmc[:, u // 4, u % 4 : u % 4 + 1], 0.0, MULT, ADD)
+                halves[u, h] = half
+                for j0, n in ((CH * h, CH),) if u < 4 else PIECES[h : 1 + 2 * h if u == 4 else 1 + h]:
+                    nc.gpsimd.tensor_scalar(
+                        pair_slot(u, j0, n), half[:, j0 - CH * h : j0 - CH * h + n], gmc[:, u // 4, u % 4 : u % 4 + 1], 0.0, MULT, ADD
+                    )
 
-        def gain_scalar(u, j0, n):
-            nc.scalar.activation(pair_slot(u, j0, n), picked[u][:, j0 : j0 + n], ACT.Copy, scale=gmc[:, u // 4, u % 4 : u % 4 + 1])
+        def gain_scalar(u, j0, n, src):
+            nc.scalar.activation(pair_slot(u, j0, n), src, ACT.Copy, scale=gmc[:, u // 4, u % 4 : u % 4 + 1])
 
         todo = [(u, c) for c in (2, 3) for u in range(2)] + [(u, c) for u in range(2) for c in (0, 1)]
         todo += [(u, c) for u in range(2, 8) for c in range(4 if u < 5 else 3)]
@@ -333,14 +347,15 @@ def tile_list_exoskeleton_gait_features_kernel(
         for j0 in (0, CH):
             gather(7, j0, CH)
         squash(6, 0, NP)
-        squash(7, 0, CH)
-        for u in (6, 7):
-            gain_scalar(u, 0, CH)
-        squash(7, CH, CH)
-        for u in (6, 7):
-            gain_scalar(u, CH, CH)
+        for j0, n in PIECES:
+            last = sb([P, n], F32, f"last{j0}", LAST + 4 * j0)
+            nc.scalar.activation(last[:], picked[7][:, j0 : j0 + n], ACT.Tanh, bias=zero[:])
+            if j0 == PIECES[-1][0]:
+                gain_scalar(5, j0, n, halves[5, 1][:, j0 - CH : j0 - CH + n])
+            gain_scalar(6, j0, n, picked[6][:, j0 : j0 + n])
+            gain_scalar(7, j0, n, last[:])
 
-        ost = [sb([P, NP], F32, f"ost{h}", LATE + 2 * KB + 4 * KB * h) for h in range(2)]
+        ost = [sb([P, NP], F32, f"ost{h}", PLANE + 8 * KB + 4 * KB * h) for h in range(2)]
         w8b = w8c[:].rearrange("p a n -> p (a n)").bitcast(U8)
         ybank = {}
 
@@ -355,31 +370,38 @@ def tile_list_exoskeleton_gait_features_kernel(
                 stop=stop,
             )
 
-        for k in range(4):
-            shared = next_bank([P, 2, Q], f"y{k}") if k < 3 else None
+        for k, (j0, n) in enumerate(RANGES):
+            shared = next_bank([P, 2, n], f"y{k}")
             for h in range(2):
-                ybank[k, h] = shared[:, h, :] if k < 3 else next_bank([P, Q], f"y{k}{h}")[:]
+                ybank[k, h] = shared[:, h, :]
                 for a in range(2):
-                    y_pass(k, h, w8b, w8s, a, h2c[a][:, Q * k : Q * (k + 1)], h2s[a][:, Q * k : Q * (k + 1)], a == 0 and (h == 0 or k == 3), False)
+                    y_pass(k, h, w8b, w8s, a, h2c[a][:, j0 : j0 + n], h2s[a][:, j0 : j0 + n], a == 0 and h == 0, False)
 
+        h1w1 = [sb([P, 4 * n], BF16, f"h1w1{k}", LATE + 10 * KB + 8 * j0) for k, (j0, n) in enumerate(RANGES)]
+        h1w0 = [sb([P, 4 * CH], BF16, f"h1w0{h}", at) for h, at in enumerate((SIN_EXTRA + 3 * KB, LATE + 7 * KB))]
         w1c = sb([P, 2048], U8, "w1c", SIN_EXTRA)
         w1s = sb([P, 512], U8, "w1s", SIN_EXTRA + 2 * KB)
-        h1w0 = [sb([P, 4 * CH], BF16, f"h1w0{h}", SIN_EXTRA + (3 + 4 * h) * KB) for h in range(2)]
-        h1w1 = [sb([P, 4 * Q], BF16, f"h1w1{k}", LATE + 10 * KB + 2 * KB * k) for k in range(4)]
-        code_at = [[LATE + 18 * KB] + [LATE + 10 * KB + 2 * KB * k for k in range(3)], [LATE + (19 + k) * KB for k in range(4)]]
-        h1c = [[sb([P, Q], U32, f"h1c{a}{k}", code_at[a][k]) for k in range(4)] for a in range(2)]
-        h1s = [[sb([P, Q], U8, f"h1s{a}{k}", LATE + 26 * KB + Q * (4 * a + k)) for k in range(4)] for a in range(2)]
-        quant(w1c[:], w1s[:], w1_bf[:])
-        for h in range(2):
+        code_at = [[LATE + 18 * KB, LATE + 19 * KB] + [LAST + 4 * j0 for j0, n in RANGES[2:]], [LATE + 20 * KB + 4 * j0 for j0, n in RANGES]]
+        h1c = [[sb([P, n], U32, f"h1c{a}{k}", code_at[a][k]) for k, (j0, n) in enumerate(RANGES)] for a in range(2)]
+        h1s = [[sb([P, n], U8, f"h1s{a}{k}", LATE + 24 * KB + NP * a + j0) for k, (j0, n) in enumerate(RANGES)] for a in range(2)]
+
+        def weave_first(h):
             weave(nc.vector.tensor_copy, I32, h1w0[h][:], hp0[:, :, CH * h : CH * (h + 1), :])
-        for k in range(4):
-            lo = Q * (k % 2)
-            weave(nc.vector.tensor_copy, I32, h1w1[k][:], hp1[k // 2][:, :, lo : lo + Q, :])
-            quant(h1c[0][k][:], h1s[0][k][:], h1w0[k // 2][:, 4 * lo : 4 * (lo + Q)])
+
+        weave_first(0)
+        quant(w1c[:], w1s[:], w1_bf[:])
+        for k, (j0, n) in enumerate(RANGES):
+            if k == 2:
+                weave_first(1)
+            lo = j0 % CH
+            first = j0 - PIECES[piece_of(j0)][0]
+            weave(nc.vector.tensor_copy, I32, h1w1[k][:], hp1[piece_of(j0)][:, :, first : first + n, :])
+            quant(h1c[0][k][:], h1s[0][k][:], h1w0[j0 // CH][:, 4 * lo : 4 * (lo + n)])
             quant(h1c[1][k][:], h1s[1][k][:], h1w1[k][:])
-            for a in (0, 1) if k == 0 else (1, 0):
+            for a in range(2):
                 for h in range(2):
-                    y_pass(k, h, w1c, w1s, a, h1c[a][k][:], h1s[a][k][:], False, (a == 1) == (k == 0) and (h == 1 or k == 3))
+                    y_pass(k, h, w1c, w1s, a, h1c[a][k][:], h1s[a][k][:], False, a == 1 and h == 1)
             for h in range(2):
-                nc.scalar.activation(ost[h][:, Q * k : Q * (k + 1)], ybank[k, h], ACT.Tanh, bias=boc[:, h : h + 1])
-                nc.sync.dma_start(out[P * h : P * (h + 1), Q * k : Q * (k + 1)], ost[h][:, Q * k : Q * (k + 1)])
+                nc.scalar.activation(ost[h][:, j0 : j0 + n], ybank[k, h], ACT.Tanh, bias=boc[:, h : h + 1])
+                queue = nc.scalar if (k, h) == (len(RANGES) - 1, 1) else nc.sync
+                queue.dma_start(out[P * h : P * (h + 1), j0 : j0 + n], ost[h][:, j0 : j0 + n])

@@ -22,6 +22,7 @@ KB = 1024
 REP = 32
 FIRST = 256
 CH = 512
+GAIN_GROUPS = (((0, 2), (2, 2), (4, 4)), ((0, 4), (4, 4)))
 PIECES = ((0, 512), (512, 256), (768, 256))
 RANGES = ((0, 256), (256, 256), (512, 256), (768, 128), (896, 128))
 
@@ -81,10 +82,10 @@ def tile_list_exoskeleton_gait_features_kernel(
         zin = sb([P, 1], F32, "zin", SMALL + 11 * KB + 192)
         zero = sb([P, 1], F32, "zero", SMALL + 11 * KB + 256)
         nc.vector.memset(ts[:].bitcast(I32), 0)
-        nc.gpsimd.memset(zin[:], 0.0)
+        nc.vector.memset(zin[:], 0.0)
         nc.vector.memset(w4s_raw[:].bitcast(I32), 0)
-        nc.gpsimd.memset(vs[1][:].bitcast(I32), 0)
-        nc.gpsimd.memset(w8s[:].bitcast(I32), 0)
+        nc.vector.memset(vs[1][:].bitcast(I32), 0)
+        nc.vector.memset(w8s[:].bitcast(I32), 0)
         nc.scalar.activation(zero[:], zin[:], ACT.Silu)
 
         l1 = lists.tile([P, NP // 16], U16, name="l1")
@@ -178,11 +179,12 @@ def tile_list_exoskeleton_gait_features_kernel(
 
         h2bf = [sb([P, 4 * NP], BF16, f"h2bf{g}", H2BF + 8 * KB * g) for g in range(2)]
         for g in range(2):
-            for pair in range(4):
-                sines = sb([P, 2, 512], F32, f"sines{g}{pair}", TAB + 4 * KB * ((4 * g + pair) % 6))
-                for half in range(2):
-                    j0 = P * (2 * pair + half)
-                    bank = next_bank([P, 4, P], f"phase{g}{pair}{half}")
+            for first, count in GAIN_GROUPS[g]:
+                at = TAB + 2 * KB * (8 * g + first) if 8 * g + first < 12 else WM_BF
+                sines = sb([P, count, 512], F32, f"sines{g}{first}", at)
+                for half in range(count):
+                    j0 = P * (first + half)
+                    bank = next_bank([P, 4, P], f"phase{g}{first}{half}")
                     for t in range(4):
                         for ka in range(2):
                             nc.tensor.matmul_mx(
@@ -197,15 +199,15 @@ def tile_list_exoskeleton_gait_features_kernel(
                     nc.scalar.activation(
                         sines[:, half, :].rearrange("p (j t) -> p j t", t=4), bank[:].rearrange("p t j -> p j t"), ACT.Sin, bias=zero[:]
                     )
-                reps = 1024 // (4 * REP)
+                reps = 512 * count // (4 * REP)
                 gain = grep[:, g, :, :].rearrange("p r t -> p (r t)").unsqueeze(1).to_broadcast([P, reps, 4 * REP])
                 nc.gpsimd.tensor_tensor(
-                    h2bf[g][:, 1024 * pair : 1024 * (pair + 1)].rearrange("p (k e) -> p k e", k=reps),
+                    h2bf[g][:, 512 * first : 512 * (first + count)].rearrange("p (k e) -> p k e", k=reps),
                     sines[:].rearrange("p h (k e) -> p (h k) e", e=4 * REP),
                     gain,
                     MULT,
                 )
-                if (g, pair) == (0, 1):
+                if (g, first) == (0, 2):
                     order_w4(nc.scalar.copy, 1)
 
         pairs = [sb([P, 2, CH, 2], BF16, f"pairs{c}", PAIRS + 4 * KB * ((c + 2) % 4))[:] for c in range(4)]

@@ -21,6 +21,7 @@ P = 128
 KB = 1024
 REP = 32
 FIRST = 256
+EARLY_BANKS = 4
 CH = 512
 GAIN_GROUPS = (((0, 2), (2, 2), (4, 4)), ((0, 4), (4, 4)))
 PIECES = ((0, 512), (512, 256), (768, 256))
@@ -178,24 +179,34 @@ def tile_list_exoskeleton_gait_features_kernel(
             nc.vector.tensor_copy(planes[i][:].indirect(l2[:]), xs_t[i][:])
 
         h2bf = [sb([P, 4 * NP], BF16, f"h2bf{g}", H2BF + 8 * KB * g) for g in range(2)]
+        phase = {}
+
+        def phase_passes(g, j0, ka):
+            if ka == 0:
+                phase[g, j0] = psum.tile([P, 4, P], F32, name=f"phase{g}{j0}", offset=2 * KB * (4 + j0 // P % EARLY_BANKS))
+            for t in range(4):
+                nc.tensor.matmul_mx(
+                    out=phase[g, j0][:, t, :],
+                    lhsT=w4p[g][:, ka, 2 * P * t : 2 * P * (t + 1)].bitcast(FP4X4),
+                    lhsT_scale=w4sp[g][:, ka, P * t : P * (t + 1)],
+                    rhs=vw[ka][:, j0 : j0 + P].bitcast(FP8X4),
+                    rhs_scale=vs[ka][:, j0 : j0 + P],
+                    start=(ka == 0 and t == 0),
+                    stop=(ka == 1 and t == 3),
+                )
+
+        for k in range(EARLY_BANKS):
+            phase_passes(0, P * k, 0)
         for g in range(2):
             for first, count in GAIN_GROUPS[g]:
                 at = TAB + 2 * KB * (8 * g + first) if 8 * g + first < 12 else WM_BF
                 sines = sb([P, count, 512], F32, f"sines{g}{first}", at)
                 for half in range(count):
                     j0 = P * (first + half)
-                    bank = next_bank([P, 4, P], f"phase{g}{first}{half}")
-                    for t in range(4):
-                        for ka in range(2):
-                            nc.tensor.matmul_mx(
-                                out=bank[:, t, :],
-                                lhsT=w4p[g][:, ka, 2 * P * t : 2 * P * (t + 1)].bitcast(FP4X4),
-                                lhsT_scale=w4sp[g][:, ka, P * t : P * (t + 1)],
-                                rhs=vw[ka][:, j0 : j0 + P].bitcast(FP8X4),
-                                rhs_scale=vs[ka][:, j0 : j0 + P],
-                                start=(ka == 0),
-                                stop=(ka == 1),
-                            )
+                    if (g, j0) not in phase:
+                        phase_passes(g, j0, 0)
+                    phase_passes(g, j0, 1)
+                    bank = phase[g, j0]
                     nc.scalar.activation(
                         sines[:, half, :].rearrange("p (j t) -> p j t", t=4), bank[:].rearrange("p t j -> p j t"), ACT.Sin, bias=zero[:]
                     )
@@ -318,7 +329,7 @@ def tile_list_exoskeleton_gait_features_kernel(
 
         def squash_and_gain(u):
             for h in range(2):
-                half = sb([P, CH], F32, f"half{u}{h}", WOVEN + 2 * KB * h)
+                half = sb([P, CH], F32, f"half{u}{h}", (WOVEN if u % 2 or u == 0 else PLANE) + 2 * KB * h)
                 nc.scalar.activation(half[:], picked[u][:, CH * h : CH * (h + 1)], ACT.Tanh, bias=zero[:])
                 halves[u, h] = half
                 for j0, n in ((CH * h, CH),) if u < 4 else PIECES[h : 1 + 2 * h if u == 4 else 1 + h]:
@@ -349,8 +360,9 @@ def tile_list_exoskeleton_gait_features_kernel(
         for j0 in (0, CH):
             gather(7, j0, CH)
         squash(6, 0, NP)
-        for j0, n in PIECES:
-            last = sb([P, n], F32, f"last{j0}", LAST + 4 * j0)
+        last_at = (LAST, LAST + 2 * KB, PLANE + 2 * KB)
+        for (j0, n), at in zip(PIECES, last_at):
+            last = sb([P, n], F32, f"last{j0}", at)
             nc.scalar.activation(last[:], picked[7][:, j0 : j0 + n], ACT.Tanh, bias=zero[:])
             if j0 == PIECES[-1][0]:
                 gain_scalar(5, j0, n, halves[5, 1][:, j0 - CH : j0 - CH + n])
@@ -380,10 +392,10 @@ def tile_list_exoskeleton_gait_features_kernel(
                     y_pass(k, h, w8b, w8s, a, h2c[a][:, j0 : j0 + n], h2s[a][:, j0 : j0 + n], a == 0 and h == 0, False)
 
         h1w1 = [sb([P, 4 * n], BF16, f"h1w1{k}", LATE + 10 * KB + 8 * j0) for k, (j0, n) in enumerate(RANGES)]
-        h1w0 = [sb([P, 4 * CH], BF16, f"h1w0{h}", at) for h, at in enumerate((SIN_EXTRA + 3 * KB, LATE + 7 * KB))]
-        w1c = sb([P, 2048], U8, "w1c", SIN_EXTRA)
-        w1s = sb([P, 512], U8, "w1s", SIN_EXTRA + 2 * KB)
-        code_at = [[LATE + 18 * KB, LATE + 19 * KB] + [LAST + 4 * j0 for j0, n in RANGES[2:]], [LATE + 20 * KB + 4 * j0 for j0, n in RANGES]]
+        h1w0 = [sb([P, 4 * CH], BF16, f"h1w0{h}", at) for h, at in enumerate((WOVEN - 3 * KB, LATE + 7 * KB))]
+        w1c = sb([P, 2048], U8, "w1c", LATE + 2 * KB)
+        w1s = sb([P, 512], U8, "w1s", WOVEN + KB)
+        code_at = [[LATE + 18 * KB, LATE + 19 * KB, last_at[1], last_at[2], last_at[2] + 512], [LATE + 20 * KB + 4 * j0 for j0, n in RANGES]]
         h1c = [[sb([P, n], U32, f"h1c{a}{k}", code_at[a][k]) for k, (j0, n) in enumerate(RANGES)] for a in range(2)]
         h1s = [[sb([P, n], U8, f"h1s{a}{k}", LATE + 24 * KB + NP * a + j0) for k, (j0, n) in enumerate(RANGES)] for a in range(2)]
 

@@ -21,6 +21,8 @@ P = 128
 KB = 1024
 REP = 32
 FIRST = 256
+V_COLUMNS = (256, 512, 512)
+PAGE_PIECES = ((1024, 256), (1280, 256), (1536, 512), (0, 512), (512, 512))
 EARLY_BANKS = 4
 CH = 512
 GAIN_GROUPS = (((0, 2), (2, 2), (4, 4)), ((0, 4), (4, 4)))
@@ -221,11 +223,12 @@ def tile_list_exoskeleton_gait_features_kernel(
                 if (g, first) == (0, 2):
                     order_w4(nc.scalar.copy, 1)
 
-        pairs = [sb([P, 2, CH, 2], BF16, f"pairs{c}", PAIRS + 4 * KB * ((c + 2) % 4))[:] for c in range(4)]
+        pairs = {t0: sb([P, 2, n, 2], BF16, f"pairs{t0}", PAIRS + 8 * ((t0 + 2 * CH) % T2))[:] for t0, n in PAGE_PIECES}
         wm_bf = [sb([P, 2048], BF16, f"wm_bf{g}", at) for g, at in enumerate((SMALL + 3 * KB, VS))]
 
-        def round_chunk(copy, i, c):
-            copy(pairs[c][:, i // 2, :, i % 2], planes[i][:, CH * c : CH * (c + 1)])
+        def round_plane(i):
+            for t0, n in PAGE_PIECES:
+                nc.scalar.copy(pairs[t0][:, i // 2, :, i % 2], planes[i][:, t0 : t0 + n])
 
         def weave(copy, dtype, dst, src):
             copy(dst.bitcast(dtype).rearrange("p (c u) -> p c u", u=2), src.rearrange("p u c e -> p u (c e)").bitcast(dtype).rearrange("p u c -> p c u"))
@@ -237,8 +240,7 @@ def tile_list_exoskeleton_gait_features_kernel(
             )
 
         for i in (2, 0, 1):
-            for c in (2, 3, 0, 1):
-                round_chunk(nc.scalar.copy, i, c)
+            round_plane(i)
             if i == 2:
                 cast_wm(0, 0, 4)
         nc.gpsimd.tensor_scalar(
@@ -250,31 +252,37 @@ def tile_list_exoskeleton_gait_features_kernel(
             ADD,
         )
         cast_wm(1, 2, 4)
-        for c in range(2):
-            round_chunk(nc.scalar.copy, 3, c)
+        round_plane(3)
         woven = [sb([P, 4 * CH], BF16, f"woven{c}", WOVEN + 4 * KB * ((c + 2) % 4)) for c in range(4)]
-        for c in range(2):
-            weave(nc.scalar.copy, U32, woven[c][:], pairs[c])
 
         pc = [sb([P, CH], U32, f"page_c{c}", PAGE_C + 2 * KB * c) for c in range(4)]
         ps = [sb([P, CH], U8, f"page_s{c}", PAGE_S + 512 * c) for c in range(4)]
-        wmq = [sb([P, 1280], U8, "wmq0", XS + 12 * KB), sb([P, 1280], U8, "wmq1", XS + 14 * KB), sb([P, 640], U8, "wmq2", WOVEN + 2 * KB - 320), sb([P, 1920], U8, "wmq3", PAIRS + 12 * KB)]
+        wmq = [sb([P, 1280], U8, "wmq0", XS + 12 * KB + 512), sb([P, 1280], U8, "wmq1", XS + 14 * KB), sb([P, 640], U8, "wmq2", WOVEN + 2 * KB - 320), sb([P, 1920], U8, "wmq3", XS + 11 * KB - 512)]
 
-        def quant_page(c):
-            quant(pc[c][:], ps[c][:], woven[c][:])
+        def weave_page(k):
+            t0, n = PAGE_PIECES[k]
+            weave(nc.vector.tensor_copy, I32, woven[t0 // CH][:, 4 * (t0 % CH) : 4 * (t0 % CH + n)], pairs[t0])
+
+        def quant_page(k):
+            t0, n = PAGE_PIECES[k]
+            c, lo = divmod(t0, CH)
+            quant(pc[c][:, lo : lo + n], ps[c][:, lo : lo + n], woven[c][:, 4 * lo : 4 * (lo + n)])
 
         quant(wmq[0][:, 0:1024], wmq[0][:, 1024:1280], wm_bf[0][:, 0:1024])
-        for c in (2, 3):
-            round_chunk(nc.vector.tensor_copy, 3, c)
-        weave(nc.vector.tensor_copy, I32, woven[2][:], pairs[2])
         quant(wmq[1][:, 0:1024], wmq[1][:, 1024:1280], wm_bf[0][:, 1024:2048])
-        quant_page(2)
-        weave(nc.vector.tensor_copy, I32, woven[3][:], pairs[3])
-        quant(wmq[2][:, 0:512], wmq[2][:, 512:640], wm_bf[1][:, 0:512])
-        for c in (3, 0, 1):
-            quant_page(c)
         quant(wmq[3][:, 0:1536], wmq[3][:, 1536:1920], wm_bf[1][:, 512:2048])
-        h2c = [sb([P, NP], U32, f"h2c{a}", WOVEN + (10 + 4 * a) * KB) for a in range(2)]
+        weave_page(0)
+        weave_page(1)
+        quant_page(0)
+        quant_page(1)
+        weave_page(2)
+        quant(wmq[2][:, 0:512], wmq[2][:, 512:640], wm_bf[1][:, 0:512])
+        quant_page(2)
+        weave_page(3)
+        weave_page(4)
+        quant_page(3)
+        quant_page(4)
+        h2c = [sb([P, NP], U32, f"h2c{a}", WOVEN + (8 + 4 * a) * KB) for a in range(2)]
         h2s = [sb([P, NP], U8, f"h2s{a}", LATE + KB * a) for a in range(2)]
         for a in range(2):
             quant(h2c[a][:], h2s[a][:], h2bf[a][:])
@@ -294,20 +302,29 @@ def tile_list_exoskeleton_gait_features_kernel(
             return tile[:, 512 * first : 512 * (first + 1)], tile[:, 512 * count + P * first : 512 * count + P * (first + 1)]
 
         row_at = (PLANE, PLANE + 8 * KB, PLANE + 16 * KB, WM_RAW, WM_RAW + 8 * KB, TAB, TAB + 8 * KB, SIN_EXTRA)
-        pick_at = (XS, XS + 4 * KB, XS + 8 * KB, PLANE + 24 * KB, PLANE + 28 * KB, WM_BF + 4 * KB, VS, PAIRS)
+        pick_at = (XS, XS + 4 * KB, VW, PLANE + 24 * KB, PLANE + 28 * KB, WM_BF + 4 * KB, VS, PAIRS)
         rows = [sb([P, T2], F32, f"row{u}", row_at[u]) for u in range(8)]
         picked = [sb([P, NP], F32, f"picked{u}", pick_at[u]) for u in range(8)]
         hp0 = sb([P, 2, NP, 2], BF16, "hp0", H2BF)
         hp1 = [sb([P, 2, n, 2], BF16, f"hp1{j0}", W1_RAW + 8 * j0) for j0, n in PIECES]
 
-        def project(u, c, by_vector=False):
-            bank = next_bank([P, CH], f"muscle{u}{c}", not by_vector)
+        def project(u, t0, n, by_vector=False):
+            bank = next_bank([P, n], f"muscle{u}{t0}", not by_vector)
             codes, scales = wm_operand(u)
-            nc.tensor.matmul_mx(
-                out=bank[:], lhsT=codes.bitcast(FP8X4), lhsT_scale=scales, rhs=pc[c][:].bitcast(FP8X4), rhs_scale=ps[c][:], start=True, stop=True
-            )
+            c, first = divmod(t0, CH)
+            step = CH // 2 if (u, c) == (0, 2) else n
+            for lo in range(0, n, step):
+                nc.tensor.matmul_mx(
+                    out=bank[:, lo : lo + step],
+                    lhsT=codes.bitcast(FP8X4),
+                    lhsT_scale=scales,
+                    rhs=pc[c][:, first + lo : first + lo + step].bitcast(FP8X4),
+                    rhs_scale=ps[c][:, first + lo : first + lo + step],
+                    start=True,
+                    stop=True,
+                )
             copy = nc.vector.tensor_copy if by_vector else nc.scalar.copy
-            copy(rows[u][:, CH * c : CH * (c + 1)], bank[:])
+            copy(rows[u][:, t0 : t0 + n], bank[:])
 
         def gather(u, j0, n):
             nc.vector.tensor_copy(picked[u][:, j0 : j0 + n], rows[u][:].indirect(l3[:, j0 // 16 : (j0 + n) // 16]))
@@ -340,8 +357,11 @@ def tile_list_exoskeleton_gait_features_kernel(
         def gain_scalar(u, j0, n, src):
             nc.scalar.activation(pair_slot(u, j0, n), src, ACT.Copy, scale=gmc[:, u // 4, u % 4 : u % 4 + 1])
 
-        todo = [(u, c) for c in (2, 3) for u in range(2)] + [(u, c) for u in range(2) for c in (0, 1)]
-        todo += [(u, c) for u in range(2, 8) for c in range(4 if u < 5 else 3)]
+        todo = [(u, 2 * CH, CH) for u in range(3)] + [(u, CH * c, CH) for u in range(2) for c in (3, 0, 1)]
+        for u in range(2, 8):
+            todo += [(u, CH * c, CH) for c in range(4 if u < 5 else 3) if (u, c) != (2, 2)]
+            if u >= 5 and V_COLUMNS[u - 5] < CH:
+                todo.append((u, 3 * CH, CH - V_COLUMNS[u - 5]))
 
         def project_next(count):
             for k in range(count):
@@ -351,9 +371,9 @@ def tile_list_exoskeleton_gait_features_kernel(
         for u in range(5):
             gather(u, 0, NP)
             if u >= 2:
-                project(u + 3, 3, True)
+                project(u + 3, T2 - V_COLUMNS[u - 2], V_COLUMNS[u - 2], True)
             squash_and_gain(u)
-            project_next(3)
+            project_next(4 if u == 1 else 3)
         gather(5, 0, NP)
         squash_and_gain(5)
         gather(6, 0, NP)

from contextlib import ExitStack

import concourse.mybir as mybir

K, T, K2, T2, S, NP, H, N = 1024, 2048, 512, 2048, 1024, 1024, 1024, 256
FLOPS = 2 * (K2 * H * T2 + K * H * NP + 2 * H * N * NP)

F32 = mybir.dt.float32
BF16 = mybir.dt.bfloat16
I32 = mybir.dt.int32
U32 = mybir.dt.uint32
U16 = mybir.dt.uint16
U8 = mybir.dt.uint8
FP8X4 = mybir.dt.float8_e4m3fn_x4
FP4X4 = mybir.dt.float4_e2m1fn_x4
ACT = mybir.ActivationFunctionType
MULT = mybir.AluOpType.mult
ADD = mybir.AluOpType.add

P = 128
KB = 1024
REP = 32
FIRST = 256
V_COLUMNS = (256, 512, 512)
PAGE_PIECES = ((1024, 256), (1280, 256), (1536, 512), (0, 512), (512, 512))
EARLY_BANKS = 4
CH = 512
GAIN_GROUPS = (((0, 2), (2, 2), (4, 4)), ((0, 4), (4, 4)))
PIECES = ((0, 512), (512, 256), (768, 256))
RANGES = ((0, 256), (256, 256), (512, 256), (768, 128), (896, 128))

TAB = 0
SIN_EXTRA = 16 * KB
PLANE = 24 * KB
XS = 56 * KB
WM_RAW = 72 * KB
W1_RAW = 88 * KB
H2BF = 96 * KB
PAIRS = 112 * KB
WOVEN = 128 * KB
WM_BF = 144 * KB
PAGE_C = 152 * KB
PAGE_S = 160 * KB
VW = 162 * KB
W4_RAW = 170 * KB
VS = 174 * KB
SMALL = 178 * KB
LATE = 192 * KB
LAST = 222 * KB


def tile_list_exoskeleton_gait_features_kernel(
    tc, tab_words, tab_scales, offs, base, xs, offs2, offs3, wm, gm, w4_words, w4_scales, gs, w1, w8_words, w8_scales, bo, out
):
    nc = tc.nc
    with ExitStack() as ctx:
        lists = ctx.enter_context(tc.tile_pool(name="lists", bufs=1))
        keep = ctx.enter_context(tc.tile_pool(name="keep", bufs=1))
        psum = ctx.enter_context(tc.psum_pool(name="psum", bufs=1))

        def sb(shape, dtype, name, offset):
            return keep.tile(shape, dtype, name=name, align_bytes=64, offset=offset)

        ring = list(range(8))

        def next_bank(shape, name, again=True):
            slot = ring.pop(0)
            if again:
                ring.append(slot)
            return psum.tile(shape, F32, name=name, offset=2 * KB * slot)

        def quant(codes, scales, src):
            nc.vector.quantize_mx(out=codes.bitcast(FP8X4), scales=scales, in_=src)

        ts = sb([P, T], U8, "ts", SMALL)
        w4s_raw = sb([P, 2 * H], U8, "w4s_raw", SMALL + 2 * KB)
        vs = [sb([P, NP], U8, f"vs{a}", VS + KB * a) for a in range(2)]
        w4sp = [sb([P, 2, 512], U8, f"w4sp{g}", at) for g, at in enumerate((PAIRS + 12 * KB - 512, SMALL + 6 * KB))]
        grep = sb([P, 2, REP, 4], F32, "grep", SMALL + 7 * KB)
        w8c = sb([P, 2, N], I32, "w8c", SMALL + 8 * KB)
        w8s = sb([P, 2 * N], U8, "w8s", SMALL + 10 * KB)
        gsc = sb([P, 2, 4], F32, "gsc", SMALL + 11 * KB)
        gmc = sb([P, 2, 4], F32, "gmc", SMALL + 11 * KB + 64)
        boc = sb([P, 2], F32, "boc", SMALL + 11 * KB + 128)
        zin = sb([P, 1], F32, "zin", SMALL + 11 * KB + 192)
        zero = sb([P, 1], F32, "zero", SMALL + 11 * KB + 256)
        nc.vector.memset(ts[:].bitcast(I32), 0)
        nc.vector.memset(zin[:], 0.0)
        nc.vector.memset(w4s_raw[:].bitcast(I32), 0)
        nc.vector.memset(vs[1][:].bitcast(I32), 0)
        nc.vector.memset(w8s[:].bitcast(I32), 0)
        nc.scalar.activation(zero[:], zin[:], ACT.Silu)

        l1 = lists.tile([P, NP // 16], U16, name="l1")
        l2 = lists.tile([P, S // 16], U16, name="l2")
        l3 = lists.tile([P, NP // 16], U16, name="l3")
        w4_raw = [sb([P, 2, H], U8, f"w4_raw{g}", W4_RAW + 2 * KB * g) for g in range(2)]
        tabw = [sb([P, T], I32, f"tabw{a}", TAB + 8 * KB * a) for a in range(2)]
        planes = [sb([P, T2], F32, f"plane{i}", PLANE + 8 * KB * i) for i in range(4)]
        xs2 = [sb([P, FIRST], F32, "xs2a", XS + 8 * KB), sb([P, S - FIRST], F32, "xs2b", XS + 8 * KB + 4 * FIRST)]
        xs_t = {i: sb([P, S], F32, f"xs{i}", XS + 4 * KB * i) for i in (0, 1, 3)}
        wm_raw = [sb([P, 4, 512], F32, f"wm_raw{g}", WM_RAW + 8 * KB * g) for g in range(2)]
        w1_raw = sb([P, 2, 4, N], F32, "w1_raw", W1_RAW)
        base_v = base.rearrange("(p i) t -> p i t", i=4)
        xs_v = xs.rearrange("(p i) t -> p i t", i=4)
        wm_v = wm.rearrange("(p j) c -> p j c", j=4)

        def load_w4(g):
            nc.sync.dma_start(w4_raw[g][:].bitcast(I32), w4_words[:, :, H * g : H * (g + 1)].rearrange("a p c -> p a c").bitcast(I32))

        def load_scale_rows(tile, rows):
            by_row = rows.rearrange("a (q r) t -> r q a t", r=4)
            for r in range(4):
                nc.sync.dma_start(tile[r:P:16, :].bitcast(I32), by_row[r].bitcast(I32))

        def load_table(a):
            nc.sync.dma_start(tabw[a][:], tab_words[a].rearrange("p t i -> p (t i)").bitcast(I32))

        load_w4(0)
        nc.sync.dma_start(l1[:], offs)
        load_scale_rows(ts, tab_scales)
        load_table(0)
        for q in range(4):
            nc.sync.dma_start(
                w4s_raw[32 * q : 32 * q + 4, :].rearrange("r (a c) -> r a c", a=2).bitcast(I32),
                w4_scales[:, 4 * q : 4 * q + 4, :].rearrange("a r c -> r a c").bitcast(I32),
            )
        load_table(1)
        nc.sync.dma_start(l2[:], offs2)
        nc.sync.dma_start(xs2[0][:], xs_v[:, 2, 0:FIRST])
        nc.sync.dma_start(planes[2][:], base_v[:, 2, :])
        nc.sync.dma_start(gsc[:], gs.rearrange("(a p t) -> p a t", a=2, t=4))
        nc.sync.dma_start(xs2[1][:], xs_v[:, 2, FIRST:S])
        load_w4(1)
        nc.sync.dma_start(gmc[:], gm.rearrange("(a p t) -> p a t", a=2, t=4))
        nc.sync.dma_start(l3[:], offs3)
        for q in range(4):
            nc.sync.dma_start(
                w8s[32 * q : 32 * q + 4, :].rearrange("r (a c) -> r a c", a=2).bitcast(I32),
                w8_scales[:, 4 * q : 4 * q + 4, :].rearrange("a r c -> r a c").bitcast(I32),
            )
        for i in (0, 1, 3):
            nc.sync.dma_start(xs_t[i][:], xs_v[:, i, :])
            nc.sync.dma_start(planes[i][:], base_v[:, i, :])
            if i < 2:
                nc.sync.dma_start(wm_raw[i][:], wm_v[:, :, 512 * i : 512 * (i + 1)])
        nc.sync.dma_start(w1_raw[:].rearrange("p a j n -> p a (j n)"), w1.rearrange("(a p j) n -> p a (j n)", a=2, j=4))
        nc.sync.dma_start(w8c[:], w8_words.rearrange("a p c i -> p a (c i)").bitcast(I32))
        with nc.allow_non_contiguous_dma(reason="one bias value a partition"):
            nc.sync.dma_start(boc[:], bo.rearrange("(h p) -> p h", p=P))

        w4p = [sb([P, 2, H], U8, f"w4p{g}", at) for g, at in enumerate((PAIRS + 3 * KB, VS + 2 * KB))]

        def order_w4(copy, g):
            copy(
                w4p[g][:].bitcast(U16).rearrange("p a (t m) -> p a t m", t=4),
                w4_raw[g][:].bitcast(U16).rearrange("p a (m t) -> p a t m", t=4),
            )

        def move_second_pass(dst, src):
            nc.gpsimd.dma_start(dst[0:112, :].bitcast(I32), src[16:128, :].bitcast(I32))

        order_w4(nc.vector.tensor_copy, 0)

        nc.vector.tensor_copy(vs[0][:], ts[:].indirect(l1[:]))
        move_second_pass(vs[1], vs[0])
        for g in range(2):
            nc.gpsimd.tensor_copy(
                w4sp[g][:].rearrange("p a (t m) -> p a t m", t=4),
                w4s_raw[:].rearrange("p (a g m t) -> p g a t m", a=2, g=2, t=4)[:, g],
            )
        vw = [sb([P, NP], U32, f"vw{a}", VW + 4 * KB * a) for a in range(2)]
        for a in range(2):
            nc.vector.tensor_copy(vw[a][:], tabw[a][:].bitcast(U32).indirect(l1[:]))
        for a in range(2):
            nc.gpsimd.tensor_scalar(grep[:, a, :, :], gsc[:, a, :].unsqueeze(1).to_broadcast([P, REP, 4]), 1.0, 0.0, MULT, ADD)

        nc.vector.tensor_copy(planes[2][:].indirect(l2[:, 0 : FIRST // 16]), xs2[0][:])
        nc.vector.tensor_copy(planes[2][:].indirect(l2[:, FIRST // 16 : S // 16]), xs2[1][:])
        for i in (0, 1, 3):
            nc.vector.tensor_copy(planes[i][:].indirect(l2[:]), xs_t[i][:])

        h2bf = [sb([P, 4 * NP], BF16, f"h2bf{g}", H2BF + 8 * KB * g) for g in range(2)]
        phase = {}

        def phase_passes(g, j0, ka):
            if ka == 0:
                phase[g, j0] = psum.tile([P, 4, P], F32, name=f"phase{g}{j0}", offset=2 * KB * (4 + j0 // P % EARLY_BANKS))
            for t in range(4):
                nc.tensor.matmul_mx(
                    out=phase[g, j0][:, t, :],
                    lhsT=w4p[g][:, ka, 2 * P * t : 2 * P * (t + 1)].bitcast(FP4X4),
                    lhsT_scale=w4sp[g][:, ka, P * t : P * (t + 1)],
                    rhs=vw[ka][:, j0 : j0 + P].bitcast(FP8X4),
                    rhs_scale=vs[ka][:, j0 : j0 + P],
                    start=(ka == 0 and t == 0),
                    stop=(ka == 1 and t == 3),
                )

        for k in range(EARLY_BANKS):
            phase_passes(0, P * k, 0)
        for g in range(2):
            for first, count in GAIN_GROUPS[g]:
                at = TAB + 2 * KB * (8 * g + first) if 8 * g + first < 12 else WM_BF
                sines = sb([P, count, 512], F32, f"sines{g}{first}", at)
                for half in range(count):
                    j0 = P * (first + half)
                    if (g, j0) not in phase:
                        phase_passes(g, j0, 0)
                    phase_passes(g, j0, 1)
                    bank = phase[g, j0]
                    nc.scalar.activation(
                        sines[:, half, :].rearrange("p (j t) -> p j t", t=4), bank[:].rearrange("p t j -> p j t"), ACT.Sin, bias=zero[:]
                    )
                reps = 512 * count // (4 * REP)
                gain = grep[:, g, :, :].rearrange("p r t -> p (r t)").unsqueeze(1).to_broadcast([P, reps, 4 * REP])
                nc.gpsimd.tensor_tensor(
                    h2bf[g][:, 512 * first : 512 * (first + count)].rearrange("p (k e) -> p k e", k=reps),
                    sines[:].rearrange("p h (k e) -> p (h k) e", e=4 * REP),
                    gain,
                    MULT,
                )
                if (g, first) == (0, 2):
                    order_w4(nc.scalar.copy, 1)

        pairs = {t0: sb([P, 2, n, 2], BF16, f"pairs{t0}", PAIRS + 8 * ((t0 + 2 * CH) % T2))[:] for t0, n in PAGE_PIECES}
        wm_bf = [sb([P, 2048], BF16, f"wm_bf{g}", at) for g, at in enumerate((SMALL + 3 * KB, VS))]

        def round_plane(i):
            for t0, n in PAGE_PIECES:
                nc.scalar.copy(pairs[t0][:, i // 2, :, i % 2], planes[i][:, t0 : t0 + n])

        def weave(copy, dtype, dst, src):
            copy(dst.bitcast(dtype).rearrange("p (c u) -> p c u", u=2), src.rearrange("p u c e -> p u (c e)").bitcast(dtype).rearrange("p u c -> p c u"))

        def cast_wm(g, t0, t1):
            nc.scalar.copy(
                wm_bf[g][:].rearrange("p (t m j) -> p m j t", t=4, j=4)[:, :, :, t0:t1],
                wm_raw[g][:].rearrange("p j (m t) -> p m j t", t=4)[:, :, :, t0:t1],
            )

        for i in (2, 0, 1):
            round_plane(i)
            if i == 2:
                cast_wm(0, 0, 4)
        nc.gpsimd.tensor_scalar(
            wm_bf[1][:, 0:1024].rearrange("p (t m j) -> p t m j", t=2, j=4),
            wm_raw[1][:].rearrange("p j (m t) -> p t m j", t=4)[:, 0:2],
            1.0,
            0.0,
            MULT,
            ADD,
        )
        cast_wm(1, 2, 4)
        round_plane(3)
        woven = [sb([P, 4 * CH], BF16, f"woven{c}", WOVEN + 4 * KB * ((c + 2) % 4)) for c in range(4)]

        pc = [sb([P, CH], U32, f"page_c{c}", PAGE_C + 2 * KB * c) for c in range(4)]
        ps = [sb([P, CH], U8, f"page_s{c}", PAGE_S + 512 * c) for c in range(4)]
        wmq = [sb([P, 1280], U8, "wmq0", XS + 12 * KB + 512), sb([P, 1280], U8, "wmq1", XS + 14 * KB), sb([P, 640], U8, "wmq2", WOVEN + 2 * KB - 320), sb([P, 1920], U8, "wmq3", XS + 11 * KB - 512)]

        def weave_page(k):
            t0, n = PAGE_PIECES[k]
            weave(nc.vector.tensor_copy, I32, woven[t0 // CH][:, 4 * (t0 % CH) : 4 * (t0 % CH + n)], pairs[t0])

        def quant_page(k):
            t0, n = PAGE_PIECES[k]
            c, lo = divmod(t0, CH)
            quant(pc[c][:, lo : lo + n], ps[c][:, lo : lo + n], woven[c][:, 4 * lo : 4 * (lo + n)])

        quant(wmq[0][:, 0:1024], wmq[0][:, 1024:1280], wm_bf[0][:, 0:1024])
        quant(wmq[1][:, 0:1024], wmq[1][:, 1024:1280], wm_bf[0][:, 1024:2048])
        quant(wmq[3][:, 0:1536], wmq[3][:, 1536:1920], wm_bf[1][:, 512:2048])
        weave_page(0)
        weave_page(1)
        quant_page(0)
        quant_page(1)
        weave_page(2)
        quant(wmq[2][:, 0:512], wmq[2][:, 512:640], wm_bf[1][:, 0:512])
        quant_page(2)
        weave_page(3)
        weave_page(4)
        quant_page(3)
        quant_page(4)
        h2c = [sb([P, NP], U32, f"h2c{a}", WOVEN + (8 + 4 * a) * KB) for a in range(2)]
        h2s = [sb([P, NP], U8, f"h2s{a}", LATE + KB * a) for a in range(2)]
        for a in range(2):
            quant(h2c[a][:], h2s[a][:], h2bf[a][:])
        w1_bf = sb([P, 2048], BF16, "w1_bf", H2BF + 8 * KB)
        for a in range(2):
            nc.gpsimd.tensor_scalar(
                w1_bf[:, 1024 * a : 1024 * (a + 1)].rearrange("p (c j) -> p c j", j=4),
                w1_raw[:, a, :, :].rearrange("p j c -> p c j"),
                1.0,
                0.0,
                MULT,
                ADD,
            )

        def wm_operand(u):
            tile, first, count = (wmq[u // 2], u % 2, 2) if u < 4 else (wmq[2], 0, 1) if u == 4 else (wmq[3], u - 5, 3)
            return tile[:, 512 * first : 512 * (first + 1)], tile[:, 512 * count + P * first : 512 * count + P * (first + 1)]

        row_at = (PLANE, PLANE + 8 * KB, PLANE + 16 * KB, WM_RAW, WM_RAW + 8 * KB, TAB, TAB + 8 * KB, SIN_EXTRA)
        pick_at = (XS, XS + 4 * KB, VW, PLANE + 24 * KB, PLANE + 28 * KB, WM_BF + 4 * KB, VS, PAIRS)
        rows = [sb([P, T2], F32, f"row{u}", row_at[u]) for u in range(8)]
        picked = [sb([P, NP], F32, f"picked{u}", pick_at[u]) for u in range(8)]
        hp0 = sb([P, 2, NP, 2], BF16, "hp0", H2BF)
        hp1 = [sb([P, 2, n, 2], BF16, f"hp1{j0}", W1_RAW + 8 * j0) for j0, n in PIECES]

        def project(u, t0, n, by_vector=False):
            bank = next_bank([P, n], f"muscle{u}{t0}", not by_vector)
            codes, scales = wm_operand(u)
            c, first = divmod(t0, CH)
            step = CH // 2 if (u, c) == (0, 2) else n
            for lo in range(0, n, step):
                nc.tensor.matmul_mx(
                    out=bank[:, lo : lo + step],
                    lhsT=codes.bitcast(FP8X4),
                    lhsT_scale=scales,
                    rhs=pc[c][:, first + lo : first + lo + step].bitcast(FP8X4),
                    rhs_scale=ps[c][:, first + lo : first + lo + step],
                    start=True,
                    stop=True,
                )
            copy = nc.vector.tensor_copy if by_vector else nc.scalar.copy
            copy(rows[u][:, t0 : t0 + n], bank[:])

        def gather(u, j0, n):
            nc.vector.tensor_copy(picked[u][:, j0 : j0 + n], rows[u][:].indirect(l3[:, j0 // 16 : (j0 + n) // 16]))

        def squash(u, j0, n):
            nc.scalar.activation(picked[u][:, j0 : j0 + n], picked[u][:, j0 : j0 + n], ACT.Tanh, bias=zero[:])

        def piece_of(j0):
            return max(k for k, (first, n) in enumerate(PIECES) if first <= j0)

        def pair_slot(u, j0, n):
            t = u % 4
            if u < 4:
                return hp0[:, t // 2, j0 : j0 + n, t % 2]
            lo = j0 - PIECES[piece_of(j0)][0]
            return hp1[piece_of(j0)][:, t // 2, lo : lo + n, t % 2]

        halves = {}

        def squash_and_gain(u):
            for h in range(2):
                half = sb([P, CH], F32, f"half{u}{h}", (WOVEN if u % 2 or u == 0 else PLANE) + 2 * KB * h)
                nc.scalar.activation(half[:], picked[u][:, CH * h : CH * (h + 1)], ACT.Tanh, bias=zero[:])
                halves[u, h] = half
                for j0, n in ((CH * h, CH),) if u < 4 else PIECES[h : 1 + 2 * h if u == 4 else 1 + h]:
                    nc.gpsimd.tensor_scalar(
                        pair_slot(u, j0, n), half[:, j0 - CH * h : j0 - CH * h + n], gmc[:, u // 4, u % 4 : u % 4 + 1], 0.0, MULT, ADD
                    )

        def gain_scalar(u, j0, n, src):
            nc.scalar.activation(pair_slot(u, j0, n), src, ACT.Copy, scale=gmc[:, u // 4, u % 4 : u % 4 + 1])

        todo = [(u, 2 * CH, CH) for u in range(3)] + [(u, CH * c, CH) for u in range(2) for c in (3, 0, 1)]
        for u in range(2, 8):
            todo += [(u, CH * c, CH) for c in range(4 if u < 5 else 3) if (u, c) != (2, 2)]
            if u >= 5 and V_COLUMNS[u - 5] < CH:
                todo.append((u, 3 * CH, CH - V_COLUMNS[u - 5]))

        def project_next(count):
            for k in range(count):
                project(*todo.pop(0))

        project_next(14)
        for u in range(5):
            gather(u, 0, NP)
            if u >= 2:
                project(u + 3, T2 - V_COLUMNS[u - 2], V_COLUMNS[u - 2], True)
            squash_and_gain(u)
            project_next(4 if u == 1 else 3)
        gather(5, 0, NP)
        squash_and_gain(5)
        gather(6, 0, NP)
        for j0 in (0, CH):
            gather(7, j0, CH)
        squash(6, 0, NP)
        last_at = (LAST, LAST + 2 * KB, PLANE + 2 * KB)
        for (j0, n), at in zip(PIECES, last_at):
            last = sb([P, n], F32, f"last{j0}", at)
            nc.scalar.activation(last[:], picked[7][:, j0 : j0 + n], ACT.Tanh, bias=zero[:])
            if j0 == PIECES[-1][0]:
                gain_scalar(5, j0, n, halves[5, 1][:, j0 - CH : j0 - CH + n])
            gain_scalar(6, j0, n, picked[6][:, j0 : j0 + n])
            gain_scalar(7, j0, n, last[:])

        ost = [sb([P, NP], F32, f"ost{h}", PLANE + 8 * KB + 4 * KB * h) for h in range(2)]
        w8b = w8c[:].rearrange("p a n -> p (a n)").bitcast(U8)
        ybank = {}

        def y_pass(k, h, wc, ws, a, hc, hs, start, stop):
            nc.tensor.matmul_mx(
                out=ybank[k, h],
                lhsT=wc[:, 4 * (N * a + P * h) : 4 * (N * a + P * (h + 1))].bitcast(FP8X4),
                lhsT_scale=ws[:, N * a + P * h : N * a + P * (h + 1)],
                rhs=hc.bitcast(FP8X4),
                rhs_scale=hs,
                start=start,
                stop=stop,
            )

        for k, (j0, n) in enumerate(RANGES):
            shared = next_bank([P, 2, n], f"y{k}")
            for h in range(2):
                ybank[k, h] = shared[:, h, :]
                for a in range(2):
                    y_pass(k, h, w8b, w8s, a, h2c[a][:, j0 : j0 + n], h2s[a][:, j0 : j0 + n], a == 0 and h == 0, False)

        h1w1 = [sb([P, 4 * n], BF16, f"h1w1{k}", LATE + 10 * KB + 8 * j0) for k, (j0, n) in enumerate(RANGES)]
        h1w0 = [sb([P, 4 * CH], BF16, f"h1w0{h}", at) for h, at in enumerate((WOVEN - 3 * KB, LATE + 7 * KB))]
        w1c = sb([P, 2048], U8, "w1c", LATE + 2 * KB)
        w1s = sb([P, 512], U8, "w1s", WOVEN + KB)
        code_at = [[LATE + 18 * KB, LATE + 19 * KB, last_at[1], last_at[2], last_at[2] + 512], [LATE + 20 * KB + 4 * j0 for j0, n in RANGES]]
        h1c = [[sb([P, n], U32, f"h1c{a}{k}", code_at[a][k]) for k, (j0, n) in enumerate(RANGES)] for a in range(2)]
        h1s = [[sb([P, n], U8, f"h1s{a}{k}", LATE + 24 * KB + NP * a + j0) for k, (j0, n) in enumerate(RANGES)] for a in range(2)]

        def weave_first(h):
            weave(nc.vector.tensor_copy, I32, h1w0[h][:], hp0[:, :, CH * h : CH * (h + 1), :])

        weave_first(0)
        quant(w1c[:], w1s[:], w1_bf[:])
        for k, (j0, n) in enumerate(RANGES):
            if k == 2:
                weave_first(1)
            lo = j0 % CH
            first = j0 - PIECES[piece_of(j0)][0]
            weave(nc.vector.tensor_copy, I32, h1w1[k][:], hp1[piece_of(j0)][:, :, first : first + n, :])
            quant(h1c[0][k][:], h1s[0][k][:], h1w0[j0 // CH][:, 4 * lo : 4 * (lo + n)])
            quant(h1c[1][k][:], h1s[1][k][:], h1w1[k][:])
            for a in range(2):
                for h in range(2):
                    y_pass(k, h, w1c, w1s, a, h1c[a][k][:], h1s[a][k][:], False, a == 1 and h == 1)
            for h in range(2):
                nc.scalar.activation(ost[h][:, j0 : j0 + n], ybank[k, h], ACT.Tanh, bias=boc[:, h : h + 1])
                queue = nc.scalar if (k, h) == (len(RANGES) - 1, 1) else nc.sync
                queue.dma_start(out[P * h : P * (h + 1), j0 : j0 + n], ost[h][:, j0 : j0 + n])
